import numpy as np
import ml_dtypes


def mxq(x, axis, fmt="e4m3"):
    dtype, down = {"e4m3": (ml_dtypes.float8_e4m3fn, 7), "e5m2": (ml_dtypes.float8_e5m2, 14)}[fmt]
    v = np.moveaxis(np.asarray(x, np.float32).astype(ml_dtypes.bfloat16).astype(np.float64), axis, -1)
    blocks = v.reshape(v.shape[:-1] + (-1, 32))
    amax = np.abs(blocks).max(-1, keepdims=True)
    byte = np.maximum(np.where(amax > 0, np.frexp(amax)[1] - 1 + 127, 0) - down, 1)
    scale = np.exp2(byte - 127.0)
    codes = (blocks / scale).astype(np.float32).astype(dtype).astype(np.float64)
    return np.moveaxis((codes * scale).reshape(v.shape), -1, axis)


WIDE = False


def mx_kscale(k):
    if not WIDE:
        return np.ones(k)
    levels = np.array([10, -10, 5, -5, 0])
    if k % 512:
        return np.exp2(np.random.permutation(np.resize(levels, k // 32))).repeat(32)
    a = np.empty((k // 512, 16))
    for p in range(k // 512):
        a[p, :8] = np.random.permutation(np.resize(levels, 8))
        for g in range(8):
            far = levels[np.abs(levels - a[p, g]) >= 10]
            a[p, g + 8] = far[np.random.randint(len(far))]
    return np.exp2(a.ravel()).repeat(32)


def f64(x):
    return np.asarray(x).astype(np.float64)


def striped(idx):
    return np.tile(np.asarray(idx).reshape(-1, 16).T, (8, 1)).astype(np.uint16)


def unstriped(offs):
    return offs[:16].T.reshape(-1).astype(np.int64)


B, N, T, D, DV, NQ = 2, 512, 2048, 512, 128, 512
CAP = 2.0


def setup_inputs():
    n = np.random.standard_normal
    seg = T // B
    idx = np.concatenate([b * seg + np.random.permutation(seg)[:N] for b in range(B)])
    s = mx_kscale(D)[:, None]
    u = np.ones(T)
    u[idx] = mx_kscale(B * N)
    r = np.random.uniform(0.5, 2.0, T)
    qidx = idx
    k = n((D, T)) / s
    v = n((DV, T)) / (u * r)
    return {
        "xq": (n((D, T)) * s * (0.60 / np.sqrt(D))).astype(np.float32),
        "kT": k.astype(np.float32),
        "vT": v.astype(np.float32),
        "vs": np.tile(u * r, (128, 1)).astype(np.float32),
        "offs": striped(idx),
        "qoffs": striped(qidx),
    }


def reference(xq, kT, vT, vs, offs, qoffs):
    idx = unstriped(offs)
    k = f64(kT)
    v = f64(vT)
    pick = lambda x: x[:, idx].reshape(x.shape[0], B, N).transpose(1, 0, 2)
    q = f64(xq)[:, unstriped(qoffs)].reshape(D, B, NQ).transpose(1, 0, 2)
    score = mxq(q, 1, "e4m3").transpose(0, 2, 1) @ mxq(pick(k), 1, "e4m3")
    score = CAP * np.tanh(score / CAP)
    m = score.max(-1, keepdims=True)
    p = np.exp(score - m)
    total = p.sum(-1, keepdims=True)
    w = p * pick(f64(vs))[:, :1, :]
    y = mxq(w, 2, "e4m3") @ mxq(pick(v).transpose(0, 2, 1), 1, "e4m3")
    y = y / total
    out = np.zeros((DV, T))
    out[:, unstriped(qoffs)] = y.transpose(2, 0, 1).reshape(-1, B * NQ)
    return out

@@ -1,0 +1,366 @@
+from contextlib import ExitStack
+
+import concourse.mybir as mybir
+from concourse.masks import make_identity
+
+P = 128
+B, N, T, D, DV, NQ = 2, 512, 2048, 512, 128, 512
+SEG = T // B
+PACK = 4
+LOADS = "M k012 L k112 q112 q01 q10 k00 q00 v1 k102 v0 s1 s0"
+PLAN = """cak00 cak11 cak01 caq11 caq01 gaq01 caq00 gak01 gak00 vg1 cak10 gaq11 caq10 quq1 gak11 gaq00 quk1 sc10 sc11 gaq10 sc12 mx10 gak10 vv1 sc13 quk0 ex10 mx11 quq0 vg0 sc00 sc01 ex11 ex12 ex13 sg ss1 mx00 we10 we11 sc02 sc03 ss0 mx01 qw102 ex00 we12 ex03 ex01 vv0 ex02 sp104 we13 we00 pr102 qw124 we01 we03 sp004 sx102 pr124 qw034 we02 qw002 pr034 sx124 st1 sx034 qw023 pr002 sx002 pr023 sx023 st0"""
+SHARES = {"cak00": [["V",512],["S",512]], "cak11": [["S",512],["S",256],["V",256]], "cak01": [["V",512],["V",512]], "caq11": [["S",512],["S",512]], "caq01": [["S",512],["V",512]], "caq00": [["S",1024]], "cak10": [["S",512],["S",256],["V",256]], "caq10": [["S",512],["S",512]]}
+INTER = {("k", 0): "G", ("k", 1): "G", ("q", 0): "V", ("q", 1): "V"}
+VS = "SV"
+BY_G = ()
+BY_S = ((0, 2),)
+NRAW = 7
+NWORK = 4
+NPS = [3,3,1,1]
+ZERO = "Gk0 Gk1 Gi Vq0 Vq1 Gv Gh Gp1 Gp0"
+FLOPS = 2 * B * NQ * N * (D + DV)
+
+F32 = mybir.dt.float32
+BF16 = mybir.dt.bfloat16
+U32 = mybir.dt.uint32
+I32 = mybir.dt.int32
+U16 = mybir.dt.uint16
+U8 = mybir.dt.uint8
+FP8X4 = mybir.dt.float8_e4m3fn_x4
+ACT = mybir.ActivationFunctionType
+ALU = mybir.AluOpType
+
+
+def tile_attend_x_cluster_cap_kernel(tc, xq, kT, vT, vs, offs, qoffs, out):
+    nc = tc.nc
+    with ExitStack() as ctx:
+        keep = ctx.enter_context(tc.tile_pool(name="keep", bufs=1))
+        raws = ctx.enter_context(tc.tile_pool(name="raws", bufs=1))
+        seqs = ctx.enter_context(tc.tile_pool(name="seqs", bufs=2))
+        work = ctx.enter_context(tc.tile_pool(name="work", bufs=NWORK))
+        ps_s = ctx.enter_context(tc.psum_pool(name="ps_s", bufs=NPS[0]))
+        ps_p = ctx.enter_context(tc.psum_pool(name="ps_p", bufs=NPS[1]))
+        ps_y = ctx.enter_context(tc.psum_pool(name="ps_y", bufs=NPS[2]))
+        ps_t = ctx.enter_context(tc.psum_pool(name="ps_t", bufs=NPS[3]))
+
+        lists = keep.tile([P, B * N // 16], U16, name="lists")
+        qlists = keep.tile([P, B * NQ // 16], U16, name="qlists")
+        words, v_pool, placed = {}, {}, {}
+        for b in range(B):
+            wide = (b + 1) * SEG
+            for name in ("k", "q"):
+                for u in range(2):
+                    words[name, u, b] = keep.tile([P, 2 * wide], BF16, name="words_%s%d%d" % (name, u, b))
+            v_pool[b] = keep.tile([P, wide], BF16 if VS[b] == "S" else F32, name="v_pool%d" % b)
+            placed[b] = keep.tile([P, wide], F32, name="placed%d" % b)
+        s_pool = keep.tile([P, T], F32, name="s_pool")
+        s_rows = keep.tile([P, B * N], F32, name="s_rows")
+        ident = keep.tile([P, P], F32, name="ident")
+        ident_h = keep.tile([P, P], BF16, name="ident_h")
+        warm = keep.tile([P, 1], F32, name="warm")
+
+        source = {"k": kT.rearrange("(p j) w -> p j w", j=PACK), "q": xq.rearrange("(p j) w -> p j w", j=PACK)}
+        raw, raw_tiles = {}, {}
+
+        def load_rows(name, u, b, lo, hi):
+            if lo == 0:
+                raw[name, u, b] = []
+                raw_tiles[name, u, b] = raws.tile([P, 2 * SEG], F32, name="raw", bufs=NRAW)
+            piece = raw_tiles[name, u, b][:, 2 * lo : 2 * hi].rearrange("p (e w) -> p e w", e=2)
+            nc.sync.dma_start(
+                out=piece,
+                in_=source[name][:, 2 * u : 2 * u + 2, b * SEG + lo : b * SEG + hi],
+            )
+            raw[name, u, b].append((lo, hi, piece))
+
+        v_raw = {}
+        for step in LOADS.split():
+            if step == "L":
+                nc.sync.dma_start(lists[:], offs)
+            elif step == "M":
+                nc.sync.dma_start(qlists[:], qoffs)
+            elif step[0] == "s":
+                b = int(step[1])
+                nc.sync.dma_start(out=s_pool[:, b * SEG : (b + 1) * SEG], in_=vs[:, b * SEG : (b + 1) * SEG])
+            elif step[0] == "v":
+                b = int(step[1])
+                if VS[b] == "S":
+                    v_raw[b] = raws.tile([P, SEG], F32, name="v_raw%d" % b)
+                    nc.sync.dma_start(out=v_raw[b][:], in_=vT[:, b * SEG : (b + 1) * SEG])
+                else:
+                    nc.sync.dma_start(out=v_pool[b][:, b * SEG : (b + 1) * SEG], in_=vT[:, b * SEG : (b + 1) * SEG])
+            else:
+                parts = int(step[3]) if len(step) > 3 else 1
+                for i in range(parts):
+                    load_rows(step[0], int(step[1]), int(step[2]), i * SEG // parts, (i + 1) * SEG // parts)
+
+        nc.vector.memset(warm[:], 0.0)
+        nc.scalar.activation(warm[:], warm[:], ACT.Exp)
+        def zero(which):
+            for step in which.split():
+                eng = nc.vector if step[0] == "V" else nc.gpsimd
+                if step[1] in "kq":
+                    eng.memset(words[step[1], int(step[2]), 1][:, 0 : 2 * SEG].bitcast(U32), 0)
+                elif step[1] == "v":
+                    eng.memset(v_pool[1][:, 0:SEG], 0.0)
+                elif step[1] == "i":
+                    make_identity(nc, ident[:])
+                elif step[1] == "h":
+                    make_identity(nc, ident_h[:])
+                elif step[1] == "p":
+                    b = int(step[2])
+                    eng.memset(placed[b][:, b * SEG : (b + 1) * SEG], 0.0)
+
+        zero(ZERO)
+
+        def cast(name, u, b, shares):
+            full = words[name, u, b][:].rearrange("p (w e) -> p w e", e=2)
+            lo = 0
+            for engine, width in shares:
+                o = full[:, b * SEG + lo : b * SEG + lo + width, :]
+                for a, z, piece in raw[name, u, b]:
+                    if a <= lo < z:
+                        i = piece.rearrange("p e w -> p w e")[:, lo - a : lo - a + width, :]
+                if engine == "S":
+                    nc.scalar.activation(o, i, ACT.Copy)
+                elif engine == "G":
+                    nc.gpsimd.tensor_copy(o, i)
+                else:
+                    nc.vector.tensor_copy(o, i)
+                lo += width
+
+        grouped, codes, scales, apart = {}, {}, {}, {}
+
+        def gather(name, u, b):
+            mode = INTER[name, b]
+            if u == 0:
+                grouped[name, b] = seqs.tile([P, N * PACK], BF16, name="grouped_" + name, align_bytes=64)
+                if mode != "step":
+                    apart[name, b] = seqs.tile([P, 2, N], U32, name="apart_" + name, bufs=1)
+            window = words[name, u, b][:].bitcast(U32)
+            index = lists if name == "k" else qlists
+            dest = grouped[name, b][:].bitcast(U32).rearrange("p (n u) -> p n u", u=2)
+            picked = window.indirect(index[:, b * 32 : (b + 1) * 32])
+            if mode == "step":
+                nc.vector.tensor_copy(dest[:, :, u], picked)
+            else:
+                nc.vector.tensor_copy(apart[name, b][:, u, :], picked)
+                if u == 1:
+                    src = apart[name, b][:].rearrange("p u n -> p n u")
+                    if mode == "S":
+                        nc.scalar.copy(dest, src)
+                    elif mode == "V":
+                        nc.vector.tensor_copy(
+                            grouped[name, b][:].bitcast(I32).rearrange("p (n u) -> p n u", u=2),
+                            apart[name, b][:].bitcast(I32).rearrange("p u n -> p n u"),
+                        )
+                    else:
+                        nc.gpsimd.tensor_copy(dest, src)
+
+        def quantize(name, b):
+            codes[name, b] = seqs.tile([P, N], U32, name="codes_" + name, align_bytes=64)
+            scales[name, b] = seqs.tile([P, N], U8, name="scales_" + name, align_bytes=64)
+            nc.vector.quantize_mx(
+                out=codes[name, b][:].bitcast(FP8X4), scales=scales[name, b][:], in_=grouped[name, b][:]
+            )
+
+        slot_scale, v_codes, v_scales, v_rows = {}, {}, {}, {}
+
+        def gather_scales():
+            nc.vector.tensor_copy(s_rows[:], s_pool[:].indirect(lists[:]))
+
+        def prepare_scales(b):
+            bank = ps_t.tile([P, PACK, P], F32, name="bank_t")
+            slots = s_rows[:, b * N : (b + 1) * N].rearrange("p (s t) -> p t s", t=PACK)
+            for t in range(PACK):
+                nc.tensor.transpose(bank[:, t, :], slots[:, t, :], ident[:])
+            slot_scale[b] = seqs.tile([P, PACK], F32, name="slot_scale")
+            nc.scalar.activation(slot_scale[b][:], bank[:, :, 0], ACT.Copy)
+
+        def gather_values(b):
+            if VS[b] == "S":
+                nc.scalar.activation(v_pool[b][:, b * SEG : (b + 1) * SEG], v_raw[b][:], ACT.Copy)
+                g = seqs.tile([P, N, 2], BF16, name="v_rows_h")
+                nc.scalar.activation(g[:, :, 0], v_pool[b][:].indirect(lists[:, b * 32 : (b + 1) * 32]), ACT.Copy)
+                v_rows[b] = (g[:, :, 0], BF16, ident_h)
+            else:
+                g = seqs.tile([P, N], F32, name="v_rows")
+                nc.vector.tensor_copy(g[:], v_pool[b][:].indirect(lists[:, b * 32 : (b + 1) * 32]))
+                v_rows[b] = (g[:], F32, ident)
+
+        def prepare_values(b):
+            rows, kind, eye = v_rows[b]
+            bank = ps_t.tile([P, PACK, P], kind, name="bank_t")
+            slots = rows.rearrange("p (s t) -> p t s", t=PACK)
+            for t in range(PACK):
+                nc.tensor.transpose(bank[:, t, :], slots[:, t, :], eye[:])
+            g = seqs.tile([P, DV * PACK], BF16, name="grouped_v", align_bytes=64)
+            nc.scalar.activation(g[:].rearrange("p (e t) -> p e t", t=PACK), bank[:].rearrange("p t e -> p e t"), ACT.Copy)
+            v_codes[b] = seqs.tile([P, DV], U32, name="codes_v", align_bytes=64)
+            v_scales[b] = seqs.tile([P, DV], U8, name="scales_v", align_bytes=64)
+            nc.vector.quantize_mx(out=v_codes[b][:].bitcast(FP8X4), scales=v_scales[b][:], in_=g[:])
+
+        sums, w_codes, w_scales, weights, capped, lows, w_rows = {}, {}, {}, {}, {}, {}, {}
+
+        def score(b, j):
+            bank = ps_s.tile([P, N], F32, name="bank_s")
+            cols = slice(j * P, (j + 1) * P)
+            nc.tensor.matmul_mx(
+                out=bank[:],
+                lhsT=codes["q", b][:, cols].bitcast(FP8X4),
+                lhsT_scale=scales["q", b][:, cols],
+                rhs=codes["k", b][:].bitcast(FP8X4),
+                rhs_scale=scales["k", b][:],
+                start=True,
+                stop=True,
+            )
+            if j % 2 == 0:
+                capped[b, j // 2] = work.tile([P, 2, PACK, P], F32, name="th", bufs=3)
+            if (b, j) in BY_G:
+                nc.scalar.activation(
+                    capped[b, j // 2][:, j % 2].rearrange("q t s -> q (t s)"), bank[:], ACT.Tanh, scale=0.5
+                )
+            else:
+                nc.scalar.activation(
+                    capped[b, j // 2][:, j % 2], bank[:].rearrange("q (s t) -> q t s", t=PACK), ACT.Tanh, scale=0.5
+                )
+
+        def lowest(b, h):
+            top = work.tile([P, 2], F32, name="top", bufs=3)
+            nc.vector.reduce_max(
+                top[:], capped[b, h][:].rearrange("q j t s -> q j (t s)"), axis=mybir.AxisListType.X
+            )
+            lows[b, h] = work.tile([P, 2], F32, name="low", bufs=4)
+            nc.scalar.activation(lows[b, h][:], top[:], ACT.Copy, scale=-2.0)
+
+        def exponent(b, j):
+            p = work.tile([P, PACK, P], F32, name="p", bufs=4)
+            if j == 0:
+                sums[b] = seqs.tile([P, NQ // P], F32, name="sums")
+            i = j % 2
+            nc.scalar.activation(
+                p[:], capped[b, j // 2][:, i], ACT.Exp, bias=lows[b, j // 2][:, i : i + 1], scale=2.0,
+                accum_out=sums[b][:, j : j + 1],
+            )
+            weights[b, j] = p
+
+        def weigh(b, j):
+            p = weights[b, j]
+            if (b, j) in BY_G:
+                weighed = work.tile([P, N], BF16, name="weighed", bufs=3)
+                nc.gpsimd.tensor_tensor(weighed[:], p[:].rearrange("q t s -> q (t s)"), s_rows[:, b * N : (b + 1) * N], ALU.mult)
+                turned = ps_p.tile([P, PACK, P], BF16, name="turned")
+                slots = weighed[:].rearrange("q (s t) -> q t s", t=PACK)
+                for t in range(PACK):
+                    nc.tensor.transpose(turned[:, t, :], slots[:, t, :], ident_h[:])
+            else:
+                turned = ps_p.tile([P, PACK, P], F32, name="turned")
+                for t in range(PACK):
+                    nc.tensor.transpose(turned[:, t, :], p[:, t, :], ident[:])
+            if j == 0:
+                w_rows[b] = seqs.tile([P, NQ, PACK], BF16, name="w", align_bytes=64)
+                w_codes[b] = seqs.tile([P, NQ], U32, name="codes_w", align_bytes=64)
+                w_scales[b] = seqs.tile([P, NQ], U8, name="scales_w", align_bytes=64)
+            w = w_rows[b][:, j * P : (j + 1) * P, :]
+            if (b, j) in BY_G:
+                nc.scalar.activation(w, turned[:].rearrange("s t q -> s q t"), ACT.Copy)
+            elif (b, j) in BY_S:
+                for t in range(PACK):
+                    nc.scalar.activation(w[:, :, t], turned[:, t, :], ACT.Copy, scale=slot_scale[b][:, t : t + 1])
+            else:
+                nc.vector.tensor_tensor(
+                    w,
+                    turned[:].rearrange("s t q -> s q t"),
+                    slot_scale[b][:].unsqueeze(1).to_broadcast([P, P, PACK]),
+                    ALU.mult,
+                )
+
+        def quantize_weights(b, lo, hi):
+            here = slice(lo * P, hi * P)
+            nc.vector.quantize_mx(
+                out=w_codes[b][:, here].bitcast(FP8X4),
+                scales=w_scales[b][:, here],
+                in_=w_rows[b][:, here, :].rearrange("s q t -> s (q t)"),
+            )
+
+        ready = {}
+
+        def product(b, lo, hi):
+            width = (hi - lo) * P
+            bank = ps_y.tile([P, width], F32, name="bank_y")
+            nc.tensor.matmul_mx(
+                out=bank[:],
+                lhsT=v_codes[b][:].bitcast(FP8X4),
+                lhsT_scale=v_scales[b][:],
+                rhs=w_codes[b][:, lo * P : hi * P].bitcast(FP8X4),
+                rhs_scale=w_scales[b][:, lo * P : hi * P],
+                start=True,
+                stop=True,
+            )
+            y = work.tile([P, width], F32, name="y", bufs=4)
+            nc.scalar.activation(y[:], bank[:], ACT.Copy)
+            ready[b, lo] = y
+
+        factors = {}
+
+        def spread(b, lo, hi):
+            inv = work.tile([P, hi - lo], F32, name="inv", bufs=2)
+            nc.vector.reciprocal(inv[:], sums[b][:, lo:hi])
+            bank = ps_t.tile([P, hi - lo, P], F32, name="bank_t")
+            for i in range(hi - lo):
+                nc.tensor.transpose(bank[:, i, :], inv[:, i : i + 1].to_broadcast([P, P]), ident[:])
+            factor = work.tile([P, (hi - lo) * P], F32, name="factor", bufs=2)
+            nc.scalar.activation(factor[:], bank[:].rearrange("p i q -> p (i q)"), ACT.Copy)
+            for i in range(hi - lo):
+                factors[b, lo + i] = (factor, i)
+
+        def scatter(b, lo, hi):
+            factor, i = factors[b, lo]
+            first = b * 32 + 8 * lo
+            nc.vector.tensor_tensor(
+                placed[b][:].indirect(qlists[:, first : first + 8 * (hi - lo)]),
+                ready[b, lo][:],
+                factor[:, i * P : (i + hi - lo) * P],
+                ALU.mult,
+            )
+
+        def store(b):
+            nc.sync.dma_start(out=out[:, b * SEG : (b + 1) * SEG], in_=placed[b][:, b * SEG : (b + 1) * SEG])
+
+        for step in PLAN.split():
+            kind, rest = step[:2], step[2:]
+            d = [c if c in "kq" else int(c) for c in rest]
+            if kind == "ca":
+                cast(d[0], d[1], d[2], SHARES[step])
+            elif kind == "ga":
+                gather(d[0], d[1], d[2])
+            elif kind == "qu":
+                quantize(d[0], d[1])
+            elif kind == "sg":
+                gather_scales()
+            elif kind == "ss":
+                prepare_scales(d[0])
+            elif kind == "vg":
+                gather_values(d[0])
+            elif kind == "vv":
+                prepare_values(d[0])
+            elif kind == "sc":
+                score(d[0], d[1])
+            elif kind == "mx":
+                lowest(d[0], d[1])
+            elif kind == "ex":
+                exponent(d[0], d[1])
+            elif kind == "we":
+                weigh(d[0], d[1])
+            elif kind == "qw":
+                quantize_weights(d[0], d[1], d[2])
+            elif kind == "pr":
+                product(d[0], d[1], d[2])
+            elif kind == "sp":
+                spread(d[0], d[1], d[2])
+            elif kind == "sx":
+                scatter(d[0], d[1], d[2])
+            elif kind == "st":
+                store(d[0])
+            else:
+                assert False

@@ -7,17 +7,8 @@ P = 128
 B, N, T, D, DV, NQ = 2, 512, 2048, 512, 128, 512
 SEG = T // B
 PACK = 4
-LOADS = "M k012 L k112 q112 q01 q10 k00 q00 v1 k102 v0 s1 s0"
-PLAN = """cak00 cak11 cak01 caq11 caq01 gaq01 caq00 gak01 gak00 vg1 cak10 gaq11 caq10 quq1 gak11 gaq00 quk1 sc10 sc11 gaq10 sc12 mx10 gak10 vv1 sc13 quk0 ex10 mx11 quq0 vg0 sc00 sc01 ex11 ex12 ex13 sg ss1 mx00 we10 we11 sc02 sc03 ss0 mx01 qw102 ex00 we12 ex03 ex01 vv0 ex02 sp104 we13 we00 pr102 qw124 we01 we03 sp004 sx102 pr124 qw034 we02 qw002 pr034 sx124 st1 sx034 qw023 pr002 sx002 pr023 sx023 st0"""
-SHARES = {"cak00": [["V",512],["S",512]], "cak11": [["S",512],["S",256],["V",256]], "cak01": [["V",512],["V",512]], "caq11": [["S",512],["S",512]], "caq01": [["S",512],["V",512]], "caq00": [["S",1024]], "cak10": [["S",512],["S",256],["V",256]], "caq10": [["S",512],["S",512]]}
-INTER = {("k", 0): "G", ("k", 1): "G", ("q", 0): "V", ("q", 1): "V"}
-VS = "SV"
-BY_G = ()
-BY_S = ((0, 2),)
-NRAW = 7
-NWORK = 4
-NPS = [3,3,1,1]
-ZERO = "Gk0 Gk1 Gi Vq0 Vq1 Gv Gh Gp1 Gp0"
+TILES = NQ // P
+COLS = N // 16
 FLOPS = 2 * B * NQ * N * (D + DV)
 
 F32 = mybir.dt.float32
@@ -35,172 +26,144 @@ def tile_attend_x_cluster_cap_kernel(tc, xq, kT, vT, vs, offs, qoffs, out):
     nc = tc.nc
     with ExitStack() as ctx:
         keep = ctx.enter_context(tc.tile_pool(name="keep", bufs=1))
-        raws = ctx.enter_context(tc.tile_pool(name="raws", bufs=1))
         seqs = ctx.enter_context(tc.tile_pool(name="seqs", bufs=2))
-        work = ctx.enter_context(tc.tile_pool(name="work", bufs=NWORK))
-        ps_s = ctx.enter_context(tc.psum_pool(name="ps_s", bufs=NPS[0]))
-        ps_p = ctx.enter_context(tc.psum_pool(name="ps_p", bufs=NPS[1]))
-        ps_y = ctx.enter_context(tc.psum_pool(name="ps_y", bufs=NPS[2]))
-        ps_t = ctx.enter_context(tc.psum_pool(name="ps_t", bufs=NPS[3]))
+        work = ctx.enter_context(tc.tile_pool(name="work", bufs=4))
+        ps_s = ctx.enter_context(tc.psum_pool(name="ps_s", bufs=3))
+        ps_p = ctx.enter_context(tc.psum_pool(name="ps_p", bufs=2))
+        ps_y = ctx.enter_context(tc.psum_pool(name="ps_y", bufs=1))
+        ps_t = ctx.enter_context(tc.psum_pool(name="ps_t", bufs=2))
 
-        lists = keep.tile([P, B * N // 16], U16, name="lists")
-        qlists = keep.tile([P, B * NQ // 16], U16, name="qlists")
-        words, v_pool, placed = {}, {}, {}
+        lists = {"k": keep.tile([P, B * COLS], U16, name="lists"), "q": keep.tile([P, B * COLS], U16, name="qlists")}
+        words = {}
+        for name in "kq":
+            for u in range(2):
+                words[name, u] = keep.tile([P, 2 * T], BF16, name="words_%s%d" % (name, u))
+        v_pool, placed = {}, {}
         for b in range(B):
-            wide = (b + 1) * SEG
-            for name in ("k", "q"):
-                for u in range(2):
-                    words[name, u, b] = keep.tile([P, 2 * wide], BF16, name="words_%s%d%d" % (name, u, b))
-            v_pool[b] = keep.tile([P, wide], BF16 if VS[b] == "S" else F32, name="v_pool%d" % b)
-            placed[b] = keep.tile([P, wide], F32, name="placed%d" % b)
+            v_pool[b] = keep.tile([P, (b + 1) * SEG], (F32, BF16)[b], name="v_pool%d" % b)
+            placed[b] = keep.tile([P, (b + 1) * SEG], F32, name="placed%d" % b)
         s_pool = keep.tile([P, T], F32, name="s_pool")
         s_rows = keep.tile([P, B * N], F32, name="s_rows")
         ident = keep.tile([P, P], F32, name="ident")
-        ident_h = keep.tile([P, P], BF16, name="ident_h")
         warm = keep.tile([P, 1], F32, name="warm")
 
         source = {"k": kT.rearrange("(p j) w -> p j w", j=PACK), "q": xq.rearrange("(p j) w -> p j w", j=PACK)}
-        raw, raw_tiles = {}, {}
+        raw, v_raw = {}, {}
 
-        def load_rows(name, u, b, lo, hi):
-            if lo == 0:
-                raw[name, u, b] = []
-                raw_tiles[name, u, b] = raws.tile([P, 2 * SEG], F32, name="raw", bufs=NRAW)
-            piece = raw_tiles[name, u, b][:, 2 * lo : 2 * hi].rearrange("p (e w) -> p e w", e=2)
-            nc.sync.dma_start(
-                out=piece,
-                in_=source[name][:, 2 * u : 2 * u + 2, b * SEG + lo : b * SEG + hi],
-            )
-            raw[name, u, b].append((lo, hi, piece))
+        def load_rows(name, u, b, parts):
+            width = SEG // parts
+            raw[name, u, b] = []
+            for i in range(parts):
+                piece = keep.tile([P, 2, width], F32, name="raw_%s%d%d%d" % (name, u, b, i), align_bytes=64)
+                first = b * SEG + i * width
+                nc.sync.dma_start(out=piece[:], in_=source[name][:, 2 * u : 2 * u + 2, first : first + width])
+                raw[name, u, b].append((first, width, piece))
 
-        v_raw = {}
-        for step in LOADS.split():
-            if step == "L":
-                nc.sync.dma_start(lists[:], offs)
-            elif step == "M":
-                nc.sync.dma_start(qlists[:], qoffs)
-            elif step[0] == "s":
-                b = int(step[1])
-                nc.sync.dma_start(out=s_pool[:, b * SEG : (b + 1) * SEG], in_=vs[:, b * SEG : (b + 1) * SEG])
-            elif step[0] == "v":
-                b = int(step[1])
-                if VS[b] == "S":
-                    v_raw[b] = raws.tile([P, SEG], F32, name="v_raw%d" % b)
-                    nc.sync.dma_start(out=v_raw[b][:], in_=vT[:, b * SEG : (b + 1) * SEG])
-                else:
-                    nc.sync.dma_start(out=v_pool[b][:, b * SEG : (b + 1) * SEG], in_=vT[:, b * SEG : (b + 1) * SEG])
-            else:
-                parts = int(step[3]) if len(step) > 3 else 1
-                for i in range(parts):
-                    load_rows(step[0], int(step[1]), int(step[2]), i * SEG // parts, (i + 1) * SEG // parts)
+        def load_values(b):
+            v_raw[b] = keep.tile([P, SEG], F32, name="v_raw%d" % b, align_bytes=64) if b else v_pool[0]
+            nc.sync.dma_start(out=v_raw[b][:], in_=vT[:, b * SEG : (b + 1) * SEG])
 
         nc.vector.memset(warm[:], 0.0)
         nc.scalar.activation(warm[:], warm[:], ACT.Exp)
-        def zero(which):
-            for step in which.split():
-                eng = nc.vector if step[0] == "V" else nc.gpsimd
-                if step[1] in "kq":
-                    eng.memset(words[step[1], int(step[2]), 1][:, 0 : 2 * SEG].bitcast(U32), 0)
-                elif step[1] == "v":
-                    eng.memset(v_pool[1][:, 0:SEG], 0.0)
-                elif step[1] == "i":
-                    make_identity(nc, ident[:])
-                elif step[1] == "h":
-                    make_identity(nc, ident_h[:])
-                elif step[1] == "p":
-                    b = int(step[2])
-                    eng.memset(placed[b][:, b * SEG : (b + 1) * SEG], 0.0)
+        nc.gpsimd.memset(s_pool[:], 0.0)
+        load_rows("k", 0, 0, 4)
+        nc.sync.dma_start(lists["k"][:], offs)
+        load_rows("k", 1, 0, 2)
+        nc.sync.dma_start(out=s_pool[0:1, :], in_=vs[0:1, :])
+        nc.sync.dma_start(lists["q"][:], qoffs)
+        load_rows("q", 0, 0, 2)
+        load_rows("q", 1, 0, 2)
+        load_rows("k", 0, 1, 2)
+        load_rows("k", 1, 1, 2)
+        load_values(0)
+        load_rows("q", 0, 1, 2)
+        load_rows("q", 1, 1, 2)
+        load_values(1)
 
-        zero(ZERO)
+        make_identity(nc, ident[:])
+        nc.gpsimd.memset(v_pool[1][:, 0:SEG], 0.0)
+        for b in range(B):
+            nc.gpsimd.memset(placed[b][:, b * SEG : (b + 1) * SEG], 0.0)
 
-        def cast(name, u, b, shares):
-            full = words[name, u, b][:].rearrange("p (w e) -> p w e", e=2)
-            lo = 0
-            for engine, width in shares:
-                o = full[:, b * SEG + lo : b * SEG + lo + width, :]
-                for a, z, piece in raw[name, u, b]:
-                    if a <= lo < z:
-                        i = piece.rearrange("p e w -> p w e")[:, lo - a : lo - a + width, :]
-                if engine == "S":
-                    nc.scalar.activation(o, i, ACT.Copy)
-                elif engine == "G":
-                    nc.gpsimd.tensor_copy(o, i)
-                else:
-                    nc.vector.tensor_copy(o, i)
-                lo += width
+        slot_scale = {}
 
-        grouped, codes, scales, apart = {}, {}, {}, {}
+        def place(key, pool, shape, kind):
+            if key in after:
+                return keep.tile(shape, kind, name=after[key], align_bytes=64)
+            return pool.tile(shape, kind, name=key[0], align_bytes=64)
 
-        def gather(name, u, b):
-            mode = INTER[name, b]
-            if u == 0:
-                grouped[name, b] = seqs.tile([P, N * PACK], BF16, name="grouped_" + name, align_bytes=64)
-                if mode != "step":
-                    apart[name, b] = seqs.tile([P, 2, N], U32, name="apart_" + name, bufs=1)
-            window = words[name, u, b][:].bitcast(U32)
-            index = lists if name == "k" else qlists
-            dest = grouped[name, b][:].bitcast(U32).rearrange("p (n u) -> p n u", u=2)
-            picked = window.indirect(index[:, b * 32 : (b + 1) * 32])
-            if mode == "step":
-                nc.vector.tensor_copy(dest[:, :, u], picked)
+        def cast(name, u, b, i, engine=nc.scalar):
+            first, width, piece = raw[name, u, b][i]
+            dest = words[name, u][:].rearrange("p (w e) -> p w e", e=2)[:, first : first + width, :]
+            src = piece[:].rearrange("p e w -> p w e")
+            if engine is nc.vector:
+                nc.vector.tensor_copy(dest, src)
             else:
-                nc.vector.tensor_copy(apart[name, b][:, u, :], picked)
-                if u == 1:
-                    src = apart[name, b][:].rearrange("p u n -> p n u")
-                    if mode == "S":
-                        nc.scalar.copy(dest, src)
-                    elif mode == "V":
-                        nc.vector.tensor_copy(
-                            grouped[name, b][:].bitcast(I32).rearrange("p (n u) -> p n u", u=2),
-                            apart[name, b][:].bitcast(I32).rearrange("p u n -> p n u"),
-                        )
-                    else:
-                        nc.gpsimd.tensor_copy(dest, src)
+                nc.scalar.activation(dest, src, ACT.Copy)
 
-        def quantize(name, b):
-            codes[name, b] = seqs.tile([P, N], U32, name="codes_" + name, align_bytes=64)
-            scales[name, b] = seqs.tile([P, N], U8, name="scales_" + name, align_bytes=64)
+        apart, grouped, codes, scales = {}, {}, {}, {}
+
+        def gather(name, u, b, lo=0, hi=N):
+            if (name, b) not in apart:
+                apart[name, b] = keep.tile([P, 2, N], U32, name="apart_%s%d" % (name, b), align_bytes=64)
+                grouped[name, b] = keep.tile([P, N * PACK], BF16, name="grouped_%s%d" % (name, b), align_bytes=64)
+                codes[name, b] = place(("codes_" + name, b), seqs, [P, N], U32)
+                scales[name, b] = seqs.tile([P, N], U8, name="scales_" + name, align_bytes=64)
+            window = words[name, u][:, 0 : 2 * (b + 1) * SEG].bitcast(U32)
+            offsets = lists[name][:, b * COLS + lo // 16 : b * COLS + hi // 16]
+            nc.vector.tensor_copy(apart[name, b][:, u, lo:hi], window.indirect(offsets))
+
+        def weave(name, b, engine, lo=0, hi=N):
+            dest = grouped[name, b][:, lo * PACK : hi * PACK].bitcast(I32).rearrange("p (n u) -> p n u", u=2)
+            engine.tensor_copy(dest, apart[name, b][:, :, lo:hi].bitcast(I32).rearrange("p u n -> p n u"))
+
+        def quantize(name, b, lo=0, hi=N):
             nc.vector.quantize_mx(
-                out=codes[name, b][:].bitcast(FP8X4), scales=scales[name, b][:], in_=grouped[name, b][:]
+                out=codes[name, b][:, lo:hi].bitcast(FP8X4),
+                scales=scales[name, b][:, lo:hi],
+                in_=grouped[name, b][:, lo * PACK : hi * PACK],
             )
 
-        slot_scale, v_codes, v_scales, v_rows = {}, {}, {}, {}
-
         def gather_scales():
-            nc.vector.tensor_copy(s_rows[:], s_pool[:].indirect(lists[:]))
+            nc.vector.tensor_copy(s_rows[:], s_pool[:].indirect(lists["k"][:]))
 
-        def prepare_scales(b):
+        def turn_scales(b):
             bank = ps_t.tile([P, PACK, P], F32, name="bank_t")
             slots = s_rows[:, b * N : (b + 1) * N].rearrange("p (s t) -> p t s", t=PACK)
             for t in range(PACK):
                 nc.tensor.transpose(bank[:, t, :], slots[:, t, :], ident[:])
-            slot_scale[b] = seqs.tile([P, PACK], F32, name="slot_scale")
+            slot_scale[b] = place(("scale", b), seqs, [P, PACK], F32)
             nc.scalar.activation(slot_scale[b][:], bank[:, :, 0], ACT.Copy)
 
+        v_rows, v_grouped, v_codes, v_scales = {}, {}, {}, {}
+
+        def cast_values(b):
+            nc.scalar.activation(v_pool[b][:, b * SEG : (b + 1) * SEG], v_raw[b][:], ACT.Copy)
+
         def gather_values(b):
-            if VS[b] == "S":
-                nc.scalar.activation(v_pool[b][:, b * SEG : (b + 1) * SEG], v_raw[b][:], ACT.Copy)
-                g = seqs.tile([P, N, 2], BF16, name="v_rows_h")
-                nc.scalar.activation(g[:, :, 0], v_pool[b][:].indirect(lists[:, b * 32 : (b + 1) * 32]), ACT.Copy)
-                v_rows[b] = (g[:, :, 0], BF16, ident_h)
+            v_rows[b] = place(("v_rows", b), seqs, [P, N], BF16)
+            picked = v_pool[b][:].indirect(lists["k"][:, b * COLS : (b + 1) * COLS])
+            if b == 0:
+                nc.vector.tensor_copy(v_rows[b][:], picked)
             else:
-                g = seqs.tile([P, N], F32, name="v_rows")
-                nc.vector.tensor_copy(g[:], v_pool[b][:].indirect(lists[:, b * 32 : (b + 1) * 32]))
-                v_rows[b] = (g[:], F32, ident)
+                nc.scalar.activation(v_rows[b][:], picked, ACT.Copy)
 
-        def prepare_values(b):
-            rows, kind, eye = v_rows[b]
-            bank = ps_t.tile([P, PACK, P], kind, name="bank_t")
-            slots = rows.rearrange("p (s t) -> p t s", t=PACK)
-            for t in range(PACK):
-                nc.tensor.transpose(bank[:, t, :], slots[:, t, :], eye[:])
-            g = seqs.tile([P, DV * PACK], BF16, name="grouped_v", align_bytes=64)
-            nc.scalar.activation(g[:].rearrange("p (e t) -> p e t", t=PACK), bank[:].rearrange("p t e -> p e t"), ACT.Copy)
-            v_codes[b] = seqs.tile([P, DV], U32, name="codes_v", align_bytes=64)
+        def turn_values(b):
+            bank = ps_t.tile([P, 2, P], F32, name="bank_t")
+            pairs = v_rows[b][:].bitcast(F32).rearrange("p (s u) -> p u s", u=2)
+            for u in range(2):
+                nc.tensor.transpose(bank[:, u, :], pairs[:, u, :], ident[:])
+            v_grouped[b] = place(("grouped_v", b), seqs, [P, DV * PACK], BF16)
+            nc.scalar.copy(
+                v_grouped[b][:].bitcast(F32).rearrange("p (e u) -> p e u", u=2), bank[:].rearrange("p u e -> p e u")
+            )
+
+        def quantize_values(b):
+            v_codes[b] = place(("codes_v", b), seqs, [P, DV], U32)
             v_scales[b] = seqs.tile([P, DV], U8, name="scales_v", align_bytes=64)
-            nc.vector.quantize_mx(out=v_codes[b][:].bitcast(FP8X4), scales=v_scales[b][:], in_=g[:])
+            nc.vector.quantize_mx(out=v_codes[b][:].bitcast(FP8X4), scales=v_scales[b][:], in_=v_grouped[b][:])
 
-        sums, w_codes, w_scales, weights, capped, lows, w_rows = {}, {}, {}, {}, {}, {}, {}
+        capped, lows, sums, weights, w_rows, w_codes, w_scales = {}, {}, {}, {}, {}, {}, {}
 
         def score(b, j):
             bank = ps_s.tile([P, N], F32, name="bank_s")
@@ -215,152 +178,158 @@ def tile_attend_x_cluster_cap_kernel(tc, xq, kT, vT, vs, offs, qoffs, out):
                 stop=True,
             )
             if j % 2 == 0:
-                capped[b, j // 2] = work.tile([P, 2, PACK, P], F32, name="th", bufs=3)
-            if (b, j) in BY_G:
-                nc.scalar.activation(
-                    capped[b, j // 2][:, j % 2].rearrange("q t s -> q (t s)"), bank[:], ACT.Tanh, scale=0.5
-                )
-            else:
-                nc.scalar.activation(
-                    capped[b, j // 2][:, j % 2], bank[:].rearrange("q (s t) -> q t s", t=PACK), ACT.Tanh, scale=0.5
-                )
+                capped[b, j // 2] = place(("capped", b, j // 2), work, [P, 2, PACK, P], F32)
+            nc.scalar.activation(capped[b, j // 2][:, j % 2], bank[:].rearrange("q (s t) -> q t s", t=PACK), ACT.Tanh, scale=0.5)
 
         def lowest(b, h):
-            top = work.tile([P, 2], F32, name="top", bufs=3)
+            top = place(("top", b, h), work, [P, 2], F32)
             nc.vector.reduce_max(
                 top[:], capped[b, h][:].rearrange("q j t s -> q j (t s)"), axis=mybir.AxisListType.X
             )
-            lows[b, h] = work.tile([P, 2], F32, name="low", bufs=4)
-            nc.scalar.activation(lows[b, h][:], top[:], ACT.Copy, scale=-2.0)
+            lows[b, h] = work.tile([P, 2], F32, name="low")
+            nc.gpsimd.tensor_scalar(lows[b, h][:], top[:], -2.0, 0.0, ALU.mult, ALU.add)
 
         def exponent(b, j):
-            p = work.tile([P, PACK, P], F32, name="p", bufs=4)
             if j == 0:
-                sums[b] = seqs.tile([P, NQ // P], F32, name="sums")
-            i = j % 2
+                sums[b] = seqs.tile([P, TILES], F32, name="sums")
+            weights[b, j] = place(("p", b, j), work, [P, PACK, P], F32)
             nc.scalar.activation(
-                p[:], capped[b, j // 2][:, i], ACT.Exp, bias=lows[b, j // 2][:, i : i + 1], scale=2.0,
+                weights[b, j][:], capped[b, j // 2][:, j % 2], ACT.Exp, bias=lows[b, j // 2][:, j % 2 : j % 2 + 1], scale=2.0,
                 accum_out=sums[b][:, j : j + 1],
             )
-            weights[b, j] = p
 
         def weigh(b, j):
-            p = weights[b, j]
-            if (b, j) in BY_G:
-                weighed = work.tile([P, N], BF16, name="weighed", bufs=3)
-                nc.gpsimd.tensor_tensor(weighed[:], p[:].rearrange("q t s -> q (t s)"), s_rows[:, b * N : (b + 1) * N], ALU.mult)
-                turned = ps_p.tile([P, PACK, P], BF16, name="turned")
-                slots = weighed[:].rearrange("q (s t) -> q t s", t=PACK)
-                for t in range(PACK):
-                    nc.tensor.transpose(turned[:, t, :], slots[:, t, :], ident_h[:])
-            else:
-                turned = ps_p.tile([P, PACK, P], F32, name="turned")
-                for t in range(PACK):
-                    nc.tensor.transpose(turned[:, t, :], p[:, t, :], ident[:])
+            turned = ps_p.tile([P, PACK, P], F32, name="turned")
+            for t in range(PACK):
+                nc.tensor.transpose(turned[:, t, :], weights[b, j][:, t, :], ident[:])
             if j == 0:
                 w_rows[b] = seqs.tile([P, NQ, PACK], BF16, name="w", align_bytes=64)
                 w_codes[b] = seqs.tile([P, NQ], U32, name="codes_w", align_bytes=64)
                 w_scales[b] = seqs.tile([P, NQ], U8, name="scales_w", align_bytes=64)
-            w = w_rows[b][:, j * P : (j + 1) * P, :]
-            if (b, j) in BY_G:
-                nc.scalar.activation(w, turned[:].rearrange("s t q -> s q t"), ACT.Copy)
-            elif (b, j) in BY_S:
-                for t in range(PACK):
-                    nc.scalar.activation(w[:, :, t], turned[:, t, :], ACT.Copy, scale=slot_scale[b][:, t : t + 1])
-            else:
-                nc.vector.tensor_tensor(
-                    w,
-                    turned[:].rearrange("s t q -> s q t"),
-                    slot_scale[b][:].unsqueeze(1).to_broadcast([P, P, PACK]),
-                    ALU.mult,
-                )
+            nc.vector.tensor_tensor(
+                w_rows[b][:, j * P : (j + 1) * P, :],
+                turned[:].rearrange("s t q -> s q t"),
+                slot_scale[b][:].unsqueeze(1).to_broadcast([P, P, PACK]),
+                ALU.mult,
+            )
 
-        def quantize_weights(b, lo, hi):
-            here = slice(lo * P, hi * P)
+        def quantize_weights(b, h):
+            here = slice(2 * h * P, 2 * (h + 1) * P)
             nc.vector.quantize_mx(
                 out=w_codes[b][:, here].bitcast(FP8X4),
                 scales=w_scales[b][:, here],
                 in_=w_rows[b][:, here, :].rearrange("s q t -> s (q t)"),
             )
 
-        ready = {}
+        ready, factors = {}, {}
 
-        def product(b, lo, hi):
-            width = (hi - lo) * P
-            bank = ps_y.tile([P, width], F32, name="bank_y")
+        def product(b, h):
+            here = slice(2 * h * P, 2 * (h + 1) * P)
+            bank = ps_y.tile([P, 2 * P], F32, name="bank_y")
             nc.tensor.matmul_mx(
                 out=bank[:],
                 lhsT=v_codes[b][:].bitcast(FP8X4),
                 lhsT_scale=v_scales[b][:],
-                rhs=w_codes[b][:, lo * P : hi * P].bitcast(FP8X4),
-                rhs_scale=w_scales[b][:, lo * P : hi * P],
+                rhs=w_codes[b][:, here].bitcast(FP8X4),
+                rhs_scale=w_scales[b][:, here],
                 start=True,
                 stop=True,
             )
-            y = work.tile([P, width], F32, name="y", bufs=4)
-            nc.scalar.activation(y[:], bank[:], ACT.Copy)
-            ready[b, lo] = y
-
-        factors = {}
+            ready[b, h] = place(("y", b, h), work, [P, 2 * P], F32)
+            nc.scalar.activation(ready[b, h][:], bank[:], ACT.Copy)
 
         def spread(b, lo, hi):
-            inv = work.tile([P, hi - lo], F32, name="inv", bufs=2)
+            inv = place(("inv", b, lo), work, [P, hi - lo], F32)
             nc.vector.reciprocal(inv[:], sums[b][:, lo:hi])
             bank = ps_t.tile([P, hi - lo, P], F32, name="bank_t")
             for i in range(hi - lo):
                 nc.tensor.transpose(bank[:, i, :], inv[:, i : i + 1].to_broadcast([P, P]), ident[:])
-            factor = work.tile([P, (hi - lo) * P], F32, name="factor", bufs=2)
+            factor = place(("factor", b, lo), work, [P, (hi - lo) * P], F32)
             nc.scalar.activation(factor[:], bank[:].rearrange("p i q -> p (i q)"), ACT.Copy)
-            for i in range(hi - lo):
-                factors[b, lo + i] = (factor, i)
+            for h in range(lo // 2, hi // 2):
+                factors[b, h] = factor[:, (2 * h - lo) * P : (2 * h - lo + 2) * P]
 
-        def scatter(b, lo, hi):
-            factor, i = factors[b, lo]
-            first = b * 32 + 8 * lo
+        def scatter(b, h):
+            first = b * COLS + 16 * h
             nc.vector.tensor_tensor(
-                placed[b][:].indirect(qlists[:, first : first + 8 * (hi - lo)]),
-                ready[b, lo][:],
-                factor[:, i * P : (i + hi - lo) * P],
-                ALU.mult,
+                placed[b][:].indirect(lists["q"][:, first : first + 16]), ready[b, h][:], factors[b, h], ALU.mult
             )
 
         def store(b):
             nc.sync.dma_start(out=out[:, b * SEG : (b + 1) * SEG], in_=placed[b][:, b * SEG : (b + 1) * SEG])
 
-        for step in PLAN.split():
-            kind, rest = step[:2], step[2:]
-            d = [c if c in "kq" else int(c) for c in rest]
-            if kind == "ca":
-                cast(d[0], d[1], d[2], SHARES[step])
-            elif kind == "ga":
-                gather(d[0], d[1], d[2])
-            elif kind == "qu":
-                quantize(d[0], d[1])
-            elif kind == "sg":
-                gather_scales()
-            elif kind == "ss":
-                prepare_scales(d[0])
-            elif kind == "vg":
-                gather_values(d[0])
-            elif kind == "vv":
-                prepare_values(d[0])
-            elif kind == "sc":
-                score(d[0], d[1])
-            elif kind == "mx":
-                lowest(d[0], d[1])
-            elif kind == "ex":
-                exponent(d[0], d[1])
-            elif kind == "we":
-                weigh(d[0], d[1])
-            elif kind == "qw":
-                quantize_weights(d[0], d[1], d[2])
-            elif kind == "pr":
-                product(d[0], d[1], d[2])
-            elif kind == "sp":
-                spread(d[0], d[1], d[2])
-            elif kind == "sx":
-                scatter(d[0], d[1], d[2])
-            elif kind == "st":
-                store(d[0])
+        after = {
+            ("codes_k", 0): "raw_q001", ("scale", 0): "raw_k010", ("scale", 1): "raw_k011", ("grouped_v", 0): "raw_q010",
+            ("codes_k", 1): "raw_q011", ("factor", 0, 0): "raw_q110", ("factor", 0, 2): "apart_q1", ("capped", 0, 0): "raw_k110",
+        }
+        V, G = nc.vector, nc.gpsimd
+
+        def plane(name, u, b):
+            for i in range(len(raw[name, u, b])):
+                cast(name, u, b, i, V if (name, u, b, i % 2) == ("k", 0, 0, 1) else nc.scalar)
+            if (name, u) == ("q", 1):
+                for lo in (0, N // 2):
+                    gather(name, u, b, lo, lo + N // 2)
+                    weave(name, b, G, lo, lo + N // 2)
             else:
-                assert False
+                gather(name, u, b)
+                if u == 1:
+                    weave(name, b, G)
+
+        def scores(b, h):
+            score(b, 2 * h)
+            score(b, 2 * h + 1)
+            lowest(b, h)
+
+        def weights_of(b, h):
+            for j in (2 * h, 2 * h + 1):
+                exponent(b, j)
+                weigh(b, j)
+            quantize_weights(b, h)
+
+        plane("k", 0, 0)
+        plane("k", 1, 0)
+        gather_scales()
+        plane("q", 0, 0)
+        quantize("k", 0)
+        plane("q", 1, 0)
+        quantize("q", 0, 0, N // 2)
+        quantize("q", 0, N // 2, N)
+        turn_scales(0)
+        turn_scales(1)
+        plane("k", 0, 1)
+        scores(0, 0)
+        scores(0, 1)
+        plane("k", 1, 1)
+        weights_of(0, 0)
+        gather_values(0)
+        plane("q", 0, 1)
+        turn_values(0)
+        quantize_values(0)
+        quantize("k", 1)
+        weights_of(0, 1)
+        product(0, 0)
+        plane("q", 1, 1)
+        product(0, 1)
+        spread(0, 0, 2)
+        cast_values(1)
+        gather_values(1)
+        quantize("q", 1, 0, N // 2)
+        quantize("q", 1, N // 2, N)
+        scatter(0, 0)
+        spread(0, 2, 4)
+        scatter(0, 1)
+        store(0)
+        scores(1, 0)
+        scores(1, 1)
+        turn_values(1)
+        quantize_values(1)
+        weights_of(1, 0)
+        spread(1, 0, 2)
+        product(1, 0)
+        weights_of(1, 1)
+        spread(1, 2, 4)
+        product(1, 1)
+        scatter(1, 0)
+        scatter(1, 1)
+        store(1)

@@ -65,11 +65,11 @@ def tile_attend_x_cluster_cap_kernel(tc, xq, kT, vT, vs, offs, qoffs, out):
 
         nc.vector.memset(warm[:], 0.0)
         nc.scalar.activation(warm[:], warm[:], ACT.Exp)
-        nc.gpsimd.memset(s_pool[:], 0.0)
+        nc.vector.memset(s_pool[:], 0.0)
         load_rows("k", 0, 0, 4)
         nc.sync.dma_start(lists["k"][:], offs)
-        load_rows("k", 1, 0, 2)
         nc.sync.dma_start(out=s_pool[0:1, :], in_=vs[0:1, :])
+        load_rows("k", 1, 0, 2)
         nc.sync.dma_start(lists["q"][:], qoffs)
         load_rows("q", 0, 0, 2)
         load_rows("q", 1, 0, 2)
@@ -108,14 +108,19 @@ def tile_attend_x_cluster_cap_kernel(tc, xq, kT, vT, vs, offs, qoffs, out):
                 apart[name, b] = keep.tile([P, 2, N], U32, name="apart_%s%d" % (name, b), align_bytes=64)
                 grouped[name, b] = keep.tile([P, N * PACK], BF16, name="grouped_%s%d" % (name, b), align_bytes=64)
                 codes[name, b] = place(("codes_" + name, b), seqs, [P, N], U32)
-                scales[name, b] = seqs.tile([P, N], U8, name="scales_" + name, align_bytes=64)
+                scales[name, b] = keep.tile([P, N], U8, name="scales_%s%d" % (name, b), align_bytes=64)
             window = words[name, u][:, 0 : 2 * (b + 1) * SEG].bitcast(U32)
             offsets = lists[name][:, b * COLS + lo // 16 : b * COLS + hi // 16]
             nc.vector.tensor_copy(apart[name, b][:, u, lo:hi], window.indirect(offsets))
 
         def weave(name, b, engine, lo=0, hi=N):
-            dest = grouped[name, b][:, lo * PACK : hi * PACK].bitcast(I32).rearrange("p (n u) -> p n u", u=2)
-            engine.tensor_copy(dest, apart[name, b][:, :, lo:hi].bitcast(I32).rearrange("p u n -> p n u"))
+            kind = U32 if engine is nc.scalar else I32
+            dest = grouped[name, b][:, lo * PACK : hi * PACK].bitcast(kind).rearrange("p (n u) -> p n u", u=2)
+            src = apart[name, b][:, :, lo:hi].bitcast(kind).rearrange("p u n -> p n u")
+            if engine is nc.scalar:
+                nc.scalar.copy(dest, src)
+            else:
+                engine.tensor_copy(dest, src)
 
         def quantize(name, b, lo=0, hi=N):
             nc.vector.quantize_mx(
@@ -187,7 +192,7 @@ def tile_attend_x_cluster_cap_kernel(tc, xq, kT, vT, vs, offs, qoffs, out):
                 top[:], capped[b, h][:].rearrange("q j t s -> q j (t s)"), axis=mybir.AxisListType.X
             )
             lows[b, h] = work.tile([P, 2], F32, name="low")
-            nc.gpsimd.tensor_scalar(lows[b, h][:], top[:], -2.0, 0.0, ALU.mult, ALU.add)
+            nc.scalar.activation(lows[b, h][:], top[:], ACT.Copy, scale=-2.0)
 
         def exponent(b, j):
             if j == 0:
@@ -259,22 +264,26 @@ def tile_attend_x_cluster_cap_kernel(tc, xq, kT, vT, vs, offs, qoffs, out):
             nc.sync.dma_start(out=out[:, b * SEG : (b + 1) * SEG], in_=placed[b][:, b * SEG : (b + 1) * SEG])
 
         after = {
-            ("codes_k", 0): "raw_q001", ("scale", 0): "raw_k010", ("scale", 1): "raw_k011", ("grouped_v", 0): "raw_q010",
-            ("codes_k", 1): "raw_q011", ("factor", 0, 0): "raw_q110", ("factor", 0, 2): "apart_q1", ("capped", 0, 0): "raw_k110",
+            ("scale", 0): "raw_q101", ("scale", 1): "raw_k010", ("capped", 0, 0): "raw_k110", ("capped", 0, 1): "raw_k111",
+            ("codes_k", 1): "raw_q010", ("v_rows", 0): "raw_k011", ("grouped_v", 0): "raw_q011", ("factor", 0, 0): "raw_q111",
+            ("y", 0, 0): "v_raw1", ("y", 0, 1): "scales_q1", ("grouped_v", 1): "grouped_q1", ("y", 1, 0): "raw_k010",
         }
-        V, G = nc.vector, nc.gpsimd
+        V, G, H = nc.vector, nc.gpsimd, N // 2
 
         def plane(name, u, b):
             for i in range(len(raw[name, u, b])):
                 cast(name, u, b, i, V if (name, u, b, i % 2) == ("k", 0, 0, 1) else nc.scalar)
             if (name, u) == ("q", 1):
-                for lo in (0, N // 2):
-                    gather(name, u, b, lo, lo + N // 2)
-                    weave(name, b, G, lo, lo + N // 2)
+                for lo in (0, H):
+                    gather(name, u, b, lo, lo + H)
+                for lo in (0, H):
+                    weave(name, b, V, lo, lo + H)
+                for lo in (0, H):
+                    quantize(name, b, lo, lo + H)
             else:
                 gather(name, u, b)
                 if u == 1:
-                    weave(name, b, G)
+                    weave(name, b, G if b else V)
 
         def scores(b, h):
             score(b, 2 * h)
@@ -290,38 +299,33 @@ def tile_attend_x_cluster_cap_kernel(tc, xq, kT, vT, vs, offs, qoffs, out):
         plane("k", 0, 0)
         plane("k", 1, 0)
         gather_scales()
-        plane("q", 0, 0)
         quantize("k", 0)
+        plane("q", 0, 0)
         plane("q", 1, 0)
-        quantize("q", 0, 0, N // 2)
-        quantize("q", 0, N // 2, N)
         turn_scales(0)
         turn_scales(1)
         plane("k", 0, 1)
+        plane("k", 1, 1)
         scores(0, 0)
         scores(0, 1)
-        plane("k", 1, 1)
-        weights_of(0, 0)
         gather_values(0)
+        weights_of(0, 0)
         plane("q", 0, 1)
-        turn_values(0)
-        quantize_values(0)
         quantize("k", 1)
         weights_of(0, 1)
-        product(0, 0)
+        turn_values(0)
+        spread(0, 0, 4)
+        quantize_values(0)
         plane("q", 1, 1)
-        product(0, 1)
-        spread(0, 0, 2)
         cast_values(1)
+        product(0, 0)
         gather_values(1)
-        quantize("q", 1, 0, N // 2)
-        quantize("q", 1, N // 2, N)
         scatter(0, 0)
-        spread(0, 2, 4)
-        scatter(0, 1)
-        store(0)
         scores(1, 0)
         scores(1, 1)
+        product(0, 1)
+        scatter(0, 1)
+        store(0)
         turn_values(1)
         quantize_values(1)
         weights_of(1, 0)

@@ -6,8 +6,10 @@ from concourse.masks import make_identity
 P = 128
 B, N, T, D, DV, NQ = 2, 512, 2048, 512, 128, 512
 SEG = T // B
+HALF = SEG // 2
 PACK = 4
 TILES = NQ // P
+GROUP = 2 * P
 COLS = N // 16
 FLOPS = 2 * B * NQ * N * (D + DV)
 
@@ -22,81 +24,96 @@ ACT = mybir.ActivationFunctionType
 ALU = mybir.AluOpType
 
 
+def staged(name, u, b, i):
+    return "raw_%s%d%d%d" % (name, u, b, i)
+
+
+REUSES = {
+    ("placed", 0): staged("k", 0, 0, 1),
+    ("placed", 1): staged("k", 1, 0, 0),
+    ("scale", 0): staged("q", 1, 0, 1),
+    ("scale", 1): staged("k", 0, 1, 0),
+    ("capped", 0, 0): staged("k", 0, 1, 1),
+    ("capped", 0, 1): staged("k", 1, 1, 0),
+    ("codes_k", 1): staged("q", 0, 1, 0),
+    ("grouped_v", 0): staged("q", 0, 1, 1),
+    ("factor", 0, 0): staged("q", 1, 1, 1),
+    ("y", 0, 0): "v_raw1",
+    ("y", 0, 1): "scales_q1",
+    ("grouped_v", 1): "grouped_q1",
+    ("y", 1, 0): staged("k", 0, 1, 0),
+}
+CAST_BY_VECTOR = (("k", 0, 0), ("k", 1, 1))
+
+
 def tile_attend_x_cluster_cap_kernel(tc, xq, kT, vT, vs, offs, qoffs, out):
     nc = tc.nc
     with ExitStack() as ctx:
         keep = ctx.enter_context(tc.tile_pool(name="keep", bufs=1))
-        seqs = ctx.enter_context(tc.tile_pool(name="seqs", bufs=2))
-        work = ctx.enter_context(tc.tile_pool(name="work", bufs=4))
-        ps_s = ctx.enter_context(tc.psum_pool(name="ps_s", bufs=3))
+        seqs = ctx.enter_context(tc.tile_pool(name="seqs", bufs=B))
+        work = ctx.enter_context(tc.tile_pool(name="work", bufs=TILES))
+        ps_s = ctx.enter_context(tc.psum_pool(name="ps_s", bufs=TILES))
         ps_p = ctx.enter_context(tc.psum_pool(name="ps_p", bufs=2))
         ps_y = ctx.enter_context(tc.psum_pool(name="ps_y", bufs=1))
-        ps_t = ctx.enter_context(tc.psum_pool(name="ps_t", bufs=2))
+        ps_t = ctx.enter_context(tc.psum_pool(name="ps_t", bufs=1))
+
+        def place(key, pool, shape, kind):
+            if key in REUSES:
+                return keep.tile(shape, kind, name=REUSES[key], align_bytes=64)
+            return pool.tile(shape, kind, name=key[0], align_bytes=64)
 
         lists = {"k": keep.tile([P, B * COLS], U16, name="lists"), "q": keep.tile([P, B * COLS], U16, name="qlists")}
         words = {}
         for name in "kq":
             for u in range(2):
                 words[name, u] = keep.tile([P, 2 * T], BF16, name="words_%s%d" % (name, u))
-        v_pool, placed = {}, {}
-        for b in range(B):
-            v_pool[b] = keep.tile([P, (b + 1) * SEG], (F32, BF16)[b], name="v_pool%d" % b)
-            placed[b] = keep.tile([P, (b + 1) * SEG], F32, name="placed%d" % b)
+        v_pool = {0: keep.tile([P, SEG], F32, name="v_pool0"), 1: keep.tile([P, T], BF16, name="v_pool1")}
         s_pool = keep.tile([P, T], F32, name="s_pool")
         s_rows = keep.tile([P, B * N], F32, name="s_rows")
         ident = keep.tile([P, P], F32, name="ident")
-        warm = keep.tile([P, 1], F32, name="warm")
 
         source = {"k": kT.rearrange("(p j) w -> p j w", j=PACK), "q": xq.rearrange("(p j) w -> p j w", j=PACK)}
-        raw, v_raw = {}, {}
+        raw = {}
 
-        def load_rows(name, u, b, parts):
-            width = SEG // parts
-            raw[name, u, b] = []
-            for i in range(parts):
-                piece = keep.tile([P, 2, width], F32, name="raw_%s%d%d%d" % (name, u, b, i), align_bytes=64)
-                first = b * SEG + i * width
-                nc.sync.dma_start(out=piece[:], in_=source[name][:, 2 * u : 2 * u + 2, first : first + width])
-                raw[name, u, b].append((first, width, piece))
+        def load_half(name, u, b, i):
+            raw[name, u, b, i] = keep.tile([P, 2, HALF], F32, name=staged(name, u, b, i), align_bytes=64)
+            first = b * SEG + i * HALF
+            nc.sync.dma_start(out=raw[name, u, b, i][:], in_=source[name][:, 2 * u : 2 * u + 2, first : first + HALF])
 
-        def load_values(b):
-            v_raw[b] = keep.tile([P, SEG], F32, name="v_raw%d" % b, align_bytes=64) if b else v_pool[0]
-            nc.sync.dma_start(out=v_raw[b][:], in_=vT[:, b * SEG : (b + 1) * SEG])
+        def load_pair(name, u, b):
+            for i in range(2):
+                load_half(name, u, b, i)
 
-        nc.vector.memset(warm[:], 0.0)
-        nc.scalar.activation(warm[:], warm[:], ACT.Exp)
         nc.vector.memset(s_pool[:], 0.0)
-        load_rows("k", 0, 0, 4)
+
+        load_pair("k", 0, 0)
         nc.sync.dma_start(lists["k"][:], offs)
+        load_half("k", 1, 0, 0)
         nc.sync.dma_start(out=s_pool[0:1, :], in_=vs[0:1, :])
-        load_rows("k", 1, 0, 2)
+        load_half("k", 1, 0, 1)
         nc.sync.dma_start(lists["q"][:], qoffs)
-        load_rows("q", 0, 0, 2)
-        load_rows("q", 1, 0, 2)
-        load_rows("k", 0, 1, 2)
-        load_rows("k", 1, 1, 2)
-        load_values(0)
-        load_rows("q", 0, 1, 2)
-        load_rows("q", 1, 1, 2)
-        load_values(1)
+        load_pair("q", 0, 0)
+        load_pair("q", 1, 0)
+        load_pair("k", 0, 1)
+        nc.sync.dma_start(out=v_pool[0][:], in_=vT[:, 0:SEG])
+        load_pair("k", 1, 1)
+        load_pair("q", 0, 1)
+        load_pair("q", 1, 1)
+        v_raw1 = keep.tile([P, SEG], F32, name="v_raw1", align_bytes=64)
+        nc.sync.dma_start(out=v_raw1[:], in_=vT[:, SEG:T])
 
         make_identity(nc, ident[:])
-        nc.gpsimd.memset(v_pool[1][:, 0:SEG], 0.0)
+        nc.gpsimd.memset(v_pool[1][:, 0:SEG].bitcast(U32), 0)
+        placed = {}
         for b in range(B):
+            placed[b] = place(("placed", b), keep, [P, (b + 1) * SEG], F32)
             nc.gpsimd.memset(placed[b][:, b * SEG : (b + 1) * SEG], 0.0)
 
-        slot_scale = {}
-
-        def place(key, pool, shape, kind):
-            if key in after:
-                return keep.tile(shape, kind, name=after[key], align_bytes=64)
-            return pool.tile(shape, kind, name=key[0], align_bytes=64)
-
-        def cast(name, u, b, i, engine=nc.scalar):
-            first, width, piece = raw[name, u, b][i]
-            dest = words[name, u][:].rearrange("p (w e) -> p w e", e=2)[:, first : first + width, :]
-            src = piece[:].rearrange("p e w -> p w e")
-            if engine is nc.vector:
+        def cast(name, u, b, i):
+            first = b * SEG + i * HALF
+            dest = words[name, u][:].rearrange("p (w e) -> p w e", e=2)[:, first : first + HALF, :]
+            src = raw[name, u, b, i][:].rearrange("p e w -> p w e")
+            if i == 1 and (name, u, b) in CAST_BY_VECTOR:
                 nc.vector.tensor_copy(dest, src)
             else:
                 nc.scalar.activation(dest, src, ACT.Copy)
@@ -104,7 +121,7 @@ def tile_attend_x_cluster_cap_kernel(tc, xq, kT, vT, vs, offs, qoffs, out):
         apart, grouped, codes, scales = {}, {}, {}, {}
 
         def gather(name, u, b, lo=0, hi=N):
-            if (name, b) not in apart:
+            if u == 0:
                 apart[name, b] = keep.tile([P, 2, N], U32, name="apart_%s%d" % (name, b), align_bytes=64)
                 grouped[name, b] = keep.tile([P, N * PACK], BF16, name="grouped_%s%d" % (name, b), align_bytes=64)
                 codes[name, b] = place(("codes_" + name, b), seqs, [P, N], U32)
@@ -114,13 +131,8 @@ def tile_attend_x_cluster_cap_kernel(tc, xq, kT, vT, vs, offs, qoffs, out):
             nc.vector.tensor_copy(apart[name, b][:, u, lo:hi], window.indirect(offsets))
 
         def weave(name, b, engine, lo=0, hi=N):
-            kind = U32 if engine is nc.scalar else I32
-            dest = grouped[name, b][:, lo * PACK : hi * PACK].bitcast(kind).rearrange("p (n u) -> p n u", u=2)
-            src = apart[name, b][:, :, lo:hi].bitcast(kind).rearrange("p u n -> p n u")
-            if engine is nc.scalar:
-                nc.scalar.copy(dest, src)
-            else:
-                engine.tensor_copy(dest, src)
+            dest = grouped[name, b][:, lo * PACK : hi * PACK].bitcast(I32).rearrange("p (n u) -> p n u", u=2)
+            engine.tensor_copy(dest, apart[name, b][:, :, lo:hi].bitcast(I32).rearrange("p u n -> p n u"))
 
         def quantize(name, b, lo=0, hi=N):
             nc.vector.quantize_mx(
@@ -129,11 +141,25 @@ def tile_attend_x_cluster_cap_kernel(tc, xq, kT, vT, vs, offs, qoffs, out):
                 in_=grouped[name, b][:, lo * PACK : hi * PACK],
             )
 
-        def gather_scales():
-            nc.vector.tensor_copy(s_rows[:], s_pool[:].indirect(lists["k"][:]))
+        def pair(name, u, b):
+            for i in range(2):
+                cast(name, u, b, i)
+            if (name, u) == ("q", 1):
+                for lo in range(0, NQ, GROUP):
+                    gather(name, u, b, lo, lo + GROUP)
+                for lo in range(0, NQ, GROUP):
+                    weave(name, b, nc.vector, lo, lo + GROUP)
+                for lo in range(0, NQ, GROUP):
+                    quantize(name, b, lo, lo + GROUP)
+            else:
+                gather(name, u, b)
+                if u == 1:
+                    weave(name, b, nc.gpsimd if b == 1 else nc.vector)
+
+        slot_scale = {}
 
         def turn_scales(b):
-            bank = ps_t.tile([P, PACK, P], F32, name="bank_t")
+            bank = ps_s.tile([P, PACK, P], F32, name="bank_s")
             slots = s_rows[:, b * N : (b + 1) * N].rearrange("p (s t) -> p t s", t=PACK)
             for t in range(PACK):
                 nc.tensor.transpose(bank[:, t, :], slots[:, t, :], ident[:])
@@ -141,9 +167,6 @@ def tile_attend_x_cluster_cap_kernel(tc, xq, kT, vT, vs, offs, qoffs, out):
             nc.scalar.activation(slot_scale[b][:], bank[:, :, 0], ACT.Copy)
 
         v_rows, v_grouped, v_codes, v_scales = {}, {}, {}, {}
-
-        def cast_values(b):
-            nc.scalar.activation(v_pool[b][:, b * SEG : (b + 1) * SEG], v_raw[b][:], ACT.Copy)
 
         def gather_values(b):
             v_rows[b] = place(("v_rows", b), seqs, [P, N], BF16)
@@ -155,9 +178,9 @@ def tile_attend_x_cluster_cap_kernel(tc, xq, kT, vT, vs, offs, qoffs, out):
 
         def turn_values(b):
             bank = ps_t.tile([P, 2, P], F32, name="bank_t")
-            pairs = v_rows[b][:].bitcast(F32).rearrange("p (s u) -> p u s", u=2)
+            slot_words = v_rows[b][:].bitcast(F32).rearrange("p (s u) -> p u s", u=2)
             for u in range(2):
-                nc.tensor.transpose(bank[:, u, :], pairs[:, u, :], ident[:])
+                nc.tensor.transpose(bank[:, u, :], slot_words[:, u, :], ident[:])
             v_grouped[b] = place(("grouped_v", b), seqs, [P, DV * PACK], BF16)
             nc.scalar.copy(
                 v_grouped[b][:].bitcast(F32).rearrange("p (e u) -> p e u", u=2), bank[:].rearrange("p u e -> p e u")
@@ -168,69 +191,69 @@ def tile_attend_x_cluster_cap_kernel(tc, xq, kT, vT, vs, offs, qoffs, out):
             v_scales[b] = seqs.tile([P, DV], U8, name="scales_v", align_bytes=64)
             nc.vector.quantize_mx(out=v_codes[b][:].bitcast(FP8X4), scales=v_scales[b][:], in_=v_grouped[b][:])
 
-        capped, lows, sums, weights, w_rows, w_codes, w_scales = {}, {}, {}, {}, {}, {}, {}
+        capped, lows, sums, w_rows, w_codes, w_scales = {}, {}, {}, {}, {}, {}
 
-        def score(b, j):
-            bank = ps_s.tile([P, N], F32, name="bank_s")
-            cols = slice(j * P, (j + 1) * P)
-            nc.tensor.matmul_mx(
-                out=bank[:],
-                lhsT=codes["q", b][:, cols].bitcast(FP8X4),
-                lhsT_scale=scales["q", b][:, cols],
-                rhs=codes["k", b][:].bitcast(FP8X4),
-                rhs_scale=scales["k", b][:],
-                start=True,
-                stop=True,
-            )
-            if j % 2 == 0:
-                capped[b, j // 2] = place(("capped", b, j // 2), work, [P, 2, PACK, P], F32)
-            nc.scalar.activation(capped[b, j // 2][:, j % 2], bank[:].rearrange("q (s t) -> q t s", t=PACK), ACT.Tanh, scale=0.5)
-
-        def lowest(b, h):
+        def scores(b, h):
+            for i in range(2):
+                bank = ps_s.tile([P, N], F32, name="bank_s")
+                cols = slice((2 * h + i) * P, (2 * h + i + 1) * P)
+                nc.tensor.matmul_mx(
+                    out=bank[:],
+                    lhsT=codes["q", b][:, cols].bitcast(FP8X4),
+                    lhsT_scale=scales["q", b][:, cols],
+                    rhs=codes["k", b][:].bitcast(FP8X4),
+                    rhs_scale=scales["k", b][:],
+                    start=True,
+                    stop=True,
+                )
+                if i == 0:
+                    capped[b, h] = place(("capped", b, h), work, [P, 2, PACK, P], F32)
+                nc.scalar.activation(
+                    capped[b, h][:, i].rearrange("q t (c r) -> q c t r", r=PACK),
+                    bank[:].rearrange("q (c r t) -> q c t r", r=PACK, t=PACK),
+                    ACT.Tanh,
+                    scale=0.5,
+                )
             top = place(("top", b, h), work, [P, 2], F32)
-            nc.vector.reduce_max(
-                top[:], capped[b, h][:].rearrange("q j t s -> q j (t s)"), axis=mybir.AxisListType.X
-            )
+            nc.vector.reduce_max(top[:], capped[b, h][:].rearrange("q i t s -> q i (t s)"), axis=mybir.AxisListType.X)
             lows[b, h] = work.tile([P, 2], F32, name="low")
             nc.scalar.activation(lows[b, h][:], top[:], ACT.Copy, scale=-2.0)
 
-        def exponent(b, j):
-            if j == 0:
-                sums[b] = seqs.tile([P, TILES], F32, name="sums")
-            weights[b, j] = place(("p", b, j), work, [P, PACK, P], F32)
-            nc.scalar.activation(
-                weights[b, j][:], capped[b, j // 2][:, j % 2], ACT.Exp, bias=lows[b, j // 2][:, j % 2 : j % 2 + 1], scale=2.0,
-                accum_out=sums[b][:, j : j + 1],
-            )
-
-        def weigh(b, j):
-            turned = ps_p.tile([P, PACK, P], F32, name="turned")
-            for t in range(PACK):
-                nc.tensor.transpose(turned[:, t, :], weights[b, j][:, t, :], ident[:])
-            if j == 0:
-                w_rows[b] = seqs.tile([P, NQ, PACK], BF16, name="w", align_bytes=64)
-                w_codes[b] = seqs.tile([P, NQ], U32, name="codes_w", align_bytes=64)
-                w_scales[b] = seqs.tile([P, NQ], U8, name="scales_w", align_bytes=64)
-            nc.vector.tensor_tensor(
-                w_rows[b][:, j * P : (j + 1) * P, :],
-                turned[:].rearrange("s t q -> s q t"),
-                slot_scale[b][:].unsqueeze(1).to_broadcast([P, P, PACK]),
-                ALU.mult,
-            )
-
-        def quantize_weights(b, h):
-            here = slice(2 * h * P, 2 * (h + 1) * P)
+        def weights(b, h):
+            for i in range(2):
+                j = 2 * h + i
+                if j == 0:
+                    sums[b] = seqs.tile([P, TILES], F32, name="sums")
+                p = place(("p", b, j), work, [P, PACK, P], F32)
+                nc.scalar.activation(
+                    p[:], capped[b, h][:, i], ACT.Exp, bias=lows[b, h][:, i : i + 1], scale=2.0,
+                    accum_out=sums[b][:, j : j + 1],
+                )
+                turned = ps_p.tile([P, PACK, P], F32, name="turned")
+                for t in range(PACK):
+                    nc.tensor.transpose(turned[:, t, :], p[:, t, :], ident[:])
+                if j == 0:
+                    w_rows[b] = seqs.tile([P, NQ, PACK], BF16, name="w", align_bytes=64)
+                    w_codes[b] = seqs.tile([P, NQ], U32, name="codes_w", align_bytes=64)
+                    w_scales[b] = seqs.tile([P, NQ], U8, name="scales_w", align_bytes=64)
+                nc.vector.tensor_tensor(
+                    w_rows[b][:, j * P : (j + 1) * P, :],
+                    turned[:].rearrange("s t q -> s q t"),
+                    slot_scale[b][:].unsqueeze(1).to_broadcast([P, P, PACK]),
+                    ALU.mult,
+                )
+            here = slice(h * GROUP, (h + 1) * GROUP)
             nc.vector.quantize_mx(
                 out=w_codes[b][:, here].bitcast(FP8X4),
                 scales=w_scales[b][:, here],
                 in_=w_rows[b][:, here, :].rearrange("s q t -> s (q t)"),
             )
 
-        ready, factors = {}, {}
+        results, factors = {}, {}
 
         def product(b, h):
-            here = slice(2 * h * P, 2 * (h + 1) * P)
-            bank = ps_y.tile([P, 2 * P], F32, name="bank_y")
+            here = slice(h * GROUP, (h + 1) * GROUP)
+            bank = ps_y.tile([P, GROUP], F32, name="bank_y")
             nc.tensor.matmul_mx(
                 out=bank[:],
                 lhsT=v_codes[b][:].bitcast(FP8X4),
@@ -240,8 +263,8 @@ def tile_attend_x_cluster_cap_kernel(tc, xq, kT, vT, vs, offs, qoffs, out):
                 start=True,
                 stop=True,
             )
-            ready[b, h] = place(("y", b, h), work, [P, 2 * P], F32)
-            nc.scalar.activation(ready[b, h][:], bank[:], ACT.Copy)
+            results[b, h] = place(("y", b, h), work, [P, GROUP], F32)
+            nc.scalar.activation(results[b, h][:], bank[:], ACT.Copy)
 
         def spread(b, lo, hi):
             inv = place(("inv", b, lo), work, [P, hi - lo], F32)
@@ -255,69 +278,35 @@ def tile_attend_x_cluster_cap_kernel(tc, xq, kT, vT, vs, offs, qoffs, out):
                 factors[b, h] = factor[:, (2 * h - lo) * P : (2 * h - lo + 2) * P]
 
         def scatter(b, h):
-            first = b * COLS + 16 * h
-            nc.vector.tensor_tensor(
-                placed[b][:].indirect(lists["q"][:, first : first + 16]), ready[b, h][:], factors[b, h], ALU.mult
-            )
+            first = b * COLS + h * GROUP // 16
+            offsets = lists["q"][:, first : first + GROUP // 16]
+            nc.vector.tensor_tensor(placed[b][:].indirect(offsets), results[b, h][:], factors[b, h], ALU.mult)
 
         def store(b):
             nc.sync.dma_start(out=out[:, b * SEG : (b + 1) * SEG], in_=placed[b][:, b * SEG : (b + 1) * SEG])
 
-        after = {
-            ("scale", 0): "raw_q101", ("scale", 1): "raw_k010", ("capped", 0, 0): "raw_k110", ("capped", 0, 1): "raw_k111",
-            ("codes_k", 1): "raw_q010", ("v_rows", 0): "raw_k011", ("grouped_v", 0): "raw_q011", ("factor", 0, 0): "raw_q111",
-            ("y", 0, 0): "v_raw1", ("y", 0, 1): "scales_q1", ("grouped_v", 1): "grouped_q1", ("y", 1, 0): "raw_k010",
-        }
-        V, G, H = nc.vector, nc.gpsimd, N // 2
-
-        def plane(name, u, b):
-            for i in range(len(raw[name, u, b])):
-                cast(name, u, b, i, V if (name, u, b, i % 2) == ("k", 0, 0, 1) else nc.scalar)
-            if (name, u) == ("q", 1):
-                for lo in (0, H):
-                    gather(name, u, b, lo, lo + H)
-                for lo in (0, H):
-                    weave(name, b, V, lo, lo + H)
-                for lo in (0, H):
-                    quantize(name, b, lo, lo + H)
-            else:
-                gather(name, u, b)
-                if u == 1:
-                    weave(name, b, G if b else V)
-
-        def scores(b, h):
-            score(b, 2 * h)
-            score(b, 2 * h + 1)
-            lowest(b, h)
-
-        def weights_of(b, h):
-            for j in (2 * h, 2 * h + 1):
-                exponent(b, j)
-                weigh(b, j)
-            quantize_weights(b, h)
-
-        plane("k", 0, 0)
-        plane("k", 1, 0)
-        gather_scales()
+        pair("k", 0, 0)
+        pair("k", 1, 0)
+        nc.vector.tensor_copy(s_rows[:], s_pool[:].indirect(lists["k"][:]))
         quantize("k", 0)
-        plane("q", 0, 0)
-        plane("q", 1, 0)
-        turn_scales(0)
-        turn_scales(1)
-        plane("k", 0, 1)
-        plane("k", 1, 1)
-        scores(0, 0)
-        scores(0, 1)
+        pair("q", 0, 0)
+        pair("q", 1, 0)
+        for b in range(B):
+            turn_scales(b)
+        pair("k", 0, 1)
         gather_values(0)
-        weights_of(0, 0)
-        plane("q", 0, 1)
+        scores(0, 0)
+        pair("k", 1, 1)
+        scores(0, 1)
+        weights(0, 0)
+        pair("q", 0, 1)
         quantize("k", 1)
-        weights_of(0, 1)
+        weights(0, 1)
         turn_values(0)
-        spread(0, 0, 4)
+        spread(0, 0, TILES)
         quantize_values(0)
-        plane("q", 1, 1)
-        cast_values(1)
+        pair("q", 1, 1)
+        nc.scalar.activation(v_pool[1][:, SEG:T], v_raw1[:], ACT.Copy)
         product(0, 0)
         gather_values(1)
         scatter(0, 0)
@@ -328,12 +317,10 @@ def tile_attend_x_cluster_cap_kernel(tc, xq, kT, vT, vs, offs, qoffs, out):
         store(0)
         turn_values(1)
         quantize_values(1)
-        weights_of(1, 0)
-        spread(1, 0, 2)
-        product(1, 0)
-        weights_of(1, 1)
-        spread(1, 2, 4)
-        product(1, 1)
-        scatter(1, 0)
-        scatter(1, 1)
+        for h in range(TILES // 2):
+            weights(1, h)
+            spread(1, 2 * h, 2 * h + 2)
+            product(1, h)
+        for h in range(TILES // 2):
+            scatter(1, h)
         store(1)

@@ -29,21 +29,23 @@ def staged(name, u, b, i):
 
 
 REUSES = {
-    ("placed", 0): staged("k", 0, 0, 1),
-    ("placed", 1): staged("k", 1, 0, 0),
+    ("placed", 0): staged("k", 0, 0, 0),
+    ("placed", 1): staged("k", 0, 0, 1),
     ("scale", 0): staged("q", 1, 0, 1),
     ("scale", 1): staged("k", 0, 1, 0),
     ("capped", 0, 0): staged("k", 0, 1, 1),
-    ("capped", 0, 1): staged("k", 1, 1, 0),
-    ("codes_k", 1): staged("q", 0, 1, 0),
-    ("grouped_v", 0): staged("q", 0, 1, 1),
-    ("factor", 0, 0): staged("q", 1, 1, 1),
-    ("y", 0, 0): "v_raw1",
-    ("y", 0, 1): "scales_q1",
-    ("grouped_v", 1): "grouped_q1",
     ("y", 1, 0): staged("k", 0, 1, 0),
+    ("low", 0, 1): staged("q", 0, 1, 0),
 }
-CAST_BY_VECTOR = (("k", 0, 0), ("k", 1, 1))
+SHARED = {
+    staged("k", 1, 1, 0): (("capped", 0, 1), ("low", 0, 0), ("grouped_v", 0)),
+    staged("q", 0, 1, 1): (("codes_k", 1), ("codes_w", 0, 0), ("codes_v", 0)),
+    staged("q", 1, 1, 0): (("p", 0, 2), ("p", 0, 3)),
+    staged("q", 1, 1, 1): (("y", 0, 0), ("factor", 0, 0)),
+}
+SHARED_WORDS = 1536
+WIDE_BANKS = 6
+VECTOR_SHARE = {("k", 1, 0, 1): HALF, ("q", 1, 0, 1): 320, ("k", 1, 1, 1): HALF}
 
 
 def tile_attend_x_cluster_cap_kernel(tc, xq, kT, vT, vs, offs, qoffs, out):
@@ -52,12 +54,34 @@ def tile_attend_x_cluster_cap_kernel(tc, xq, kT, vT, vs, offs, qoffs, out):
         keep = ctx.enter_context(tc.tile_pool(name="keep", bufs=1))
         seqs = ctx.enter_context(tc.tile_pool(name="seqs", bufs=B))
         work = ctx.enter_context(tc.tile_pool(name="work", bufs=TILES))
-        ps_s = ctx.enter_context(tc.psum_pool(name="ps_s", bufs=TILES))
-        ps_p = ctx.enter_context(tc.psum_pool(name="ps_p", bufs=2))
+        ps_w = ctx.enter_context(tc.psum_pool(name="ps_w", bufs=1))
         ps_y = ctx.enter_context(tc.psum_pool(name="ps_y", bufs=1))
         ps_t = ctx.enter_context(tc.psum_pool(name="ps_t", bufs=1))
 
+        shared, used, taken = {}, {}, []
+
+        def wide_bank(shape):
+            taken.append(ps_w.tile(shape, F32, name="bank_%d" % (len(taken) % WIDE_BANKS)))
+            return taken[-1]
+
         def place(key, pool, shape, kind):
+            for tag in SHARED:
+                if key in SHARED[tag]:
+                    if tag not in shared:
+                        shared[tag] = keep.tile([P, SHARED_WORDS], F32, name=tag, align_bytes=64)
+                        used[tag] = 0
+                    count = 1
+                    for size in shape[1:]:
+                        count = count * size
+                    count = count // (2 if kind == BF16 else 1)
+                    part = shared[tag][:, used[tag] : used[tag] + count]
+                    used[tag] = used[tag] + 16 * ((count + 15) // 16)
+                    part = part if kind == F32 else part.bitcast(kind)
+                    if len(shape) == 3:
+                        return part.rearrange("p (a b) -> p a b", a=shape[1])
+                    if len(shape) == 4:
+                        return part.rearrange("p (a b c) -> p a b c", a=shape[1], b=shape[2])
+                    return part
             if key in REUSES:
                 return keep.tile(shape, kind, name=REUSES[key], align_bytes=64)
             return pool.tile(shape, kind, name=key[0], align_bytes=64)
@@ -86,17 +110,18 @@ def tile_attend_x_cluster_cap_kernel(tc, xq, kT, vT, vs, offs, qoffs, out):
 
         nc.vector.memset(s_pool[:], 0.0)
 
-        load_pair("k", 0, 0)
+        nc.scalar.dma_start(out=s_pool[0:1, :], in_=vs[0:1, :])
+        load_half("k", 0, 0, 0)
         nc.sync.dma_start(lists["k"][:], offs)
-        load_half("k", 1, 0, 0)
-        nc.sync.dma_start(out=s_pool[0:1, :], in_=vs[0:1, :])
-        load_half("k", 1, 0, 1)
+        load_half("k", 0, 0, 1)
+        load_pair("k", 1, 0)
         nc.sync.dma_start(lists["q"][:], qoffs)
         load_pair("q", 0, 0)
         load_pair("q", 1, 0)
         load_pair("k", 0, 1)
         nc.sync.dma_start(out=v_pool[0][:], in_=vT[:, 0:SEG])
-        load_pair("k", 1, 1)
+        load_half("k", 1, 1, 0)
+        load_half("k", 1, 1, 1)
         load_pair("q", 0, 1)
         load_pair("q", 1, 1)
         v_raw1 = keep.tile([P, SEG], F32, name="v_raw1", align_bytes=64)
@@ -113,10 +138,11 @@ def tile_attend_x_cluster_cap_kernel(tc, xq, kT, vT, vs, offs, qoffs, out):
             first = b * SEG + i * HALF
             dest = words[name, u][:].rearrange("p (w e) -> p w e", e=2)[:, first : first + HALF, :]
             src = raw[name, u, b, i][:].rearrange("p e w -> p w e")
-            if i == 1 and (name, u, b) in CAST_BY_VECTOR:
-                nc.vector.tensor_copy(dest, src)
-            else:
-                nc.scalar.activation(dest, src, ACT.Copy)
+            cut = HALF - VECTOR_SHARE.get((name, u, b, i), 0)
+            if cut > 0:
+                nc.scalar.activation(dest[:, 0:cut, :], src[:, 0:cut, :], ACT.Copy)
+            if cut < HALF:
+                nc.vector.tensor_copy(dest[:, cut:HALF, :], src[:, cut:HALF, :])
 
         apart, grouped, codes, scales = {}, {}, {}, {}
 
@@ -124,8 +150,6 @@ def tile_attend_x_cluster_cap_kernel(tc, xq, kT, vT, vs, offs, qoffs, out):
             if u == 0:
                 apart[name, b] = keep.tile([P, 2, N], U32, name="apart_%s%d" % (name, b), align_bytes=64)
                 grouped[name, b] = keep.tile([P, N * PACK], BF16, name="grouped_%s%d" % (name, b), align_bytes=64)
-                codes[name, b] = place(("codes_" + name, b), seqs, [P, N], U32)
-                scales[name, b] = keep.tile([P, N], U8, name="scales_%s%d" % (name, b), align_bytes=64)
             window = words[name, u][:, 0 : 2 * (b + 1) * SEG].bitcast(U32)
             offsets = lists[name][:, b * COLS + lo // 16 : b * COLS + hi // 16]
             nc.vector.tensor_copy(apart[name, b][:, u, lo:hi], window.indirect(offsets))
@@ -135,38 +159,34 @@ def tile_attend_x_cluster_cap_kernel(tc, xq, kT, vT, vs, offs, qoffs, out):
             engine.tensor_copy(dest, apart[name, b][:, :, lo:hi].bitcast(I32).rearrange("p u n -> p n u"))
 
         def quantize(name, b, lo=0, hi=N):
+            if lo == 0:
+                codes[name, b] = place(("codes_" + name, b), seqs, [P, N], U32)
+                scales[name, b] = keep.tile([P, N], U8, name="scales_%s%d" % (name, b), align_bytes=64)
             nc.vector.quantize_mx(
                 out=codes[name, b][:, lo:hi].bitcast(FP8X4),
                 scales=scales[name, b][:, lo:hi],
                 in_=grouped[name, b][:, lo * PACK : hi * PACK],
             )
 
-        def pair(name, u, b):
-            for i in range(2):
-                cast(name, u, b, i)
-            if (name, u) == ("q", 1):
-                for lo in range(0, NQ, GROUP):
-                    gather(name, u, b, lo, lo + GROUP)
-                for lo in range(0, NQ, GROUP):
-                    weave(name, b, nc.vector, lo, lo + GROUP)
-                for lo in range(0, NQ, GROUP):
-                    quantize(name, b, lo, lo + GROUP)
-            else:
-                gather(name, u, b)
-                if u == 1:
-                    weave(name, b, nc.gpsimd if b == 1 else nc.vector)
+        def finish_queries(b):
+            for lo in range(0, NQ, GROUP):
+                gather("q", 1, b, lo, lo + GROUP)
+            for lo in range(0, NQ, GROUP):
+                weave("q", b, nc.vector, lo, lo + GROUP)
+            for lo in range(0, NQ, GROUP):
+                quantize("q", b, lo, lo + GROUP)
 
         slot_scale = {}
 
         def turn_scales(b):
-            bank = ps_s.tile([P, PACK, P], F32, name="bank_s")
+            bank = wide_bank([P, PACK, P])
             slots = s_rows[:, b * N : (b + 1) * N].rearrange("p (s t) -> p t s", t=PACK)
             for t in range(PACK):
                 nc.tensor.transpose(bank[:, t, :], slots[:, t, :], ident[:])
             slot_scale[b] = place(("scale", b), seqs, [P, PACK], F32)
             nc.scalar.activation(slot_scale[b][:], bank[:, :, 0], ACT.Copy)
 
-        v_rows, v_grouped, v_codes, v_scales = {}, {}, {}, {}
+        v_rows, v_bank, v_grouped, v_codes, v_scales = {}, {}, {}, {}, {}
 
         def gather_values(b):
             v_rows[b] = place(("v_rows", b), seqs, [P, N], BF16)
@@ -181,9 +201,13 @@ def tile_attend_x_cluster_cap_kernel(tc, xq, kT, vT, vs, offs, qoffs, out):
             slot_words = v_rows[b][:].bitcast(F32).rearrange("p (s u) -> p u s", u=2)
             for u in range(2):
                 nc.tensor.transpose(bank[:, u, :], slot_words[:, u, :], ident[:])
+            v_bank[b] = bank
+
+        def take_values(b):
             v_grouped[b] = place(("grouped_v", b), seqs, [P, DV * PACK], BF16)
             nc.scalar.copy(
-                v_grouped[b][:].bitcast(F32).rearrange("p (e u) -> p e u", u=2), bank[:].rearrange("p u e -> p e u")
+                v_grouped[b][:].bitcast(F32).rearrange("p (e u) -> p e u", u=2),
+                v_bank[b][:].rearrange("p u e -> p e u"),
             )
 
         def quantize_values(b):
@@ -191,89 +215,108 @@ def tile_attend_x_cluster_cap_kernel(tc, xq, kT, vT, vs, offs, qoffs, out):
             v_scales[b] = seqs.tile([P, DV], U8, name="scales_v", align_bytes=64)
             nc.vector.quantize_mx(out=v_codes[b][:].bitcast(FP8X4), scales=v_scales[b][:], in_=v_grouped[b][:])
 
-        capped, lows, sums, w_rows, w_codes, w_scales = {}, {}, {}, {}, {}, {}
+        banks, capped, tops, lows, probs, turned = {}, {}, {}, {}, {}, {}
+        sums, w_rows, w_codes, w_scales = {}, {}, {}, {}
 
-        def scores(b, h):
-            for i in range(2):
-                bank = ps_s.tile([P, N], F32, name="bank_s")
-                cols = slice((2 * h + i) * P, (2 * h + i + 1) * P)
-                nc.tensor.matmul_mx(
-                    out=bank[:],
-                    lhsT=codes["q", b][:, cols].bitcast(FP8X4),
-                    lhsT_scale=scales["q", b][:, cols],
-                    rhs=codes["k", b][:].bitcast(FP8X4),
-                    rhs_scale=scales["k", b][:],
-                    start=True,
-                    stop=True,
-                )
-                if i == 0:
-                    capped[b, h] = place(("capped", b, h), work, [P, 2, PACK, P], F32)
-                nc.scalar.activation(
-                    capped[b, h][:, i].rearrange("q t (c r) -> q c t r", r=PACK),
-                    bank[:].rearrange("q (c r t) -> q c t r", r=PACK, t=PACK),
-                    ACT.Tanh,
-                    scale=0.5,
-                )
-            top = place(("top", b, h), work, [P, 2], F32)
-            nc.vector.reduce_max(top[:], capped[b, h][:].rearrange("q i t s -> q i (t s)"), axis=mybir.AxisListType.X)
-            lows[b, h] = work.tile([P, 2], F32, name="low")
-            nc.scalar.activation(lows[b, h][:], top[:], ACT.Copy, scale=-2.0)
-
-        def weights(b, h):
-            for i in range(2):
-                j = 2 * h + i
-                if j == 0:
-                    sums[b] = seqs.tile([P, TILES], F32, name="sums")
-                p = place(("p", b, j), work, [P, PACK, P], F32)
-                nc.scalar.activation(
-                    p[:], capped[b, h][:, i], ACT.Exp, bias=lows[b, h][:, i : i + 1], scale=2.0,
-                    accum_out=sums[b][:, j : j + 1],
-                )
-                turned = ps_p.tile([P, PACK, P], F32, name="turned")
-                for t in range(PACK):
-                    nc.tensor.transpose(turned[:, t, :], p[:, t, :], ident[:])
-                if j == 0:
-                    w_rows[b] = seqs.tile([P, NQ, PACK], BF16, name="w", align_bytes=64)
-                    w_codes[b] = seqs.tile([P, NQ], U32, name="codes_w", align_bytes=64)
-                    w_scales[b] = seqs.tile([P, NQ], U8, name="scales_w", align_bytes=64)
-                nc.vector.tensor_tensor(
-                    w_rows[b][:, j * P : (j + 1) * P, :],
-                    turned[:].rearrange("s t q -> s q t"),
-                    slot_scale[b][:].unsqueeze(1).to_broadcast([P, P, PACK]),
-                    ALU.mult,
-                )
-            here = slice(h * GROUP, (h + 1) * GROUP)
-            nc.vector.quantize_mx(
-                out=w_codes[b][:, here].bitcast(FP8X4),
-                scales=w_scales[b][:, here],
-                in_=w_rows[b][:, here, :].rearrange("s q t -> s (q t)"),
-            )
-
-        results, factors = {}, {}
-
-        def product(b, h):
-            here = slice(h * GROUP, (h + 1) * GROUP)
-            bank = ps_y.tile([P, GROUP], F32, name="bank_y")
+        def scores(b, j):
+            banks[b, j] = wide_bank([P, N])
+            cols = slice(j * P, (j + 1) * P)
             nc.tensor.matmul_mx(
-                out=bank[:],
-                lhsT=v_codes[b][:].bitcast(FP8X4),
-                lhsT_scale=v_scales[b][:],
-                rhs=w_codes[b][:, here].bitcast(FP8X4),
-                rhs_scale=w_scales[b][:, here],
+                out=banks[b, j][:],
+                lhsT=codes["q", b][:, cols].bitcast(FP8X4),
+                lhsT_scale=scales["q", b][:, cols],
+                rhs=codes["k", b][:].bitcast(FP8X4),
+                rhs_scale=scales["k", b][:],
                 start=True,
                 stop=True,
             )
+
+        def cap(b, j):
+            h, i = divmod(j, 2)
+            if i == 0:
+                capped[b, h] = place(("capped", b, h), work, [P, 2, PACK, P], F32)
+            nc.scalar.activation(
+                capped[b, h][:, i].rearrange("q t (c r) -> q c t r", r=PACK),
+                banks[b, j][:].rearrange("q (c r t) -> q c t r", r=PACK, t=PACK),
+                ACT.Tanh,
+                scale=0.5,
+            )
+
+        def maxima(b, h):
+            tops[b, h] = place(("top", b, h), work, [P, 2], F32)
+            rows = capped[b, h][:].rearrange("q i t s -> q i (t s)")
+            nc.vector.reduce_max(tops[b, h][:], rows, axis=mybir.AxisListType.X)
+
+        def bias(b, h):
+            lows[b, h] = place(("low", b, h), work, [P, 2], F32)
+            nc.scalar.activation(lows[b, h][:], tops[b, h][:], ACT.Copy, scale=-2.0)
+
+        def exps(b, j):
+            h, i = divmod(j, 2)
+            if j == 0:
+                sums[b] = seqs.tile([P, TILES], F32, name="sums")
+            probs[b, j] = place(("p", b, j), work, [P, PACK, P], F32)
+            nc.scalar.activation(
+                probs[b, j][:], capped[b, h][:, i], ACT.Exp, bias=lows[b, h][:, i : i + 1], scale=2.0,
+                accum_out=sums[b][:, j : j + 1],
+            )
+
+        def turn(b, j):
+            turned[b, j] = wide_bank([P, PACK, P])
+            for t in range(PACK):
+                nc.tensor.transpose(turned[b, j][:, t, :], probs[b, j][:, t, :], ident[:])
+
+        def weigh(b, j):
+            h, i = divmod(j, 2)
+            if i == 0:
+                w_rows[b, h] = place(("w", b, h), work, [P, GROUP, PACK], BF16)
+            nc.vector.tensor_tensor(
+                w_rows[b, h][:, i * P : (i + 1) * P, :],
+                turned[b, j][:].rearrange("s t q -> s q t"),
+                slot_scale[b][:].unsqueeze(1).to_broadcast([P, P, PACK]),
+                ALU.mult,
+            )
+
+        def quantize_weights(b, h):
+            w_codes[b, h] = place(("codes_w", b, h), work, [P, GROUP], U32)
+            w_scales[b, h] = place(("scales_w", b, h), work, [P, GROUP], U8)
+            nc.vector.quantize_mx(
+                out=w_codes[b, h][:].bitcast(FP8X4),
+                scales=w_scales[b, h][:],
+                in_=w_rows[b, h][:].rearrange("s q t -> s (q t)"),
+            )
+
+        sums_y, results, factors, invs, rows_inv = {}, {}, {}, {}, {}
+
+        def product(b, h):
+            sums_y[b, h] = ps_y.tile([P, GROUP], F32, name="bank_y")
+            nc.tensor.matmul_mx(
+                out=sums_y[b, h][:],
+                lhsT=v_codes[b][:].bitcast(FP8X4),
+                lhsT_scale=v_scales[b][:],
+                rhs=w_codes[b, h][:].bitcast(FP8X4),
+                rhs_scale=w_scales[b, h][:],
+                start=True,
+                stop=True,
+            )
+
+        def take_result(b, h):
             results[b, h] = place(("y", b, h), work, [P, GROUP], F32)
-            nc.scalar.activation(results[b, h][:], bank[:], ACT.Copy)
+            nc.scalar.activation(results[b, h][:], sums_y[b, h][:], ACT.Copy)
+
+        def invert(b, lo, hi):
+            invs[b, lo] = place(("inv", b, lo), work, [P, hi - lo], F32)
+            nc.vector.reciprocal(invs[b, lo][:], sums[b][:, lo:hi])
 
         def spread(b, lo, hi):
-            inv = place(("inv", b, lo), work, [P, hi - lo], F32)
-            nc.vector.reciprocal(inv[:], sums[b][:, lo:hi])
-            bank = ps_t.tile([P, hi - lo, P], F32, name="bank_t")
+            rows_inv[b, lo] = ps_t.tile([P, hi - lo, P], F32, name="bank_t")
             for i in range(hi - lo):
-                nc.tensor.transpose(bank[:, i, :], inv[:, i : i + 1].to_broadcast([P, P]), ident[:])
+                column = invs[b, lo][:, i : i + 1].to_broadcast([P, P])
+                nc.tensor.transpose(rows_inv[b, lo][:, i, :], column, ident[:])
+
+        def take_factor(b, lo, hi):
             factor = place(("factor", b, lo), work, [P, (hi - lo) * P], F32)
-            nc.scalar.activation(factor[:], bank[:].rearrange("p i q -> p (i q)"), ACT.Copy)
+            nc.scalar.activation(factor[:], rows_inv[b, lo][:].rearrange("p i q -> p (i q)"), ACT.Copy)
             for h in range(lo // 2, hi // 2):
                 factors[b, h] = factor[:, (2 * h - lo) * P : (2 * h - lo + 2) * P]
 
@@ -285,42 +328,122 @@ def tile_attend_x_cluster_cap_kernel(tc, xq, kT, vT, vs, offs, qoffs, out):
         def store(b):
             nc.sync.dma_start(out=out[:, b * SEG : (b + 1) * SEG], in_=placed[b][:, b * SEG : (b + 1) * SEG])
 
-        pair("k", 0, 0)
-        pair("k", 1, 0)
         nc.vector.tensor_copy(s_rows[:], s_pool[:].indirect(lists["k"][:]))
-        quantize("k", 0)
-        pair("q", 0, 0)
-        pair("q", 1, 0)
-        for b in range(B):
-            turn_scales(b)
-        pair("k", 0, 1)
+        for name, u in (("k", 0), ("k", 1), ("q", 0)):
+            cast(name, u, 0, 0)
+            cast(name, u, 0, 1)
+            gather(name, u, 0)
+            if (name, u) == ("k", 1):
+                weave("k", 0, nc.vector)
+                quantize("k", 0)
+        cast("q", 1, 0, 0)
+        cast("q", 1, 0, 1)
+        finish_queries(0)
+        cast("k", 0, 1, 0)
+        turn_scales(0)
+        turn_scales(1)
+        cast("k", 0, 1, 1)
         gather_values(0)
+        gather("k", 0, 1)
         scores(0, 0)
-        pair("k", 1, 1)
         scores(0, 1)
-        weights(0, 0)
-        pair("q", 0, 1)
-        quantize("k", 1)
-        weights(0, 1)
+        scores(0, 2)
+        scores(0, 3)
         turn_values(0)
-        spread(0, 0, TILES)
+        cap(0, 0)
+        cap(0, 1)
+        maxima(0, 0)
+        cast("k", 1, 1, 0)
+        cap(0, 2)
+        cap(0, 3)
+        bias(0, 0)
+        take_values(0)
+        cast("k", 1, 1, 1)
+        gather("k", 1, 1)
+        weave("k", 1, nc.gpsimd)
+        maxima(0, 1)
+        exps(0, 0)
+        turn(0, 0)
+        exps(0, 1)
+        turn(0, 1)
+        cast("q", 0, 1, 0)
+        cast("q", 0, 1, 1)
+        weigh(0, 0)
+        weigh(0, 1)
+        invert(0, 0, 2)
+        spread(0, 0, 2)
+        cast("q", 1, 1, 0)
+        bias(0, 1)
+        cast("q", 1, 1, 1)
+        gather("q", 0, 1)
+        quantize("k", 1)
+        quantize_weights(0, 0)
         quantize_values(0)
-        pair("q", 1, 1)
-        nc.scalar.activation(v_pool[1][:, SEG:T], v_raw1[:], ACT.Copy)
         product(0, 0)
+        exps(0, 2)
+        turn(0, 2)
+        exps(0, 3)
+        turn(0, 3)
+        gather("q", 1, 1, 0, 256)
+        gather("q", 1, 1, 256, 512)
+        weave("q", 1, nc.vector, 0, 256)
+        weave("q", 1, nc.vector, 256, 512)
+        quantize("q", 1, 0, 256)
+        quantize("q", 1, 256, 512)
+        nc.scalar.activation(v_pool[1][:, SEG:T], v_raw1[:], ACT.Copy)
+        take_result(0, 0)
+        take_factor(0, 0, 2)
         gather_values(1)
-        scatter(0, 0)
         scores(1, 0)
         scores(1, 1)
+        scores(1, 2)
+        scores(1, 3)
+        weigh(0, 2)
+        invert(0, 2, 4)
+        spread(0, 2, 4)
+        weigh(0, 3)
+        cap(1, 0)
+        cap(1, 1)
+        scatter(0, 0)
+        quantize_weights(0, 1)
         product(0, 1)
+        maxima(1, 0)
+        cap(1, 2)
+        cap(1, 3)
+        take_factor(0, 2, 4)
+        turn_values(1)
+        maxima(1, 1)
+        bias(1, 0)
+        take_result(0, 1)
         scatter(0, 1)
         store(0)
-        turn_values(1)
+        exps(1, 0)
+        bias(1, 1)
+        take_values(1)
+        turn(1, 0)
+        exps(1, 1)
+        turn(1, 1)
+        exps(1, 2)
+        weigh(1, 0)
+        turn(1, 2)
+        exps(1, 3)
+        weigh(1, 1)
+        turn(1, 3)
         quantize_values(1)
-        for h in range(TILES // 2):
-            weights(1, h)
-            spread(1, 2 * h, 2 * h + 2)
-            product(1, h)
-        for h in range(TILES // 2):
-            scatter(1, h)
+        invert(1, 0, 2)
+        weigh(1, 2)
+        quantize_weights(1, 0)
+        spread(1, 0, 2)
+        product(1, 0)
+        take_factor(1, 0, 2)
+        take_result(1, 0)
+        weigh(1, 3)
+        invert(1, 2, 4)
+        quantize_weights(1, 1)
+        spread(1, 2, 4)
+        product(1, 1)
+        take_factor(1, 2, 4)
+        take_result(1, 1)
+        scatter(1, 0)
+        scatter(1, 1)
         store(1)

@@ -36,6 +36,7 @@ REUSES = {
     ("capped", 0, 0): staged("k", 0, 1, 1),
     ("y", 1, 0): staged("k", 0, 1, 0),
     ("low", 0, 1): staged("q", 0, 1, 0),
+    ("apart_k", 0): "s_pool",
 }
 SHARED = {
     staged("k", 1, 1, 0): (("capped", 0, 1), ("low", 0, 0), ("grouped_v", 0)),
@@ -45,7 +46,7 @@ SHARED = {
 }
 SHARED_WORDS = 1536
 WIDE_BANKS = 6
-VECTOR_SHARE = {("k", 1, 0, 1): HALF, ("q", 1, 0, 1): 320, ("k", 1, 1, 1): HALF}
+VECTOR_SHARE = {("q", 1, 0, 1): 320, ("k", 1, 1, 1): HALF}
 
 
 def tile_attend_x_cluster_cap_kernel(tc, xq, kT, vT, vs, offs, qoffs, out):
@@ -92,7 +93,7 @@ def tile_attend_x_cluster_cap_kernel(tc, xq, kT, vT, vs, offs, qoffs, out):
             for u in range(2):
                 words[name, u] = keep.tile([P, 2 * T], BF16, name="words_%s%d" % (name, u))
         v_pool = {0: keep.tile([P, SEG], F32, name="v_pool0"), 1: keep.tile([P, T], BF16, name="v_pool1")}
-        s_pool = keep.tile([P, T], F32, name="s_pool")
+        s_pool = keep.tile([P, T], F32, name="s_pool", align_bytes=64)
         s_rows = keep.tile([P, B * N], F32, name="s_rows")
         ident = keep.tile([P, P], F32, name="ident")
 
@@ -110,10 +111,10 @@ def tile_attend_x_cluster_cap_kernel(tc, xq, kT, vT, vs, offs, qoffs, out):
 
         nc.vector.memset(s_pool[:], 0.0)
 
-        nc.scalar.dma_start(out=s_pool[0:1, :], in_=vs[0:1, :])
         load_half("k", 0, 0, 0)
         nc.sync.dma_start(lists["k"][:], offs)
         load_half("k", 0, 0, 1)
+        nc.sync.dma_start(out=s_pool[0:1, :], in_=vs[0:1, :])
         load_pair("k", 1, 0)
         nc.sync.dma_start(lists["q"][:], qoffs)
         load_pair("q", 0, 0)
@@ -148,7 +149,7 @@ def tile_attend_x_cluster_cap_kernel(tc, xq, kT, vT, vs, offs, qoffs, out):
 
         def gather(name, u, b, lo=0, hi=N):
             if u == 0:
-                apart[name, b] = keep.tile([P, 2, N], U32, name="apart_%s%d" % (name, b), align_bytes=64)
+                apart[name, b] = place(("apart_" + name, b), seqs, [P, 2, N], U32)
                 grouped[name, b] = keep.tile([P, N * PACK], BF16, name="grouped_%s%d" % (name, b), align_bytes=64)
             window = words[name, u][:, 0 : 2 * (b + 1) * SEG].bitcast(U32)
             offsets = lists[name][:, b * COLS + lo // 16 : b * COLS + hi // 16]
@@ -271,9 +272,9 @@ def tile_attend_x_cluster_cap_kernel(tc, xq, kT, vT, vs, offs, qoffs, out):
             if i == 0:
                 w_rows[b, h] = place(("w", b, h), work, [P, GROUP, PACK], BF16)
             nc.vector.tensor_tensor(
-                w_rows[b, h][:, i * P : (i + 1) * P, :],
-                turned[b, j][:].rearrange("s t q -> s q t"),
-                slot_scale[b][:].unsqueeze(1).to_broadcast([P, P, PACK]),
+                w_rows[b, h][:, i * P : (i + 1) * P, :].rearrange("s (c r) t -> s c t r", r=2),
+                turned[b, j][:].rearrange("s t (c r) -> s c t r", r=2),
+                slot_scale[b][:].unsqueeze(1).unsqueeze(3).to_broadcast([P, P // 2, PACK, 2]),
                 ALU.mult,
             )
 

@@ -37,16 +37,17 @@ REUSES = {
     ("y", 1, 0): staged("k", 0, 1, 0),
     ("low", 0, 1): staged("q", 0, 1, 0),
     ("apart_k", 0): "s_pool",
+    ("codes_k", 1): staged("q", 0, 1, 1),
 }
 SHARED = {
     staged("k", 1, 1, 0): (("capped", 0, 1), ("low", 0, 0), ("grouped_v", 0)),
-    staged("q", 0, 1, 1): (("codes_k", 1), ("codes_w", 0, 0), ("codes_v", 0)),
+    "words_q1": (("codes_w", 0, 0), ("codes_v", 0)),
     staged("q", 1, 1, 0): (("p", 0, 2), ("p", 0, 3)),
     staged("q", 1, 1, 1): (("y", 0, 0), ("factor", 0, 0)),
 }
 SHARED_WORDS = 1536
 WIDE_BANKS = 6
-VECTOR_SHARE = {("q", 1, 0, 1): 320, ("k", 1, 1, 1): HALF}
+VECTOR_SHARE = {("q", 1, 0, 1): 224, ("k", 1, 1, 1): HALF}
 
 
 def tile_attend_x_cluster_cap_kernel(tc, xq, kT, vT, vs, offs, qoffs, out):
@@ -91,7 +92,7 @@ def tile_attend_x_cluster_cap_kernel(tc, xq, kT, vT, vs, offs, qoffs, out):
         words = {}
         for name in "kq":
             for u in range(2):
-                words[name, u] = keep.tile([P, 2 * T], BF16, name="words_%s%d" % (name, u))
+                words[name, u] = keep.tile([P, 2 * T], BF16, name="words_%s%d" % (name, u), align_bytes=64)
         v_pool = {0: keep.tile([P, SEG], F32, name="v_pool0"), 1: keep.tile([P, T], BF16, name="v_pool1")}
         s_pool = keep.tile([P, T], F32, name="s_pool", align_bytes=64)
         s_rows = keep.tile([P, B * N], F32, name="s_rows")
@@ -120,8 +121,8 @@ def tile_attend_x_cluster_cap_kernel(tc, xq, kT, vT, vs, offs, qoffs, out):
         load_pair("q", 0, 0)
         load_pair("q", 1, 0)
         load_pair("k", 0, 1)
-        nc.sync.dma_start(out=v_pool[0][:], in_=vT[:, 0:SEG])
         load_half("k", 1, 1, 0)
+        nc.sync.dma_start(out=v_pool[0][:], in_=vT[:, 0:SEG])
         load_half("k", 1, 1, 1)
         load_pair("q", 0, 1)
         load_pair("q", 1, 1)
@@ -157,7 +158,22 @@ def tile_attend_x_cluster_cap_kernel(tc, xq, kT, vT, vs, offs, qoffs, out):
 
         def weave(name, b, engine, lo=0, hi=N):
             dest = grouped[name, b][:, lo * PACK : hi * PACK].bitcast(I32).rearrange("p (n u) -> p n u", u=2)
-            engine.tensor_copy(dest, apart[name, b][:, :, lo:hi].bitcast(I32).rearrange("p u n -> p n u"))
+            if engine is None:
+                dest = grouped[name, b][:, lo * PACK : hi * PACK].bitcast(U32).rearrange("p (n u) -> p n u", u=2)
+                nc.scalar.copy(dest, apart[name, b][:, :, lo:hi].rearrange("p u n -> p n u"))
+                return
+            src = apart[name, b][:, :, lo:hi].bitcast(I32)
+            if name == "q":
+                engine.tensor_copy(dest, src.rearrange("p u n -> p n u"))
+            elif b == 0:
+                engine.tensor_copy(
+                    dest.rearrange("p (t c r) u -> p c t r u", t=PACK, r=2),
+                    src.rearrange("p u (c r t) -> p c t r u", t=PACK, r=2),
+                )
+            else:
+                engine.tensor_copy(
+                    dest.rearrange("p (t s) u -> p t s u", t=PACK), src.rearrange("p u (s t) -> p t s u", t=PACK)
+                )
 
         def quantize(name, b, lo=0, hi=N):
             if lo == 0:
@@ -237,8 +253,8 @@ def tile_attend_x_cluster_cap_kernel(tc, xq, kT, vT, vs, offs, qoffs, out):
             if i == 0:
                 capped[b, h] = place(("capped", b, h), work, [P, 2, PACK, P], F32)
             nc.scalar.activation(
-                capped[b, h][:, i].rearrange("q t (c r) -> q c t r", r=PACK),
-                banks[b, j][:].rearrange("q (c r t) -> q c t r", r=PACK, t=PACK),
+                capped[b, h][:, i].rearrange("q t s -> q (t s)"),
+                banks[b, j][:],
                 ACT.Tanh,
                 scale=0.5,
             )
@@ -344,8 +360,9 @@ def tile_attend_x_cluster_cap_kernel(tc, xq, kT, vT, vs, offs, qoffs, out):
         turn_scales(0)
         turn_scales(1)
         cast("k", 0, 1, 1)
-        gather_values(0)
+        cast("k", 1, 1, 0)
         gather("k", 0, 1)
+        gather_values(0)
         scores(0, 0)
         scores(0, 1)
         scores(0, 2)
@@ -354,7 +371,6 @@ def tile_attend_x_cluster_cap_kernel(tc, xq, kT, vT, vs, offs, qoffs, out):
         cap(0, 0)
         cap(0, 1)
         maxima(0, 0)
-        cast("k", 1, 1, 0)
         cap(0, 2)
         cap(0, 3)
         bias(0, 0)
@@ -378,9 +394,6 @@ def tile_attend_x_cluster_cap_kernel(tc, xq, kT, vT, vs, offs, qoffs, out):
         cast("q", 1, 1, 1)
         gather("q", 0, 1)
         quantize("k", 1)
-        quantize_weights(0, 0)
-        quantize_values(0)
-        product(0, 0)
         exps(0, 2)
         turn(0, 2)
         exps(0, 3)
@@ -388,18 +401,21 @@ def tile_attend_x_cluster_cap_kernel(tc, xq, kT, vT, vs, offs, qoffs, out):
         gather("q", 1, 1, 0, 256)
         gather("q", 1, 1, 256, 512)
         weave("q", 1, nc.vector, 0, 256)
-        weave("q", 1, nc.vector, 256, 512)
+        quantize_weights(0, 0)
+        quantize_values(0)
+        product(0, 0)
         quantize("q", 1, 0, 256)
-        quantize("q", 1, 256, 512)
         nc.scalar.activation(v_pool[1][:, SEG:T], v_raw1[:], ACT.Copy)
-        take_result(0, 0)
+        weave("q", 1, None, 256, 512)
         take_factor(0, 0, 2)
+        take_result(0, 0)
         gather_values(1)
         scores(1, 0)
         scores(1, 1)
+        weigh(0, 2)
+        quantize("q", 1, 256, 512)
         scores(1, 2)
         scores(1, 3)
-        weigh(0, 2)
         invert(0, 2, 4)
         spread(0, 2, 4)
         weigh(0, 3)
@@ -431,19 +447,16 @@ def tile_attend_x_cluster_cap_kernel(tc, xq, kT, vT, vs, offs, qoffs, out):
         weigh(1, 1)
         turn(1, 3)
         quantize_values(1)
-        invert(1, 0, 2)
+        invert(1, 0, 4)
         weigh(1, 2)
         quantize_weights(1, 0)
-        spread(1, 0, 2)
+        spread(1, 0, 4)
         product(1, 0)
-        take_factor(1, 0, 2)
+        take_factor(1, 0, 4)
         take_result(1, 0)
         weigh(1, 3)
-        invert(1, 2, 4)
         quantize_weights(1, 1)
-        spread(1, 2, 4)
         product(1, 1)
-        take_factor(1, 2, 4)
         take_result(1, 1)
         scatter(1, 0)
         scatter(1, 1)

@@ -31,13 +31,15 @@ def staged(name, u, b, i):
 REUSES = {
     ("placed", 0): staged("k", 0, 0, 0),
     ("placed", 1): staged("k", 0, 0, 1),
-    ("scale", 0): staged("q", 1, 0, 1),
-    ("scale", 1): staged("k", 0, 1, 0),
+    ("scale", 0): staged("k", 0, 1, 0),
+    ("scale", 1): staged("q", 0, 0, 0),
     ("capped", 0, 0): staged("k", 0, 1, 1),
-    ("y", 1, 0): staged("k", 0, 1, 0),
+    ("y", 1, 0): staged("q", 0, 0, 0),
     ("low", 0, 1): staged("q", 0, 1, 0),
     ("apart_k", 0): "s_pool",
     ("codes_k", 1): staged("q", 0, 1, 1),
+    ("y", 0, 1): "top10",
+    ("grouped_v", 1): "low11",
 }
 SHARED = {
     staged("k", 1, 1, 0): (("capped", 0, 1), ("low", 0, 0), ("grouped_v", 0)),
@@ -45,9 +47,11 @@ SHARED = {
     staged("q", 1, 1, 0): (("p", 0, 2), ("p", 0, 3)),
     staged("q", 1, 1, 1): (("y", 0, 0), ("factor", 0, 0)),
 }
+OWN = {("top", 1, 0): "top10", ("low", 1, 1): "low11"}
 SHARED_WORDS = 1536
 WIDE_BANKS = 6
-VECTOR_SHARE = {("q", 1, 0, 1): 224, ("k", 1, 1, 1): HALF}
+BY_GPSIMD = ((1, 2),)
+VECTOR_SHARE = {("q", 1, 0, 1): 400, ("k", 1, 1, 1): HALF}
 
 
 def tile_attend_x_cluster_cap_kernel(tc, xq, kT, vT, vs, offs, qoffs, out):
@@ -86,6 +90,8 @@ def tile_attend_x_cluster_cap_kernel(tc, xq, kT, vT, vs, offs, qoffs, out):
                     return part
             if key in REUSES:
                 return keep.tile(shape, kind, name=REUSES[key], align_bytes=64)
+            if key in OWN:
+                return keep.tile(shape, kind, name=OWN[key], align_bytes=64)
             return pool.tile(shape, kind, name=key[0], align_bytes=64)
 
         lists = {"k": keep.tile([P, B * COLS], U16, name="lists"), "q": keep.tile([P, B * COLS], U16, name="qlists")}
@@ -252,6 +258,11 @@ def tile_attend_x_cluster_cap_kernel(tc, xq, kT, vT, vs, offs, qoffs, out):
             h, i = divmod(j, 2)
             if i == 0:
                 capped[b, h] = place(("capped", b, h), work, [P, 2, PACK, P], F32)
+            if (b, j) in BY_GPSIMD:
+                flat = capped[b, h][:, i].rearrange("q t s -> q (t s)").rearrange("q (u s e) -> q u s e", u=2, e=2)
+                src = banks[b, j][:].rearrange("q (u e s) -> q u s e", u=2, e=2)
+                nc.scalar.activation(flat, src, ACT.Tanh, scale=0.5)
+                return
             nc.scalar.activation(
                 capped[b, h][:, i].rearrange("q t s -> q (t s)"),
                 banks[b, j][:],
@@ -283,9 +294,43 @@ def tile_attend_x_cluster_cap_kernel(tc, xq, kT, vT, vs, offs, qoffs, out):
             for t in range(PACK):
                 nc.tensor.transpose(turned[b, j][:, t, :], probs[b, j][:, t, :], ident[:])
 
+        w_flat, scale_row, row_bank = {}, {}, {}
+
+        def spread_scales(b):
+            row_bank[b] = wide_bank([P, PACK, P])
+            for t in range(PACK):
+                nc.tensor.transpose(row_bank[b][:, t, :], slot_scale[b][:, t : t + 1].to_broadcast([P, P]), ident[:])
+
+        def take_scale_row(b):
+            scale_row[b] = place(("scale_row", b), seqs, [P, N], F32)
+            nc.scalar.activation(
+                scale_row[b][:].rearrange("p (u s e) -> p u s e", u=2, e=2),
+                row_bank[b][:].rearrange("p (u e) s -> p u s e", u=2), ACT.Copy,
+            )
+
+        def weigh_rows(b, j):
+            w_flat[b, j] = place(("w_flat", b, j), seqs, [P, N], BF16)
+            nc.gpsimd.tensor_tensor(
+                w_flat[b, j][:], probs[b, j][:].rearrange("q t s -> q (t s)"),
+                scale_row[b][:], ALU.mult,
+            )
+
+        def turn_words(b, j):
+            turned[b, j] = wide_bank([P, 2, P])
+            slot_words = w_flat[b, j][:].bitcast(F32).rearrange("p (u s) -> p u s", u=2)
+            for u in range(2):
+                nc.tensor.transpose(turned[b, j][:, u, :], slot_words[:, u, :], ident[:])
+
+        def take_words(b, j):
+            h, i = divmod(j, 2)
+            if (b, h) not in w_rows:
+                w_rows[b, h] = place(("w", b, h), work, [P, GROUP, PACK], BF16)
+            dest = w_rows[b, h][:, i * P : (i + 1) * P, :].rearrange("s q t -> s (q t)").bitcast(F32)
+            nc.scalar.copy(dest.rearrange("s (q u) -> s q u", u=2), turned[b, j][:].rearrange("s u q -> s q u"))
+
         def weigh(b, j):
             h, i = divmod(j, 2)
-            if i == 0:
+            if (b, h) not in w_rows:
                 w_rows[b, h] = place(("w", b, h), work, [P, GROUP, PACK], BF16)
             nc.vector.tensor_tensor(
                 w_rows[b, h][:, i * P : (i + 1) * P, :].rearrange("s (c r) t -> s c t r", r=2),
@@ -326,7 +371,10 @@ def tile_attend_x_cluster_cap_kernel(tc, xq, kT, vT, vs, offs, qoffs, out):
             nc.vector.reciprocal(invs[b, lo][:], sums[b][:, lo:hi])
 
         def spread(b, lo, hi):
-            rows_inv[b, lo] = ps_t.tile([P, hi - lo, P], F32, name="bank_t")
+            if (b, lo) == (1, 2):
+                rows_inv[b, lo] = ps_w.tile([P, hi - lo, P], F32, name="bank_%d" % ((len(taken) - 1) % WIDE_BANKS))
+            else:
+                rows_inv[b, lo] = ps_t.tile([P, hi - lo, P], F32, name="bank_t")
             for i in range(hi - lo):
                 column = invs[b, lo][:, i : i + 1].to_broadcast([P, P])
                 nc.tensor.transpose(rows_inv[b, lo][:, i, :], column, ident[:])
@@ -353,12 +401,14 @@ def tile_attend_x_cluster_cap_kernel(tc, xq, kT, vT, vs, offs, qoffs, out):
             if (name, u) == ("k", 1):
                 weave("k", 0, nc.vector)
                 quantize("k", 0)
+        turn_scales(1)
+        spread_scales(1)
         cast("q", 1, 0, 0)
         cast("q", 1, 0, 1)
+        take_scale_row(1)
         finish_queries(0)
         cast("k", 0, 1, 0)
         turn_scales(0)
-        turn_scales(1)
         cast("k", 0, 1, 1)
         cast("k", 1, 1, 0)
         gather("k", 0, 1)
@@ -436,27 +486,31 @@ def tile_attend_x_cluster_cap_kernel(tc, xq, kT, vT, vs, offs, qoffs, out):
         store(0)
         exps(1, 0)
         bias(1, 1)
-        take_values(1)
         turn(1, 0)
         exps(1, 1)
         turn(1, 1)
         exps(1, 2)
+        invert(1, 0, 2)
+        spread(1, 0, 2)
         weigh(1, 0)
-        turn(1, 2)
+        weigh_rows(1, 2)
         exps(1, 3)
+        take_values(1)
         weigh(1, 1)
-        turn(1, 3)
+        invert(1, 2, 4)
         quantize_values(1)
-        invert(1, 0, 4)
-        weigh(1, 2)
         quantize_weights(1, 0)
-        spread(1, 0, 4)
+        turn(1, 3)
+        turn_words(1, 2)
+        take_factor(1, 0, 2)
+        take_words(1, 2)
         product(1, 0)
-        take_factor(1, 0, 4)
         take_result(1, 0)
         weigh(1, 3)
         quantize_weights(1, 1)
+        spread(1, 2, 4)
         product(1, 1)
+        take_factor(1, 2, 4)
         take_result(1, 1)
         scatter(1, 0)
         scatter(1, 1)

@@ -51,7 +51,7 @@ OWN = {("top", 1, 0): "top10", ("low", 1, 1): "low11"}
 SHARED_WORDS = 1536
 WIDE_BANKS = 6
 BY_GPSIMD = ((1, 2),)
-VECTOR_SHARE = {("q", 1, 0, 1): 400, ("k", 1, 1, 1): HALF}
+VECTOR_SHARE = {("q", 0, 1, 0): 256, ("q", 1, 0, 1): 400, ("k", 1, 1, 1): HALF}
 
 
 def tile_attend_x_cluster_cap_kernel(tc, xq, kT, vT, vs, offs, qoffs, out):
@@ -142,14 +142,14 @@ def tile_attend_x_cluster_cap_kernel(tc, xq, kT, vT, vs, offs, qoffs, out):
             placed[b] = place(("placed", b), keep, [P, (b + 1) * SEG], F32)
             nc.gpsimd.memset(placed[b][:, b * SEG : (b + 1) * SEG], 0.0)
 
-        def cast(name, u, b, i):
+        def cast(name, u, b, i, parts="sv"):
             first = b * SEG + i * HALF
             dest = words[name, u][:].rearrange("p (w e) -> p w e", e=2)[:, first : first + HALF, :]
             src = raw[name, u, b, i][:].rearrange("p e w -> p w e")
             cut = HALF - VECTOR_SHARE.get((name, u, b, i), 0)
-            if cut > 0:
+            if cut > 0 and "s" in parts:
                 nc.scalar.activation(dest[:, 0:cut, :], src[:, 0:cut, :], ACT.Copy)
-            if cut < HALF:
+            if cut < HALF and "v" in parts:
                 nc.vector.tensor_copy(dest[:, cut:HALF, :], src[:, cut:HALF, :])
 
         apart, grouped, codes, scales = {}, {}, {}, {}
@@ -426,6 +426,7 @@ def tile_attend_x_cluster_cap_kernel(tc, xq, kT, vT, vs, offs, qoffs, out):
         bias(0, 0)
         take_values(0)
         cast("k", 1, 1, 1)
+        cast("q", 0, 1, 0, "v")
         gather("k", 1, 1)
         weave("k", 1, nc.gpsimd)
         maxima(0, 1)
@@ -433,7 +434,7 @@ def tile_attend_x_cluster_cap_kernel(tc, xq, kT, vT, vs, offs, qoffs, out):
         turn(0, 0)
         exps(0, 1)
         turn(0, 1)
-        cast("q", 0, 1, 0)
+        cast("q", 0, 1, 0, "s")
         cast("q", 0, 1, 1)
         weigh(0, 0)
         weigh(0, 1)

@@ -6,243 +6,162 @@ from concourse.masks import make_identity
 P = 128
 B, N, T, D, DV, NQ = 2, 512, 2048, 512, 128, 512
 SEG = T // B
-HALF = SEG // 2
 PACK = 4
 TILES = NQ // P
-GROUP = 2 * P
 COLS = N // 16
 FLOPS = 2 * B * NQ * N * (D + DV)
+FIRST, LAST = 1, 0
 
 F32 = mybir.dt.float32
 BF16 = mybir.dt.bfloat16
 U32 = mybir.dt.uint32
-I32 = mybir.dt.int32
 U16 = mybir.dt.uint16
 U8 = mybir.dt.uint8
 FP8X4 = mybir.dt.float8_e4m3fn_x4
 ACT = mybir.ActivationFunctionType
 ALU = mybir.AluOpType
-
-
-def staged(name, u, b, i):
-    return "raw_%s%d%d%d" % (name, u, b, i)
-
-
 REUSES = {
-    ("placed", 0): staged("k", 0, 0, 0),
-    ("placed", 1): staged("k", 0, 0, 1),
-    ("scale", 0): staged("k", 0, 1, 0),
-    ("scale", 1): staged("q", 0, 0, 0),
-    ("capped", 0, 0): staged("k", 0, 1, 1),
-    ("y", 1, 0): staged("q", 0, 0, 0),
-    ("low", 0, 1): staged("q", 0, 1, 0),
-    ("apart_k", 0): "s_pool",
-    ("codes_k", 1): staged("q", 0, 1, 1),
-    ("y", 0, 1): "top10",
-    ("grouped_v", 1): "low11",
+    "scale": "grouped_q_1",
+    "capped_1_0": "plane_k_1",
+    "low_1": "plane_k_3",
+    "p_1_1": "plane_q_3",
+    "codes_k_0": "p_1_0",
 }
-SHARED = {
-    staged("k", 1, 1, 0): (("capped", 0, 1), ("low", 0, 0), ("grouped_v", 0)),
-    "words_q1": (("codes_w", 0, 0), ("codes_v", 0)),
-    staged("q", 1, 1, 0): (("p", 0, 2), ("p", 0, 3)),
-    staged("q", 1, 1, 1): (("y", 0, 0), ("factor", 0, 0)),
-}
-OWN = {("top", 1, 0): "top10", ("low", 1, 1): "low11"}
-SHARED_WORDS = 1536
-WIDE_BANKS = 6
-BY_GPSIMD = ((1, 2),)
-VECTOR_SHARE = {("q", 0, 1, 0): 256, ("q", 1, 0, 1): 400, ("k", 1, 1, 1): HALF}
 
 
 def tile_attend_x_cluster_cap_kernel(tc, xq, kT, vT, vs, offs, qoffs, out):
     nc = tc.nc
     with ExitStack() as ctx:
         keep = ctx.enter_context(tc.tile_pool(name="keep", bufs=1))
-        seqs = ctx.enter_context(tc.tile_pool(name="seqs", bufs=B))
-        work = ctx.enter_context(tc.tile_pool(name="work", bufs=TILES))
-        ps_w = ctx.enter_context(tc.psum_pool(name="ps_w", bufs=1))
-        ps_y = ctx.enter_context(tc.psum_pool(name="ps_y", bufs=1))
-        ps_t = ctx.enter_context(tc.psum_pool(name="ps_t", bufs=1))
+        ps = ctx.enter_context(tc.psum_pool(name="ps", bufs=1))
 
-        shared, used, taken = {}, {}, []
+        def bank_tile(shape, number):
+            return ps.tile(shape, F32, name="bank_%d" % number)
 
-        def wide_bank(shape):
-            taken.append(ps_w.tile(shape, F32, name="bank_%d" % (len(taken) % WIDE_BANKS)))
-            return taken[-1]
+        def place(key, shape, kind):
+            own = "_".join(str(part) for part in key)
+            return keep.tile(shape, kind, name=REUSES.get(own, own), align_bytes=64)
 
-        def place(key, pool, shape, kind):
-            for tag in SHARED:
-                if key in SHARED[tag]:
-                    if tag not in shared:
-                        shared[tag] = keep.tile([P, SHARED_WORDS], F32, name=tag, align_bytes=64)
-                        used[tag] = 0
-                    count = 1
-                    for size in shape[1:]:
-                        count = count * size
-                    count = count // (2 if kind == BF16 else 1)
-                    part = shared[tag][:, used[tag] : used[tag] + count]
-                    used[tag] = used[tag] + 16 * ((count + 15) // 16)
-                    part = part if kind == F32 else part.bitcast(kind)
-                    if len(shape) == 3:
-                        return part.rearrange("p (a b) -> p a b", a=shape[1])
-                    if len(shape) == 4:
-                        return part.rearrange("p (a b c) -> p a b c", a=shape[1], b=shape[2])
-                    return part
-            if key in REUSES:
-                return keep.tile(shape, kind, name=REUSES[key], align_bytes=64)
-            if key in OWN:
-                return keep.tile(shape, kind, name=OWN[key], align_bytes=64)
-            return pool.tile(shape, kind, name=key[0], align_bytes=64)
+        def copy_on(engine, dest, src):
+            if engine == "s":
+                nc.scalar.activation(dest, src, ACT.Copy)
+            else:
+                nc.vector.tensor_copy(dest, src)
 
         lists = {"k": keep.tile([P, B * COLS], U16, name="lists"), "q": keep.tile([P, B * COLS], U16, name="qlists")}
-        words = {}
-        for name in "kq":
-            for u in range(2):
-                words[name, u] = keep.tile([P, 2 * T], BF16, name="words_%s%d" % (name, u), align_bytes=64)
-        v_pool = {0: keep.tile([P, SEG], F32, name="v_pool0"), 1: keep.tile([P, T], BF16, name="v_pool1")}
+        source = {"k": kT.rearrange("(p j) w -> p j w", j=PACK), "q": xq.rearrange("(p j) w -> p j w", j=PACK)}
+        chain = {name: keep.tile([P, (PACK + 1) * SEG], F32, name="chain_" + name, align_bytes=64) for name in "kq"}
+        window = {}
+        v_pool = {0: keep.tile([P, SEG], F32, name="v_pool0"), 1: keep.tile([P, T], F32, name="v_pool1")}
         s_pool = keep.tile([P, T], F32, name="s_pool", align_bytes=64)
         s_rows = keep.tile([P, B * N], F32, name="s_rows")
         ident = keep.tile([P, P], F32, name="ident")
 
-        source = {"k": kT.rearrange("(p j) w -> p j w", j=PACK), "q": xq.rearrange("(p j) w -> p j w", j=PACK)}
-        raw = {}
+        def load(name, b, j):
+            if b == 1:
+                window[name, b, j] = chain[name][:, j * SEG : (j + 2) * SEG]
+                dest = chain[name][:, (j + 1) * SEG : (j + 2) * SEG]
+            else:
+                plane = place(("plane", name, j), [P, SEG], F32)
+                window[name, b, j] = plane[:]
+                dest = plane[:]
+            nc.sync.dma_start(out=dest, in_=source[name][:, j, b * SEG : (b + 1) * SEG])
 
-        def load_half(name, u, b, i):
-            raw[name, u, b, i] = keep.tile([P, 2, HALF], F32, name=staged(name, u, b, i), align_bytes=64)
-            first = b * SEG + i * HALF
-            nc.sync.dma_start(out=raw[name, u, b, i][:], in_=source[name][:, 2 * u : 2 * u + 2, first : first + HALF])
+        def load_values(b):
+            nc.sync.dma_start(out=v_pool[b][:, b * SEG : (b + 1) * SEG], in_=vT[:, b * SEG : (b + 1) * SEG])
 
-        def load_pair(name, u, b):
-            for i in range(2):
-                load_half(name, u, b, i)
-
-        nc.vector.memset(s_pool[:], 0.0)
-
-        load_half("k", 0, 0, 0)
-        nc.sync.dma_start(lists["k"][:], offs)
-        load_half("k", 0, 0, 1)
-        nc.sync.dma_start(out=s_pool[0:1, :], in_=vs[0:1, :])
-        load_pair("k", 1, 0)
-        nc.sync.dma_start(lists["q"][:], qoffs)
-        load_pair("q", 0, 0)
-        load_pair("q", 1, 0)
-        load_pair("k", 0, 1)
-        load_half("k", 1, 1, 0)
-        nc.sync.dma_start(out=v_pool[0][:], in_=vT[:, 0:SEG])
-        load_half("k", 1, 1, 1)
-        load_pair("q", 0, 1)
-        load_pair("q", 1, 1)
-        v_raw1 = keep.tile([P, SEG], F32, name="v_raw1", align_bytes=64)
-        nc.sync.dma_start(out=v_raw1[:], in_=vT[:, SEG:T])
-
-        make_identity(nc, ident[:])
-        nc.gpsimd.memset(v_pool[1][:, 0:SEG].bitcast(U32), 0)
         placed = {}
-        for b in range(B):
-            placed[b] = place(("placed", b), keep, [P, (b + 1) * SEG], F32)
+
+        def clear_result(b):
+            placed[b] = place(("placed", b), [P, (b + 1) * SEG], F32)
             nc.gpsimd.memset(placed[b][:, b * SEG : (b + 1) * SEG], 0.0)
 
-        def cast(name, u, b, i, parts="sv"):
-            first = b * SEG + i * HALF
-            dest = words[name, u][:].rearrange("p (w e) -> p w e", e=2)[:, first : first + HALF, :]
-            src = raw[name, u, b, i][:].rearrange("p e w -> p w e")
-            cut = HALF - VECTOR_SHARE.get((name, u, b, i), 0)
-            if cut > 0 and "s" in parts:
-                nc.scalar.activation(dest[:, 0:cut, :], src[:, 0:cut, :], ACT.Copy)
-            if cut < HALF and "v" in parts:
-                nc.vector.tensor_copy(dest[:, cut:HALF, :], src[:, cut:HALF, :])
+        planes, grouped, codes, scales = {}, {}, {}, {}
 
-        apart, grouped, codes, scales = {}, {}, {}, {}
-
-        def gather(name, u, b, lo=0, hi=N):
-            if u == 0:
-                apart[name, b] = place(("apart_" + name, b), seqs, [P, 2, N], U32)
-                grouped[name, b] = keep.tile([P, N * PACK], BF16, name="grouped_%s%d" % (name, b), align_bytes=64)
-            window = words[name, u][:, 0 : 2 * (b + 1) * SEG].bitcast(U32)
+        def gather(name, b, j, engine, lo=0, hi=N):
+            if (name, b) not in planes:
+                planes[name, b] = place(("planes", name, b), [P, PACK, N], F32 if b == 1 else BF16)
             offsets = lists[name][:, b * COLS + lo // 16 : b * COLS + hi // 16]
-            nc.vector.tensor_copy(apart[name, b][:, u, lo:hi], window.indirect(offsets))
+            copy_on(engine, planes[name, b][:, j, lo:hi], window[name, b, j].indirect(offsets))
 
-        def weave(name, b, engine, lo=0, hi=N):
-            dest = grouped[name, b][:, lo * PACK : hi * PACK].bitcast(I32).rearrange("p (n u) -> p n u", u=2)
-            if engine is None:
-                dest = grouped[name, b][:, lo * PACK : hi * PACK].bitcast(U32).rearrange("p (n u) -> p n u", u=2)
-                nc.scalar.copy(dest, apart[name, b][:, :, lo:hi].rearrange("p u n -> p n u"))
-                return
-            src = apart[name, b][:, :, lo:hi].bitcast(I32)
+        def weave(name, b, lo=0, hi=N):
+            if (name, b) not in grouped:
+                grouped[name, b] = place(("grouped", name, b), [P, N * PACK], BF16)
+            dest = grouped[name, b][:, lo * PACK : hi * PACK]
+            src = planes[name, b][:, :, lo:hi]
             if name == "q":
-                engine.tensor_copy(dest, src.rearrange("p u n -> p n u"))
-            elif b == 0:
-                engine.tensor_copy(
-                    dest.rearrange("p (t c r) u -> p c t r u", t=PACK, r=2),
-                    src.rearrange("p u (c r t) -> p c t r u", t=PACK, r=2),
+                run = 4 if b == 1 else 8
+                nc.vector.tensor_copy(
+                    dest.rearrange("p (c i j) -> p c j i", i=run, j=PACK), src.rearrange("p j (c i) -> p c j i", i=run)
+                )
+            elif b == 1:
+                nc.vector.tensor_copy(
+                    dest.rearrange("p (t s j) -> p s j t", t=PACK, j=PACK), src.rearrange("p j (s t) -> p s j t", t=PACK)
                 )
             else:
-                engine.tensor_copy(
-                    dest.rearrange("p (t s) u -> p t s u", t=PACK), src.rearrange("p u (s t) -> p t s u", t=PACK)
+                nc.gpsimd.tensor_copy(
+                    dest.rearrange("p (t s j) -> p t s j", t=PACK, j=PACK), src.rearrange("p j (s t) -> p t s j", t=PACK)
                 )
 
         def quantize(name, b, lo=0, hi=N):
-            if lo == 0:
-                codes[name, b] = place(("codes_" + name, b), seqs, [P, N], U32)
-                scales[name, b] = keep.tile([P, N], U8, name="scales_%s%d" % (name, b), align_bytes=64)
+            if (name, b) not in codes:
+                codes[name, b] = place(("codes", name, b), [P, N], U32)
+                scales[name, b] = place(("scales", name, b), [P, N], U8)
             nc.vector.quantize_mx(
                 out=codes[name, b][:, lo:hi].bitcast(FP8X4),
                 scales=scales[name, b][:, lo:hi],
                 in_=grouped[name, b][:, lo * PACK : hi * PACK],
             )
 
-        def finish_queries(b):
-            for lo in range(0, NQ, GROUP):
-                gather("q", 1, b, lo, lo + GROUP)
-            for lo in range(0, NQ, GROUP):
-                weave("q", b, nc.vector, lo, lo + GROUP)
-            for lo in range(0, NQ, GROUP):
-                quantize("q", b, lo, lo + GROUP)
-
         slot_scale = {}
 
-        def turn_scales(b):
-            bank = wide_bank([P, PACK, P])
+        def gather_scales(engine, lo, hi):
+            copy_on(engine, s_rows[:, lo:hi], s_pool[:].indirect(lists["k"][:, lo // 16 : hi // 16]))
+
+        def turn_scales(b, engine, number):
+            bank = bank_tile([P, PACK, P], number)
             slots = s_rows[:, b * N : (b + 1) * N].rearrange("p (s t) -> p t s", t=PACK)
             for t in range(PACK):
                 nc.tensor.transpose(bank[:, t, :], slots[:, t, :], ident[:])
-            slot_scale[b] = place(("scale", b), seqs, [P, PACK], F32)
-            nc.scalar.activation(slot_scale[b][:], bank[:, :, 0], ACT.Copy)
+            if not slot_scale:
+                both = place(("scale",), [P, B * PACK], F32)
+                for seq in range(B):
+                    slot_scale[seq] = both[:, seq * PACK : (seq + 1) * PACK]
+            copy_on(engine, slot_scale[b], bank[:, :, 0])
 
         v_rows, v_bank, v_grouped, v_codes, v_scales = {}, {}, {}, {}, {}
 
-        def gather_values(b):
-            v_rows[b] = place(("v_rows", b), seqs, [P, N], BF16)
-            picked = v_pool[b][:].indirect(lists["k"][:, b * COLS : (b + 1) * COLS])
-            if b == 0:
-                nc.vector.tensor_copy(v_rows[b][:], picked)
-            else:
-                nc.scalar.activation(v_rows[b][:], picked, ACT.Copy)
+        def gather_values(b, engine):
+            v_rows[b] = place(("v_rows", b), [P, N], BF16)
+            copy_on(engine, v_rows[b][:], v_pool[b][:].indirect(lists["k"][:, b * COLS : (b + 1) * COLS]))
 
-        def turn_values(b):
-            bank = ps_t.tile([P, 2, P], F32, name="bank_t")
+        def turn_values(b, number):
+            bank = bank_tile([P, 2, P], number)
             slot_words = v_rows[b][:].bitcast(F32).rearrange("p (s u) -> p u s", u=2)
             for u in range(2):
                 nc.tensor.transpose(bank[:, u, :], slot_words[:, u, :], ident[:])
             v_bank[b] = bank
 
-        def take_values(b):
-            v_grouped[b] = place(("grouped_v", b), seqs, [P, DV * PACK], BF16)
-            nc.scalar.copy(
-                v_grouped[b][:].bitcast(F32).rearrange("p (e u) -> p e u", u=2),
-                v_bank[b][:].rearrange("p u e -> p e u"),
-            )
+        def take_values(b, engine):
+            v_grouped[b] = place(("grouped_v", b), [P, DV * PACK], BF16)
+            dest = v_grouped[b][:].bitcast(F32).rearrange("p (e u) -> p e u", u=2)
+            src = v_bank[b][:].rearrange("p u e -> p e u")
+            if engine == "s":
+                nc.scalar.copy(dest, src)
+            else:
+                nc.vector.tensor_copy(dest, src)
 
         def quantize_values(b):
-            v_codes[b] = place(("codes_v", b), seqs, [P, DV], U32)
-            v_scales[b] = seqs.tile([P, DV], U8, name="scales_v", align_bytes=64)
+            v_codes[b] = place(("codes_v", b), [P, DV], U32)
+            v_scales[b] = place(("scales_v", b), [P, DV], U8)
             nc.vector.quantize_mx(out=v_codes[b][:].bitcast(FP8X4), scales=v_scales[b][:], in_=v_grouped[b][:])
 
-        banks, capped, tops, lows, probs, turned = {}, {}, {}, {}, {}, {}
+        banks, capped, doubled, lows, probs, turned = {}, {}, {}, {}, {}, {}
+        low_tile = {}
         sums, w_rows, w_codes, w_scales = {}, {}, {}, {}
 
         def scores(b, j):
-            banks[b, j] = wide_bank([P, N])
+            banks[b, j] = bank_tile([P, N], j)
             cols = slice(j * P, (j + 1) * P)
             nc.tensor.matmul_mx(
                 out=banks[b, j][:],
@@ -254,265 +173,244 @@ def tile_attend_x_cluster_cap_kernel(tc, xq, kT, vT, vs, offs, qoffs, out):
                 stop=True,
             )
 
-        def cap(b, j):
-            h, i = divmod(j, 2)
-            if i == 0:
-                capped[b, h] = place(("capped", b, h), work, [P, 2, PACK, P], F32)
-            if (b, j) in BY_GPSIMD:
-                flat = capped[b, h][:, i].rearrange("q t s -> q (t s)").rearrange("q (u s e) -> q u s e", u=2, e=2)
-                src = banks[b, j][:].rearrange("q (u e s) -> q u s e", u=2, e=2)
-                nc.scalar.activation(flat, src, ACT.Tanh, scale=0.5)
-                return
-            nc.scalar.activation(
-                capped[b, h][:, i].rearrange("q t s -> q (t s)"),
-                banks[b, j][:],
-                ACT.Tanh,
-                scale=0.5,
+        def cap(b, j, together=1):
+            if (b, j) not in capped:
+                rows = place(("capped", b, j), [P, together, N], F32)
+                for i in range(together):
+                    capped[b, j + i] = rows[:, i]
+            nc.scalar.activation(capped[b, j], banks[b, j][:], ACT.Tanh, scale=0.5)
+
+        def maxima(b, j):
+            doubled[b, j] = capped[b, j]
+            if b not in low_tile:
+                low_tile[b] = place(("low", b), [P, TILES], F32)
+            lows[b, j] = low_tile[b][:, j : j + 1]
+            nc.vector.tensor_scalar(
+                doubled[b, j], capped[b, j], -2.0, None, ALU.mult, ALU.min, accum_out=lows[b, j]
             )
 
-        def maxima(b, h):
-            tops[b, h] = place(("top", b, h), work, [P, 2], F32)
-            rows = capped[b, h][:].rearrange("q i t s -> q i (t s)")
-            nc.vector.reduce_max(tops[b, h][:], rows, axis=mybir.AxisListType.X)
-
-        def bias(b, h):
-            lows[b, h] = place(("low", b, h), work, [P, 2], F32)
-            nc.scalar.activation(lows[b, h][:], tops[b, h][:], ACT.Copy, scale=-2.0)
-
-        def exps(b, j):
-            h, i = divmod(j, 2)
-            if j == 0:
-                sums[b] = seqs.tile([P, TILES], F32, name="sums")
-            probs[b, j] = place(("p", b, j), work, [P, PACK, P], F32)
+        def exps(b, j, together=1):
+            if b not in sums:
+                sums[b] = place(("sums", b), [P, TILES], F32)
+            if (b, j) not in probs:
+                rows = place(("p", b, j), [P, together, PACK, P], F32)
+                for i in range(together):
+                    probs[b, j + i] = rows[:, i]
             nc.scalar.activation(
-                probs[b, j][:], capped[b, h][:, i], ACT.Exp, bias=lows[b, h][:, i : i + 1], scale=2.0,
+                probs[b, j].rearrange("q t s -> q (t s)"), doubled[b, j], ACT.Exp, bias=lows[b, j], scale=-1.0,
                 accum_out=sums[b][:, j : j + 1],
             )
 
-        def turn(b, j):
-            turned[b, j] = wide_bank([P, PACK, P])
+        def turn(b, j, number):
+            turned[b, j] = bank_tile([P, PACK, P], number)
             for t in range(PACK):
                 nc.tensor.transpose(turned[b, j][:, t, :], probs[b, j][:, t, :], ident[:])
 
-        w_flat, scale_row, row_bank = {}, {}, {}
-
-        def spread_scales(b):
-            row_bank[b] = wide_bank([P, PACK, P])
-            for t in range(PACK):
-                nc.tensor.transpose(row_bank[b][:, t, :], slot_scale[b][:, t : t + 1].to_broadcast([P, P]), ident[:])
-
-        def take_scale_row(b):
-            scale_row[b] = place(("scale_row", b), seqs, [P, N], F32)
-            nc.scalar.activation(
-                scale_row[b][:].rearrange("p (u s e) -> p u s e", u=2, e=2),
-                row_bank[b][:].rearrange("p (u e) s -> p u s e", u=2), ACT.Copy,
-            )
-
-        def weigh_rows(b, j):
-            w_flat[b, j] = place(("w_flat", b, j), seqs, [P, N], BF16)
-            nc.gpsimd.tensor_tensor(
-                w_flat[b, j][:], probs[b, j][:].rearrange("q t s -> q (t s)"),
-                scale_row[b][:], ALU.mult,
-            )
-
-        def turn_words(b, j):
-            turned[b, j] = wide_bank([P, 2, P])
-            slot_words = w_flat[b, j][:].bitcast(F32).rearrange("p (u s) -> p u s", u=2)
-            for u in range(2):
-                nc.tensor.transpose(turned[b, j][:, u, :], slot_words[:, u, :], ident[:])
-
-        def take_words(b, j):
-            h, i = divmod(j, 2)
-            if (b, h) not in w_rows:
-                w_rows[b, h] = place(("w", b, h), work, [P, GROUP, PACK], BF16)
-            dest = w_rows[b, h][:, i * P : (i + 1) * P, :].rearrange("s q t -> s (q t)").bitcast(F32)
-            nc.scalar.copy(dest.rearrange("s (q u) -> s q u", u=2), turned[b, j][:].rearrange("s u q -> s q u"))
-
         def weigh(b, j):
-            h, i = divmod(j, 2)
-            if (b, h) not in w_rows:
-                w_rows[b, h] = place(("w", b, h), work, [P, GROUP, PACK], BF16)
+            if b not in w_rows:
+                w_rows[b] = place(("w", b), [P, NQ * PACK], BF16)
+            dest = w_rows[b][:, j * P * PACK : (j + 1) * P * PACK]
             nc.vector.tensor_tensor(
-                w_rows[b, h][:, i * P : (i + 1) * P, :].rearrange("s (c r) t -> s c t r", r=2),
+                dest.rearrange("s (c r t) -> s c t r", r=2, t=PACK),
                 turned[b, j][:].rearrange("s t (c r) -> s c t r", r=2),
-                slot_scale[b][:].unsqueeze(1).unsqueeze(3).to_broadcast([P, P // 2, PACK, 2]),
+                slot_scale[b].unsqueeze(1).unsqueeze(3).to_broadcast([P, P // 2, PACK, 2]),
                 ALU.mult,
             )
 
-        def quantize_weights(b, h):
-            w_codes[b, h] = place(("codes_w", b, h), work, [P, GROUP], U32)
-            w_scales[b, h] = place(("scales_w", b, h), work, [P, GROUP], U8)
+        def quantize_weights(b, lo, hi):
+            if b not in w_codes:
+                w_codes[b] = place(("codes_w", b), [P, NQ], U32)
+                w_scales[b] = place(("scales_w", b), [P, NQ], U8)
             nc.vector.quantize_mx(
-                out=w_codes[b, h][:].bitcast(FP8X4),
-                scales=w_scales[b, h][:],
-                in_=w_rows[b, h][:].rearrange("s q t -> s (q t)"),
+                out=w_codes[b][:, lo * P : hi * P].bitcast(FP8X4),
+                scales=w_scales[b][:, lo * P : hi * P],
+                in_=w_rows[b][:, lo * P * PACK : hi * P * PACK],
             )
 
         sums_y, results, factors, invs, rows_inv = {}, {}, {}, {}, {}
 
-        def product(b, h):
-            sums_y[b, h] = ps_y.tile([P, GROUP], F32, name="bank_y")
+        def product(b, lo, hi, number):
+            sums_y[b, lo] = bank_tile([P, (hi - lo) * P], number)
             nc.tensor.matmul_mx(
-                out=sums_y[b, h][:],
+                out=sums_y[b, lo][:],
                 lhsT=v_codes[b][:].bitcast(FP8X4),
                 lhsT_scale=v_scales[b][:],
-                rhs=w_codes[b, h][:].bitcast(FP8X4),
-                rhs_scale=w_scales[b, h][:],
+                rhs=w_codes[b][:, lo * P : hi * P].bitcast(FP8X4),
+                rhs_scale=w_scales[b][:, lo * P : hi * P],
                 start=True,
                 stop=True,
             )
 
-        def take_result(b, h):
-            results[b, h] = place(("y", b, h), work, [P, GROUP], F32)
-            nc.scalar.activation(results[b, h][:], sums_y[b, h][:], ACT.Copy)
-
         def invert(b, lo, hi):
-            invs[b, lo] = place(("inv", b, lo), work, [P, hi - lo], F32)
+            invs[b, lo] = place(("inv", b, lo), [P, hi - lo], F32)
             nc.vector.reciprocal(invs[b, lo][:], sums[b][:, lo:hi])
 
-        def spread(b, lo, hi):
-            if (b, lo) == (1, 2):
-                rows_inv[b, lo] = ps_w.tile([P, hi - lo, P], F32, name="bank_%d" % ((len(taken) - 1) % WIDE_BANKS))
-            else:
-                rows_inv[b, lo] = ps_t.tile([P, hi - lo, P], F32, name="bank_t")
+        def spread(b, lo, hi, number):
+            rows_inv[b, lo] = bank_tile([P, hi - lo, P], number)
             for i in range(hi - lo):
-                column = invs[b, lo][:, i : i + 1].to_broadcast([P, P])
-                nc.tensor.transpose(rows_inv[b, lo][:, i, :], column, ident[:])
+                nc.tensor.transpose(rows_inv[b, lo][:, i, :], invs[b, lo][:, i : i + 1].to_broadcast([P, P]), ident[:])
 
-        def take_factor(b, lo, hi):
-            factor = place(("factor", b, lo), work, [P, (hi - lo) * P], F32)
-            nc.scalar.activation(factor[:], rows_inv[b, lo][:].rearrange("p i q -> p (i q)"), ACT.Copy)
-            for h in range(lo // 2, hi // 2):
-                factors[b, h] = factor[:, (2 * h - lo) * P : (2 * h - lo + 2) * P]
+        def take_factor(b, lo, hi, engine):
+            factor = place(("factor", b, lo), [P, (hi - lo) * P], F32)
+            copy_on(engine, factor[:], rows_inv[b, lo][:].rearrange("p i q -> p (i q)"))
+            for j in range(lo, hi):
+                factors[b, j] = (factor, lo)
 
-        def scatter(b, h):
-            first = b * COLS + h * GROUP // 16
-            offsets = lists["q"][:, first : first + GROUP // 16]
-            nc.vector.tensor_tensor(placed[b][:].indirect(offsets), results[b, h][:], factors[b, h], ALU.mult)
+        def factor_of(b, lo, hi):
+            factor, first = factors[b, lo]
+            return factor[:, (lo - first) * P : (hi - first) * P]
+
+        def take_result(b, lo, hi, engine):
+            results[b, lo] = place(("y", b, lo), [P, (hi - lo) * P], F32)
+            copy_on(engine, results[b, lo][:], sums_y[b, lo][:])
+
+        def divide(b, lo, hi):
+            results[b, lo] = place(("y", b, lo), [P, (hi - lo) * P], F32)
+            nc.vector.tensor_tensor(results[b, lo][:], sums_y[b, lo][:], factor_of(b, lo, hi), ALU.mult)
+
+        def places(b, lo, hi):
+            return placed[b][:].indirect(lists["q"][:, b * COLS + lo * P // 16 : b * COLS + hi * P // 16])
+
+        def scatter_dividing(b, lo, hi):
+            nc.vector.tensor_tensor(places(b, lo, hi), results[b, lo][:], factor_of(b, lo, hi), ALU.mult)
+
+        def scatter(b, lo, hi, engine, first=None):
+            first = lo if first is None else first
+            copy_on(engine, places(b, lo, hi), results[b, first][:, (lo - first) * P : (hi - first) * P])
 
         def store(b):
             nc.sync.dma_start(out=out[:, b * SEG : (b + 1) * SEG], in_=placed[b][:, b * SEG : (b + 1) * SEG])
 
-        nc.vector.tensor_copy(s_rows[:], s_pool[:].indirect(lists["k"][:]))
-        for name, u in (("k", 0), ("k", 1), ("q", 0)):
-            cast(name, u, 0, 0)
-            cast(name, u, 0, 1)
-            gather(name, u, 0)
-            if (name, u) == ("k", 1):
-                weave("k", 0, nc.vector)
-                quantize("k", 0)
-        turn_scales(1)
-        spread_scales(1)
-        cast("q", 1, 0, 0)
-        cast("q", 1, 0, 1)
-        take_scale_row(1)
-        finish_queries(0)
-        cast("k", 0, 1, 0)
-        turn_scales(0)
-        cast("k", 0, 1, 1)
-        cast("k", 1, 1, 0)
-        gather("k", 0, 1)
-        gather_values(0)
-        scores(0, 0)
-        scores(0, 1)
-        scores(0, 2)
-        scores(0, 3)
-        turn_values(0)
-        cap(0, 0)
-        cap(0, 1)
-        maxima(0, 0)
-        cap(0, 2)
-        cap(0, 3)
-        bias(0, 0)
-        take_values(0)
-        cast("k", 1, 1, 1)
-        cast("q", 0, 1, 0, "v")
-        gather("k", 1, 1)
-        weave("k", 1, nc.gpsimd)
-        maxima(0, 1)
-        exps(0, 0)
-        turn(0, 0)
-        exps(0, 1)
-        turn(0, 1)
-        cast("q", 0, 1, 0, "s")
-        cast("q", 0, 1, 1)
-        weigh(0, 0)
-        weigh(0, 1)
-        invert(0, 0, 2)
-        spread(0, 0, 2)
-        cast("q", 1, 1, 0)
-        bias(0, 1)
-        cast("q", 1, 1, 1)
-        gather("q", 0, 1)
-        quantize("k", 1)
-        exps(0, 2)
-        turn(0, 2)
-        exps(0, 3)
-        turn(0, 3)
-        gather("q", 1, 1, 0, 256)
-        gather("q", 1, 1, 256, 512)
-        weave("q", 1, nc.vector, 0, 256)
-        quantize_weights(0, 0)
-        quantize_values(0)
-        product(0, 0)
-        quantize("q", 1, 0, 256)
-        nc.scalar.activation(v_pool[1][:, SEG:T], v_raw1[:], ACT.Copy)
-        weave("q", 1, None, 256, 512)
-        take_factor(0, 0, 2)
-        take_result(0, 0)
-        gather_values(1)
-        scores(1, 0)
-        scores(1, 1)
-        weigh(0, 2)
-        quantize("q", 1, 256, 512)
-        scores(1, 2)
-        scores(1, 3)
-        invert(0, 2, 4)
-        spread(0, 2, 4)
-        weigh(0, 3)
-        cap(1, 0)
-        cap(1, 1)
-        scatter(0, 0)
-        quantize_weights(0, 1)
-        product(0, 1)
-        maxima(1, 0)
-        cap(1, 2)
-        cap(1, 3)
-        take_factor(0, 2, 4)
-        turn_values(1)
-        maxima(1, 1)
-        bias(1, 0)
-        take_result(0, 1)
-        scatter(0, 1)
-        store(0)
-        exps(1, 0)
-        bias(1, 1)
-        turn(1, 0)
-        exps(1, 1)
-        turn(1, 1)
-        exps(1, 2)
-        invert(1, 0, 2)
-        spread(1, 0, 2)
-        weigh(1, 0)
-        weigh_rows(1, 2)
-        exps(1, 3)
-        take_values(1)
-        weigh(1, 1)
-        invert(1, 2, 4)
-        quantize_values(1)
-        quantize_weights(1, 0)
-        turn(1, 3)
-        turn_words(1, 2)
-        take_factor(1, 0, 2)
-        take_words(1, 2)
-        product(1, 0)
-        take_result(1, 0)
-        weigh(1, 3)
-        quantize_weights(1, 1)
-        spread(1, 2, 4)
-        product(1, 1)
-        take_factor(1, 2, 4)
-        take_result(1, 1)
-        scatter(1, 0)
-        scatter(1, 1)
-        store(1)
+        A, Z = FIRST, LAST
+        nc.vector.memset(s_pool[:], 0.0)
+        nc.vector.memset(chain["k"][:, 0:SEG], 0.0)
+        nc.vector.memset(chain["q"][:, 0:SEG], 0.0)
+        load("k", A, 0)
+        nc.sync.dma_start(lists["k"][:], offs)
+        load("k", A, 1)
+        nc.sync.dma_start(out=s_pool[0:1, :], in_=vs[0:1, :])
+        load("k", A, 2)
+        load("k", A, 3)
+        nc.sync.dma_start(lists["q"][:], qoffs)
+        for name, b in (("q", A), ("k", Z), ("q", Z)):
+            for j in range(PACK):
+                load(name, b, j)
+        load_values(A)
+        load_values(Z)
+        make_identity(nc, ident[:])
+        nc.gpsimd.memset(v_pool[1][:, 0:SEG], 0.0)
+        clear_result(A)
+        clear_result(Z)
+
+        gather("k", A, 0, "s")
+        gather("k", A, 1, "s")
+        gather_scales("v", 0, 1024)
+        gather("k", A, 2, "s")
+        gather("k", A, 3, "v")
+        weave("k", A)
+        gather("q", A, 0, "s")
+        gather("q", A, 1, "s")
+        quantize("k", A)
+        gather("q", A, 2, "v", 0, 256)
+        gather("q", A, 2, "s", 256, 512)
+        gather("q", A, 3, "v", 0, 256)
+        gather("q", A, 3, "s", 256, 512)
+        weave("q", A, 0, 256)
+        weave("q", A, 256, 512)
+        quantize("q", A, 0, 256)
+        quantize("q", A, 256, 512)
+        turn_scales(A, "v", 4)
+        turn_scales(Z, "v", 5)
+        gather("k", Z, 0, "s")
+        gather("k", Z, 1, "s")
+        for j in range(4):
+            scores(A, j)
+        gather("k", Z, 2, "v")
+        gather("k", Z, 3, "v")
+        weave("k", Z)
+        cap(A, 0, 4)
+        cap(A, 1)
+        cap(A, 2)
+        cap(A, 3)
+        maxima(A, 0)
+        gather("q", Z, 0, "s")
+        maxima(A, 1)
+        exps(A, 0)
+        turn(A, 0, 4)
+        maxima(A, 2)
+        maxima(A, 3)
+        gather("q", Z, 1, "v")
+        gather("q", Z, 2, "s", 256, 512)
+        gather("q", Z, 2, "v", 0, 256)
+        gather("q", Z, 3, "s")
+        weigh(A, 0)
+        exps(A, 1, 3)
+        turn(A, 1, 5)
+        exps(A, 2)
+        turn(A, 2, 6)
+        weave("q", Z, 0, 256)
+        quantize("k", Z)
+        exps(A, 3)
+        turn(A, 3, 7)
+        quantize("q", Z, 0, 256)
+        weave("q", Z, 256, 512)
+        scores(Z, 0)
+        scores(Z, 1)
+        weigh(A, 1)
+        quantize("q", Z, 256, 512)
+        gather_values(A, "s")
+        gather_values(Z, "s")
+        turn_values(A, 4)
+        scores(Z, 2)
+        scores(Z, 3)
+        cap(Z, 0)
+        cap(Z, 1)
+        invert(A, 0, 4)
+        weigh(A, 2)
+        spread(A, 0, 4, 5)
+        weigh(A, 3)
+        maxima(Z, 0)
+        take_values(A, "s")
+        turn_values(Z, 4)
+        cap(Z, 2)
+        maxima(Z, 1)
+        cap(Z, 3)
+        exps(Z, 0)
+        turn(Z, 0, 0)
+        quantize_values(A)
+        quantize_weights(A, 0, 4)
+        product(A, 0, 4, 7)
+        maxima(Z, 2)
+        exps(Z, 1)
+        maxima(Z, 3)
+        turn(Z, 1, 1)
+        take_factor(A, 0, 4, "s")
+        exps(Z, 2)
+        invert(Z, 0, 2)
+        weigh(Z, 0)
+        spread(Z, 0, 2, 6)
+        take_values(Z, "s")
+        turn(Z, 2, 2)
+        divide(A, 0, 4)
+        exps(Z, 3)
+        turn(Z, 3, 3)
+        weigh(Z, 1)
+        quantize_values(Z)
+        take_factor(Z, 0, 2, "s")
+        scatter(A, 0, 2, "s")
+        invert(Z, 2, 4)
+        quantize_weights(Z, 0, 2)
+        product(Z, 0, 2, 5)
+        spread(Z, 2, 4, 4)
+        weigh(Z, 2)
+        weigh(Z, 3)
+        divide(Z, 0, 2)
+        scatter(A, 2, 4, "s", 0)
+        store(A)
+        quantize_weights(Z, 2, 4)
+        product(Z, 2, 4, 7)
+        scatter(Z, 0, 2, "v")
+        take_factor(Z, 2, 4, "s")
+        take_result(Z, 2, 4, "s")
+        scatter_dividing(Z, 2, 4)
+        store(Z)

@@ -24,8 +24,11 @@ REUSES = {
     "scale": "grouped_q_1",
     "capped_1_0": "plane_k_1",
     "low_1": "plane_k_3",
-    "p_1_1": "plane_q_3",
-    "codes_k_0": "p_1_0",
+    "p_1_2": "plane_q_3",
+    "codes_k_0": "plane_q_2",
+    "w_1_0": "planes_q_0",
+    "grouped_v_0": "capped_0_1",
+    "y_1_2": "inv_0_0",
 }
 
 
@@ -52,7 +55,7 @@ def tile_attend_x_cluster_cap_kernel(tc, xq, kT, vT, vs, offs, qoffs, out):
         source = {"k": kT.rearrange("(p j) w -> p j w", j=PACK), "q": xq.rearrange("(p j) w -> p j w", j=PACK)}
         chain = {name: keep.tile([P, (PACK + 1) * SEG], F32, name="chain_" + name, align_bytes=64) for name in "kq"}
         window = {}
-        v_pool = {0: keep.tile([P, SEG], F32, name="v_pool0"), 1: keep.tile([P, T], F32, name="v_pool1")}
+        v_pool = keep.tile([P, T], F32, name="v_pool", align_bytes=64)
         s_pool = keep.tile([P, T], F32, name="s_pool", align_bytes=64)
         s_rows = keep.tile([P, B * N], F32, name="s_rows")
         ident = keep.tile([P, P], F32, name="ident")
@@ -67,14 +70,11 @@ def tile_attend_x_cluster_cap_kernel(tc, xq, kT, vT, vs, offs, qoffs, out):
                 dest = plane[:]
             nc.sync.dma_start(out=dest, in_=source[name][:, j, b * SEG : (b + 1) * SEG])
 
-        def load_values(b):
-            nc.sync.dma_start(out=v_pool[b][:, b * SEG : (b + 1) * SEG], in_=vT[:, b * SEG : (b + 1) * SEG])
-
         placed = {}
 
         def clear_result(b):
             placed[b] = place(("placed", b), [P, (b + 1) * SEG], F32)
-            nc.gpsimd.memset(placed[b][:, b * SEG : (b + 1) * SEG], 0.0)
+            nc.vector.memset(placed[b][:, b * SEG : (b + 1) * SEG], 0.0)
 
         planes, grouped, codes, scales = {}, {}, {}, {}
 
@@ -133,7 +133,7 @@ def tile_attend_x_cluster_cap_kernel(tc, xq, kT, vT, vs, offs, qoffs, out):
 
         def gather_values(b, engine):
             v_rows[b] = place(("v_rows", b), [P, N], BF16)
-            copy_on(engine, v_rows[b][:], v_pool[b][:].indirect(lists["k"][:, b * COLS : (b + 1) * COLS]))
+            copy_on(engine, v_rows[b][:], v_pool[:].indirect(lists["k"][:, b * COLS : (b + 1) * COLS]))
 
         def turn_values(b, number):
             bank = bank_tile([P, 2, P], number)
@@ -206,10 +206,13 @@ def tile_attend_x_cluster_cap_kernel(tc, xq, kT, vT, vs, offs, qoffs, out):
             for t in range(PACK):
                 nc.tensor.transpose(turned[b, j][:, t, :], probs[b, j][:, t, :], ident[:])
 
-        def weigh(b, j):
-            if b not in w_rows:
-                w_rows[b] = place(("w", b), [P, NQ * PACK], BF16)
-            dest = w_rows[b][:, j * P * PACK : (j + 1) * P * PACK]
+        def weigh(b, j, together=1):
+            if (b, j) not in w_rows:
+                rows = place(("w", b, j), [P, together * P * PACK], BF16)
+                for i in range(together):
+                    w_rows[b, j + i] = (rows, j)
+            rows, first = w_rows[b, j]
+            dest = rows[:, (j - first) * P * PACK : (j - first + 1) * P * PACK]
             nc.vector.tensor_tensor(
                 dest.rearrange("s (c r t) -> s c t r", r=2, t=PACK),
                 turned[b, j][:].rearrange("s t (c r) -> s c t r", r=2),
@@ -224,7 +227,7 @@ def tile_attend_x_cluster_cap_kernel(tc, xq, kT, vT, vs, offs, qoffs, out):
             nc.vector.quantize_mx(
                 out=w_codes[b][:, lo * P : hi * P].bitcast(FP8X4),
                 scales=w_scales[b][:, lo * P : hi * P],
-                in_=w_rows[b][:, lo * P * PACK : hi * P * PACK],
+                in_=w_rows[b, lo][0][:, (lo - w_rows[b, lo][1]) * P * PACK : (hi - w_rows[b, lo][1]) * P * PACK],
             )
 
         sums_y, results, factors, invs, rows_inv = {}, {}, {}, {}, {}
@@ -266,7 +269,9 @@ def tile_attend_x_cluster_cap_kernel(tc, xq, kT, vT, vs, offs, qoffs, out):
 
         def divide(b, lo, hi):
             results[b, lo] = place(("y", b, lo), [P, (hi - lo) * P], F32)
-            nc.vector.tensor_tensor(results[b, lo][:], sums_y[b, lo][:], factor_of(b, lo, hi), ALU.mult)
+            first = max(key[1] for key in sums_y if key[0] == b and key[1] <= lo)
+            sums_part = sums_y[b, first][:, (lo - first) * P : (hi - first) * P]
+            nc.vector.tensor_tensor(results[b, lo][:], sums_part, factor_of(b, lo, hi), ALU.mult)
 
         def places(b, lo, hi):
             return placed[b][:].indirect(lists["q"][:, b * COLS + lo * P // 16 : b * COLS + hi * P // 16])
@@ -295,10 +300,8 @@ def tile_attend_x_cluster_cap_kernel(tc, xq, kT, vT, vs, offs, qoffs, out):
         for name, b in (("q", A), ("k", Z), ("q", Z)):
             for j in range(PACK):
                 load(name, b, j)
-        load_values(A)
-        load_values(Z)
+        nc.sync.dma_start(out=v_pool[:], in_=vT)
         make_identity(nc, ident[:])
-        nc.gpsimd.memset(v_pool[1][:, 0:SEG], 0.0)
         clear_result(A)
         clear_result(Z)
 
@@ -337,78 +340,79 @@ def tile_attend_x_cluster_cap_kernel(tc, xq, kT, vT, vs, offs, qoffs, out):
         maxima(A, 1)
         exps(A, 0)
         turn(A, 0, 4)
+        exps(A, 1)
+        turn(A, 1, 5)
         maxima(A, 2)
         maxima(A, 3)
         gather("q", Z, 1, "v")
         gather("q", Z, 2, "s", 256, 512)
         gather("q", Z, 2, "v", 0, 256)
         gather("q", Z, 3, "s")
-        weigh(A, 0)
-        exps(A, 1, 3)
-        turn(A, 1, 5)
-        exps(A, 2)
-        turn(A, 2, 6)
-        weave("q", Z, 0, 256)
         quantize("k", Z)
+        weave("q", Z, 0, 256)
+        weave("q", Z, 256, 512)
+        quantize("q", Z, 0, 256)
+        quantize("q", Z, 256, 512)
+        exps(A, 2, 2)
+        turn(A, 2, 6)
         exps(A, 3)
         turn(A, 3, 7)
-        quantize("q", Z, 0, 256)
-        weave("q", Z, 256, 512)
-        scores(Z, 0)
-        scores(Z, 1)
-        weigh(A, 1)
-        quantize("q", Z, 256, 512)
         gather_values(A, "s")
         gather_values(Z, "s")
-        turn_values(A, 4)
+        invert(A, 0, 4)
+        scores(Z, 0)
+        scores(Z, 1)
+        weigh(A, 0, 4)
+        spread(A, 0, 4, 4)
+        weigh(A, 1)
+        turn_values(A, 5)
         scores(Z, 2)
         scores(Z, 3)
+        weigh(A, 2)
+        turn_values(Z, 6)
+        weigh(A, 3)
         cap(Z, 0)
         cap(Z, 1)
-        invert(A, 0, 4)
-        weigh(A, 2)
-        spread(A, 0, 4, 5)
-        weigh(A, 3)
-        maxima(Z, 0)
+        take_factor(A, 0, 4, "s")
         take_values(A, "s")
-        turn_values(Z, 4)
         cap(Z, 2)
-        maxima(Z, 1)
         cap(Z, 3)
-        exps(Z, 0)
-        turn(Z, 0, 0)
+        maxima(Z, 0)
         quantize_values(A)
         quantize_weights(A, 0, 4)
         product(A, 0, 4, 7)
+        maxima(Z, 1)
         maxima(Z, 2)
+        exps(Z, 0)
+        turn(Z, 0, 0)
         exps(Z, 1)
         maxima(Z, 3)
         turn(Z, 1, 1)
-        take_factor(A, 0, 4, "s")
         exps(Z, 2)
+        divide(A, 0, 2)
         invert(Z, 0, 2)
-        weigh(Z, 0)
-        spread(Z, 0, 2, 6)
+        weigh(Z, 0, 2)
+        spread(Z, 0, 2, 5)
         take_values(Z, "s")
         turn(Z, 2, 2)
-        divide(A, 0, 4)
         exps(Z, 3)
         turn(Z, 3, 3)
         weigh(Z, 1)
         quantize_values(Z)
-        take_factor(Z, 0, 2, "s")
+        divide(A, 2, 4)
         scatter(A, 0, 2, "s")
-        invert(Z, 2, 4)
+        take_factor(Z, 0, 2, "s")
         quantize_weights(Z, 0, 2)
-        product(Z, 0, 2, 5)
+        invert(Z, 2, 4)
+        product(Z, 0, 2, 0)
         spread(Z, 2, 4, 4)
-        weigh(Z, 2)
+        weigh(Z, 2, 2)
         weigh(Z, 3)
         divide(Z, 0, 2)
-        scatter(A, 2, 4, "s", 0)
+        scatter(A, 2, 4, "s")
         store(A)
         quantize_weights(Z, 2, 4)
-        product(Z, 2, 4, 7)
+        product(Z, 2, 4, 1)
         scatter(Z, 0, 2, "v")
         take_factor(Z, 2, 4, "s")
         take_result(Z, 2, 4, "s")

@@ -10,7 +10,7 @@ PACK = 4
 TILES = NQ // P
 COLS = N // 16
 FLOPS = 2 * B * NQ * N * (D + DV)
-FIRST, LAST = 1, 0
+FIRST, LAST = 0, 1
 
 F32 = mybir.dt.float32
 BF16 = mybir.dt.bfloat16
@@ -21,14 +21,16 @@ FP8X4 = mybir.dt.float8_e4m3fn_x4
 ACT = mybir.ActivationFunctionType
 ALU = mybir.AluOpType
 REUSES = {
-    "scale": "grouped_q_1",
-    "capped_1_0": "plane_k_1",
-    "low_1": "plane_k_3",
-    "p_1_2": "plane_q_3",
-    "codes_k_0": "plane_q_2",
-    "w_1_0": "planes_q_0",
-    "grouped_v_0": "capped_0_1",
-    "y_1_2": "inv_0_0",
+    "scale": "grouped_q_0_0",
+    "placed_0": "grouped_q_0_256",
+    "capped_0_0": "plane_k_1",
+    "low_0": "plane_k_3",
+    "p_0_2": "plane_q_3",
+    "codes_k_1_0": "plane_q_2",
+    "w_0_0": "planes_q_1",
+    "placed_1": "grouped_q_1_256",
+    "grouped_v_1": "capped_1_1",
+    "y_0_2": "inv_1_0",
 }
 
 
@@ -53,48 +55,45 @@ def tile_attend_x_cluster_cap_kernel(tc, xq, kT, vT, vs, offs, qoffs, out):
 
         lists = {"k": keep.tile([P, B * COLS], U16, name="lists"), "q": keep.tile([P, B * COLS], U16, name="qlists")}
         source = {"k": kT.rearrange("(p j) w -> p j w", j=PACK), "q": xq.rearrange("(p j) w -> p j w", j=PACK)}
-        chain = {name: keep.tile([P, (PACK + 1) * SEG], F32, name="chain_" + name, align_bytes=64) for name in "kq"}
-        window = {}
+        window, pool_plane = {}, {}
         v_pool = keep.tile([P, T], F32, name="v_pool", align_bytes=64)
         s_pool = keep.tile([P, T], F32, name="s_pool", align_bytes=64)
         s_rows = keep.tile([P, B * N], F32, name="s_rows")
         ident = keep.tile([P, P], F32, name="ident")
 
         def load(name, b, j):
-            if b == 1:
-                window[name, b, j] = chain[name][:, j * SEG : (j + 2) * SEG]
-                dest = chain[name][:, (j + 1) * SEG : (j + 2) * SEG]
-            else:
-                plane = place(("plane", name, j), [P, SEG], F32)
-                window[name, b, j] = plane[:]
-                dest = plane[:]
-            nc.sync.dma_start(out=dest, in_=source[name][:, j, b * SEG : (b + 1) * SEG])
+            if b == FIRST:
+                pool_plane[name, j] = place(("plane", name, j), [P, T], F32)
+            window[name, b, j] = pool_plane[name, j][:, 0 : (b + 1) * SEG]
+            tokens = slice(b * SEG, (b + 1) * SEG)
+            nc.sync.dma_start(out=pool_plane[name, j][:, tokens], in_=source[name][:, j, tokens])
 
         placed = {}
 
         def clear_result(b):
             placed[b] = place(("placed", b), [P, (b + 1) * SEG], F32)
-            nc.vector.memset(placed[b][:, b * SEG : (b + 1) * SEG], 0.0)
+            nc.gpsimd.memset(placed[b][:, b * SEG : (b + 1) * SEG].bitcast(U32), 0)
 
         planes, grouped, codes, scales = {}, {}, {}, {}
 
         def gather(name, b, j, engine, lo=0, hi=N):
             if (name, b) not in planes:
-                planes[name, b] = place(("planes", name, b), [P, PACK, N], F32 if b == 1 else BF16)
+                planes[name, b] = place(("planes", name, b), [P, PACK, N], F32 if b == FIRST else BF16)
             offsets = lists[name][:, b * COLS + lo // 16 : b * COLS + hi // 16]
             copy_on(engine, planes[name, b][:, j, lo:hi], window[name, b, j].indirect(offsets))
 
-        def weave(name, b, lo=0, hi=N):
-            if (name, b) not in grouped:
-                grouped[name, b] = place(("grouped", name, b), [P, N * PACK], BF16)
-            dest = grouped[name, b][:, lo * PACK : hi * PACK]
+        def weave(name, b, lo=0, hi=N, engine="v"):
+            grouped[name, b, lo] = place(("grouped", name, b, lo), [P, (hi - lo) * PACK], BF16)
+            dest = grouped[name, b, lo][:]
             src = planes[name, b][:, :, lo:hi]
-            if name == "q":
-                run = 4 if b == 1 else 8
+            if name == "q" and engine == "g":
+                nc.gpsimd.tensor_copy(dest.rearrange("p (n j) -> p n j", j=PACK), src.rearrange("p j n -> p n j"))
+            elif name == "q":
+                run = 4 if b == FIRST else 8
                 nc.vector.tensor_copy(
                     dest.rearrange("p (c i j) -> p c j i", i=run, j=PACK), src.rearrange("p j (c i) -> p c j i", i=run)
                 )
-            elif b == 1:
+            elif b == FIRST:
                 nc.vector.tensor_copy(
                     dest.rearrange("p (t s j) -> p s j t", t=PACK, j=PACK), src.rearrange("p j (s t) -> p s j t", t=PACK)
                 )
@@ -104,14 +103,11 @@ def tile_attend_x_cluster_cap_kernel(tc, xq, kT, vT, vs, offs, qoffs, out):
                 )
 
         def quantize(name, b, lo=0, hi=N):
-            if (name, b) not in codes:
-                codes[name, b] = place(("codes", name, b), [P, N], U32)
-                scales[name, b] = place(("scales", name, b), [P, N], U8)
-            nc.vector.quantize_mx(
-                out=codes[name, b][:, lo:hi].bitcast(FP8X4),
-                scales=scales[name, b][:, lo:hi],
-                in_=grouped[name, b][:, lo * PACK : hi * PACK],
-            )
+            part = place(("codes", name, b, lo), [P, hi - lo], U32)
+            part_scales = place(("scales", name, b, lo), [P, hi - lo], U8)
+            for j in range(lo // P, hi // P):
+                codes[name, b, j] = (part, part_scales, j * P - lo)
+            nc.vector.quantize_mx(out=part[:].bitcast(FP8X4), scales=part_scales[:], in_=grouped[name, b, lo][:])
 
         slot_scale = {}
 
@@ -162,13 +158,15 @@ def tile_attend_x_cluster_cap_kernel(tc, xq, kT, vT, vs, offs, qoffs, out):
 
         def scores(b, j):
             banks[b, j] = bank_tile([P, N], j)
-            cols = slice(j * P, (j + 1) * P)
+            q_codes, q_scales, first = codes["q", b, j]
+            k_codes, k_scales, first_key = codes["k", b, 0]
+            cols = slice(first, first + P)
             nc.tensor.matmul_mx(
                 out=banks[b, j][:],
-                lhsT=codes["q", b][:, cols].bitcast(FP8X4),
-                lhsT_scale=scales["q", b][:, cols],
-                rhs=codes["k", b][:].bitcast(FP8X4),
-                rhs_scale=scales["k", b][:],
+                lhsT=q_codes[:, cols].bitcast(FP8X4),
+                lhsT_scale=q_scales[:, cols],
+                rhs=k_codes[:].bitcast(FP8X4),
+                rhs_scale=k_scales[:],
                 start=True,
                 stop=True,
             )
@@ -287,9 +285,7 @@ def tile_attend_x_cluster_cap_kernel(tc, xq, kT, vT, vs, offs, qoffs, out):
             nc.sync.dma_start(out=out[:, b * SEG : (b + 1) * SEG], in_=placed[b][:, b * SEG : (b + 1) * SEG])
 
         A, Z = FIRST, LAST
-        nc.vector.memset(s_pool[:], 0.0)
-        nc.vector.memset(chain["k"][:, 0:SEG], 0.0)
-        nc.vector.memset(chain["q"][:, 0:SEG], 0.0)
+        nc.vector.memset(s_pool[:].bitcast(U32), 0)
         load("k", A, 0)
         nc.sync.dma_start(lists["k"][:], offs)
         load("k", A, 1)
@@ -302,8 +298,6 @@ def tile_attend_x_cluster_cap_kernel(tc, xq, kT, vT, vs, offs, qoffs, out):
                 load(name, b, j)
         nc.sync.dma_start(out=v_pool[:], in_=vT)
         make_identity(nc, ident[:])
-        clear_result(A)
-        clear_result(Z)
 
         gather("k", A, 0, "s")
         gather("k", A, 1, "s")
@@ -322,6 +316,7 @@ def tile_attend_x_cluster_cap_kernel(tc, xq, kT, vT, vs, offs, qoffs, out):
         weave("q", A, 256, 512)
         quantize("q", A, 0, 256)
         quantize("q", A, 256, 512)
+        clear_result(A)
         turn_scales(A, "v", 4)
         turn_scales(Z, "v", 5)
         gather("k", Z, 0, "s")
@@ -353,6 +348,7 @@ def tile_attend_x_cluster_cap_kernel(tc, xq, kT, vT, vs, offs, qoffs, out):
         weave("q", Z, 256, 512)
         quantize("q", Z, 0, 256)
         quantize("q", Z, 256, 512)
+        clear_result(Z)
         exps(A, 2, 2)
         turn(A, 2, 6)
         exps(A, 3)

@@ -22,13 +22,11 @@ ACT = mybir.ActivationFunctionType
 ALU = mybir.AluOpType
 REUSES = {
     "scale": "grouped_q_0_0",
-    "placed_0": "grouped_q_0_256",
     "capped_0_0": "plane_k_1",
     "low_0": "plane_k_3",
-    "p_0_2": "plane_q_3",
-    "codes_k_1_0": "plane_q_2",
+    "p_0_2": "plane_q_2",
+    "codes_k_1_0": "plane_q_3",
     "w_0_0": "planes_q_1",
-    "placed_1": "grouped_q_1_256",
     "grouped_v_1": "capped_1_1",
     "y_0_2": "inv_1_0",
 }
@@ -56,7 +54,7 @@ def tile_attend_x_cluster_cap_kernel(tc, xq, kT, vT, vs, offs, qoffs, out):
         lists = {"k": keep.tile([P, B * COLS], U16, name="lists"), "q": keep.tile([P, B * COLS], U16, name="qlists")}
         source = {"k": kT.rearrange("(p j) w -> p j w", j=PACK), "q": xq.rearrange("(p j) w -> p j w", j=PACK)}
         window, pool_plane = {}, {}
-        v_pool = keep.tile([P, T], F32, name="v_pool", align_bytes=64)
+        v_pool = {b: keep.tile([P, (b + 1) * SEG], F32, name="v_pool%d" % b, align_bytes=64) for b in range(B)}
         s_pool = keep.tile([P, T], F32, name="s_pool", align_bytes=64)
         s_rows = keep.tile([P, B * N], F32, name="s_rows")
         ident = keep.tile([P, P], F32, name="ident")
@@ -72,7 +70,7 @@ def tile_attend_x_cluster_cap_kernel(tc, xq, kT, vT, vs, offs, qoffs, out):
 
         def clear_result(b):
             placed[b] = place(("placed", b), [P, (b + 1) * SEG], F32)
-            nc.gpsimd.memset(placed[b][:, b * SEG : (b + 1) * SEG].bitcast(U32), 0)
+            nc.vector.memset(placed[b][:, b * SEG : (b + 1) * SEG].bitcast(U32), 0)
 
         planes, grouped, codes, scales = {}, {}, {}, {}
 
@@ -89,7 +87,7 @@ def tile_attend_x_cluster_cap_kernel(tc, xq, kT, vT, vs, offs, qoffs, out):
             if name == "q" and engine == "g":
                 nc.gpsimd.tensor_copy(dest.rearrange("p (n j) -> p n j", j=PACK), src.rearrange("p j n -> p n j"))
             elif name == "q":
-                run = 4 if b == FIRST else 8
+                run = 4
                 nc.vector.tensor_copy(
                     dest.rearrange("p (c i j) -> p c j i", i=run, j=PACK), src.rearrange("p j (c i) -> p c j i", i=run)
                 )
@@ -97,9 +95,14 @@ def tile_attend_x_cluster_cap_kernel(tc, xq, kT, vT, vs, offs, qoffs, out):
                 nc.vector.tensor_copy(
                     dest.rearrange("p (t s j) -> p s j t", t=PACK, j=PACK), src.rearrange("p j (s t) -> p s j t", t=PACK)
                 )
-            else:
+            elif engine == "g":
                 nc.gpsimd.tensor_copy(
                     dest.rearrange("p (t s j) -> p t s j", t=PACK, j=PACK), src.rearrange("p j (s t) -> p t s j", t=PACK)
+                )
+            else:
+                nc.vector.tensor_copy(
+                    dest.rearrange("p (t c r j) -> p c t r j", t=PACK, r=2, j=PACK),
+                    src.rearrange("p j (c r t) -> p c t r j", t=PACK, r=2),
                 )
 
         def quantize(name, b, lo=0, hi=N):
@@ -129,7 +132,7 @@ def tile_attend_x_cluster_cap_kernel(tc, xq, kT, vT, vs, offs, qoffs, out):
 
         def gather_values(b, engine):
             v_rows[b] = place(("v_rows", b), [P, N], BF16)
-            copy_on(engine, v_rows[b][:], v_pool[:].indirect(lists["k"][:, b * COLS : (b + 1) * COLS]))
+            copy_on(engine, v_rows[b][:], v_pool[b][:].indirect(lists["k"][:, b * COLS : (b + 1) * COLS]))
 
         def turn_values(b, number):
             bank = bank_tile([P, 2, P], number)
@@ -296,8 +299,12 @@ def tile_attend_x_cluster_cap_kernel(tc, xq, kT, vT, vs, offs, qoffs, out):
         for name, b in (("q", A), ("k", Z), ("q", Z)):
             for j in range(PACK):
                 load(name, b, j)
-        nc.sync.dma_start(out=v_pool[:], in_=vT)
+        for b in (A, Z):
+            nc.sync.dma_start(out=v_pool[b][:, b * SEG : (b + 1) * SEG], in_=vT[:, b * SEG : (b + 1) * SEG])
         make_identity(nc, ident[:])
+        nc.vector.memset(v_pool[Z][:, 0:SEG].bitcast(U32), 0)
+        clear_result(A)
+        clear_result(Z)
 
         gather("k", A, 0, "s")
         gather("k", A, 1, "s")
@@ -316,7 +323,6 @@ def tile_attend_x_cluster_cap_kernel(tc, xq, kT, vT, vs, offs, qoffs, out):
         weave("q", A, 256, 512)
         quantize("q", A, 0, 256)
         quantize("q", A, 256, 512)
-        clear_result(A)
         turn_scales(A, "v", 4)
         turn_scales(Z, "v", 5)
         gather("k", Z, 0, "s")
@@ -325,7 +331,7 @@ def tile_attend_x_cluster_cap_kernel(tc, xq, kT, vT, vs, offs, qoffs, out):
             scores(A, j)
         gather("k", Z, 2, "v")
         gather("k", Z, 3, "v")
-        weave("k", Z)
+        weave("k", Z, engine="g")
         cap(A, 0, 4)
         cap(A, 1)
         cap(A, 2)
@@ -340,15 +346,13 @@ def tile_attend_x_cluster_cap_kernel(tc, xq, kT, vT, vs, offs, qoffs, out):
         maxima(A, 2)
         maxima(A, 3)
         gather("q", Z, 1, "v")
-        gather("q", Z, 2, "s", 256, 512)
-        gather("q", Z, 2, "v", 0, 256)
-        gather("q", Z, 3, "s")
-        quantize("k", Z)
+        gather("q", Z, 2, "s")
+        gather("q", Z, 3, "v", 0, 256)
+        gather("q", Z, 3, "s", 256, 512)
         weave("q", Z, 0, 256)
+        quantize("k", Z)
         weave("q", Z, 256, 512)
         quantize("q", Z, 0, 256)
-        quantize("q", Z, 256, 512)
-        clear_result(Z)
         exps(A, 2, 2)
         turn(A, 2, 6)
         exps(A, 3)
@@ -362,6 +366,7 @@ def tile_attend_x_cluster_cap_kernel(tc, xq, kT, vT, vs, offs, qoffs, out):
         spread(A, 0, 4, 4)
         weigh(A, 1)
         turn_values(A, 5)
+        quantize("q", Z, 256, 512)
         scores(Z, 2)
         scores(Z, 3)
         weigh(A, 2)
@@ -374,8 +379,8 @@ def tile_attend_x_cluster_cap_kernel(tc, xq, kT, vT, vs, offs, qoffs, out):
         cap(Z, 2)
         cap(Z, 3)
         maxima(Z, 0)
-        quantize_values(A)
         quantize_weights(A, 0, 4)
+        quantize_values(A)
         product(A, 0, 4, 7)
         maxima(Z, 1)
         maxima(Z, 2)

from contextlib import ExitStack

import concourse.mybir as mybir
from concourse.masks import make_identity

P = 128
B, N, T, D, DV, NQ = 2, 512, 2048, 512, 128, 512
SEG = T // B
PACK = 4
TILES = NQ // P
COLS = N // 16
FLOPS = 2 * B * NQ * N * (D + DV)
FIRST, LAST = 0, 1

F32 = mybir.dt.float32
BF16 = mybir.dt.bfloat16
U32 = mybir.dt.uint32
U16 = mybir.dt.uint16
U8 = mybir.dt.uint8
FP8X4 = mybir.dt.float8_e4m3fn_x4
ACT = mybir.ActivationFunctionType
ALU = mybir.AluOpType
REUSES = {
    "scale": "grouped_q_0_0",
    "capped_0_0": "plane_k_1",
    "low_0": "plane_k_3",
    "p_0_2": "plane_q_2",
    "codes_k_1_0": "plane_q_3",
    "w_0_0": "planes_q_1",
    "grouped_v_1": "capped_1_1",
    "y_0_2": "inv_1_0",
}


def tile_attend_x_cluster_cap_kernel(tc, xq, kT, vT, vs, offs, qoffs, out):
    nc = tc.nc
    with ExitStack() as ctx:
        keep = ctx.enter_context(tc.tile_pool(name="keep", bufs=1))
        ps = ctx.enter_context(tc.psum_pool(name="ps", bufs=1))

        def bank_tile(shape, number):
            return ps.tile(shape, F32, name="bank_%d" % number)

        def place(key, shape, kind):
            own = "_".join(str(part) for part in key)
            return keep.tile(shape, kind, name=REUSES.get(own, own), align_bytes=64)

        def copy_on(engine, dest, src):
            if engine == "s":
                nc.scalar.activation(dest, src, ACT.Copy)
            else:
                nc.vector.tensor_copy(dest, src)

        lists = {"k": keep.tile([P, B * COLS], U16, name="lists"), "q": keep.tile([P, B * COLS], U16, name="qlists")}
        source = {"k": kT.rearrange("(p j) w -> p j w", j=PACK), "q": xq.rearrange("(p j) w -> p j w", j=PACK)}
        window, pool_plane = {}, {}
        v_pool = {b: keep.tile([P, (b + 1) * SEG], F32, name="v_pool%d" % b, align_bytes=64) for b in range(B)}
        s_pool = keep.tile([P, T], F32, name="s_pool", align_bytes=64)
        s_rows = keep.tile([P, B * N], F32, name="s_rows")
        ident = keep.tile([P, P], F32, name="ident")

        def load(name, b, j):
            if b == FIRST:
                pool_plane[name, j] = place(("plane", name, j), [P, T], F32)
            window[name, b, j] = pool_plane[name, j][:, 0 : (b + 1) * SEG]
            tokens = slice(b * SEG, (b + 1) * SEG)
            nc.sync.dma_start(out=pool_plane[name, j][:, tokens], in_=source[name][:, j, tokens])

        placed = {}

        def clear_result(b):
            placed[b] = place(("placed", b), [P, (b + 1) * SEG], F32)
            nc.vector.memset(placed[b][:, b * SEG : (b + 1) * SEG].bitcast(U32), 0)

        planes, grouped, codes, scales = {}, {}, {}, {}

        def gather(name, b, j, engine, lo=0, hi=N):
            if (name, b) not in planes:
                planes[name, b] = place(("planes", name, b), [P, PACK, N], F32 if b == FIRST else BF16)
            offsets = lists[name][:, b * COLS + lo // 16 : b * COLS + hi // 16]
            copy_on(engine, planes[name, b][:, j, lo:hi], window[name, b, j].indirect(offsets))

        def weave(name, b, lo=0, hi=N, engine="v"):
            grouped[name, b, lo] = place(("grouped", name, b, lo), [P, (hi - lo) * PACK], BF16)
            dest = grouped[name, b, lo][:]
            src = planes[name, b][:, :, lo:hi]
            if name == "q" and engine == "g":
                nc.gpsimd.tensor_copy(dest.rearrange("p (n j) -> p n j", j=PACK), src.rearrange("p j n -> p n j"))
            elif name == "q":
                run = 4
                nc.vector.tensor_copy(
                    dest.rearrange("p (c i j) -> p c j i", i=run, j=PACK), src.rearrange("p j (c i) -> p c j i", i=run)
                )
            elif b == FIRST:
                nc.vector.tensor_copy(
                    dest.rearrange("p (t s j) -> p s j t", t=PACK, j=PACK), src.rearrange("p j (s t) -> p s j t", t=PACK)
                )
            elif engine == "g":
                nc.gpsimd.tensor_copy(
                    dest.rearrange("p (t s j) -> p t s j", t=PACK, j=PACK), src.rearrange("p j (s t) -> p t s j", t=PACK)
                )
            else:
                nc.vector.tensor_copy(
                    dest.rearrange("p (t c r j) -> p c t r j", t=PACK, r=2, j=PACK),
                    src.rearrange("p j (c r t) -> p c t r j", t=PACK, r=2),
                )

        def quantize(name, b, lo=0, hi=N):
            part = place(("codes", name, b, lo), [P, hi - lo], U32)
            part_scales = place(("scales", name, b, lo), [P, hi - lo], U8)
            for j in range(lo // P, hi // P):
                codes[name, b, j] = (part, part_scales, j * P - lo)
            nc.vector.quantize_mx(out=part[:].bitcast(FP8X4), scales=part_scales[:], in_=grouped[name, b, lo][:])

        slot_scale = {}

        def gather_scales(engine, lo, hi):
            copy_on(engine, s_rows[:, lo:hi], s_pool[:].indirect(lists["k"][:, lo // 16 : hi // 16]))

        def turn_scales(b, engine, number):
            bank = bank_tile([P, PACK, P], number)
            slots = s_rows[:, b * N : (b + 1) * N].rearrange("p (s t) -> p t s", t=PACK)
            for t in range(PACK):
                nc.tensor.transpose(bank[:, t, :], slots[:, t, :], ident[:])
            if not slot_scale:
                both = place(("scale",), [P, B * PACK], F32)
                for seq in range(B):
                    slot_scale[seq] = both[:, seq * PACK : (seq + 1) * PACK]
            copy_on(engine, slot_scale[b], bank[:, :, 0])

        v_rows, v_bank, v_grouped, v_codes, v_scales = {}, {}, {}, {}, {}

        def gather_values(b, engine):
            v_rows[b] = place(("v_rows", b), [P, N], BF16)
            copy_on(engine, v_rows[b][:], v_pool[b][:].indirect(lists["k"][:, b * COLS : (b + 1) * COLS]))

        def turn_values(b, number):
            bank = bank_tile([P, 2, P], number)
            slot_words = v_rows[b][:].bitcast(F32).rearrange("p (s u) -> p u s", u=2)
            for u in range(2):
                nc.tensor.transpose(bank[:, u, :], slot_words[:, u, :], ident[:])
            v_bank[b] = bank

        def take_values(b, engine):
            v_grouped[b] = place(("grouped_v", b), [P, DV * PACK], BF16)
            dest = v_grouped[b][:].bitcast(F32).rearrange("p (e u) -> p e u", u=2)
            src = v_bank[b][:].rearrange("p u e -> p e u")
            if engine == "s":
                nc.scalar.copy(dest, src)
            else:
                nc.vector.tensor_copy(dest, src)

        def quantize_values(b):
            v_codes[b] = place(("codes_v", b), [P, DV], U32)
            v_scales[b] = place(("scales_v", b), [P, DV], U8)
            nc.vector.quantize_mx(out=v_codes[b][:].bitcast(FP8X4), scales=v_scales[b][:], in_=v_grouped[b][:])

        banks, capped, doubled, lows, probs, turned = {}, {}, {}, {}, {}, {}
        low_tile = {}
        sums, w_rows, w_codes, w_scales = {}, {}, {}, {}

        def scores(b, j):
            banks[b, j] = bank_tile([P, N], j)
            q_codes, q_scales, first = codes["q", b, j]
            k_codes, k_scales, first_key = codes["k", b, 0]
            cols = slice(first, first + P)
            nc.tensor.matmul_mx(
                out=banks[b, j][:],
                lhsT=q_codes[:, cols].bitcast(FP8X4),
                lhsT_scale=q_scales[:, cols],
                rhs=k_codes[:].bitcast(FP8X4),
                rhs_scale=k_scales[:],
                start=True,
                stop=True,
            )

        def cap(b, j, together=1):
            if (b, j) not in capped:
                rows = place(("capped", b, j), [P, together, N], F32)
                for i in range(together):
                    capped[b, j + i] = rows[:, i]
            nc.scalar.activation(capped[b, j], banks[b, j][:], ACT.Tanh, scale=0.5)

        def maxima(b, j):
            doubled[b, j] = capped[b, j]
            if b not in low_tile:
                low_tile[b] = place(("low", b), [P, TILES], F32)
            lows[b, j] = low_tile[b][:, j : j + 1]
            nc.vector.tensor_scalar(
                doubled[b, j], capped[b, j], -2.0, None, ALU.mult, ALU.min, accum_out=lows[b, j]
            )

        def exps(b, j, together=1):
            if b not in sums:
                sums[b] = place(("sums", b), [P, TILES], F32)
            if (b, j) not in probs:
                rows = place(("p", b, j), [P, together, PACK, P], F32)
                for i in range(together):
                    probs[b, j + i] = rows[:, i]
            nc.scalar.activation(
                probs[b, j].rearrange("q t s -> q (t s)"), doubled[b, j], ACT.Exp, bias=lows[b, j], scale=-1.0,
                accum_out=sums[b][:, j : j + 1],
            )

        def turn(b, j, number):
            turned[b, j] = bank_tile([P, PACK, P], number)
            for t in range(PACK):
                nc.tensor.transpose(turned[b, j][:, t, :], probs[b, j][:, t, :], ident[:])

        def weigh(b, j, together=1):
            if (b, j) not in w_rows:
                rows = place(("w", b, j), [P, together * P * PACK], BF16)
                for i in range(together):
                    w_rows[b, j + i] = (rows, j)
            rows, first = w_rows[b, j]
            dest = rows[:, (j - first) * P * PACK : (j - first + 1) * P * PACK]
            nc.vector.tensor_tensor(
                dest.rearrange("s (c r t) -> s c t r", r=2, t=PACK),
                turned[b, j][:].rearrange("s t (c r) -> s c t r", r=2),
                slot_scale[b].unsqueeze(1).unsqueeze(3).to_broadcast([P, P // 2, PACK, 2]),
                ALU.mult,
            )

        def quantize_weights(b, lo, hi):
            if b not in w_codes:
                w_codes[b] = place(("codes_w", b), [P, NQ], U32)
                w_scales[b] = place(("scales_w", b), [P, NQ], U8)
            nc.vector.quantize_mx(
                out=w_codes[b][:, lo * P : hi * P].bitcast(FP8X4),
                scales=w_scales[b][:, lo * P : hi * P],
                in_=w_rows[b, lo][0][:, (lo - w_rows[b, lo][1]) * P * PACK : (hi - w_rows[b, lo][1]) * P * PACK],
            )

        sums_y, results, factors, invs, rows_inv = {}, {}, {}, {}, {}

        def product(b, lo, hi, number):
            sums_y[b, lo] = bank_tile([P, (hi - lo) * P], number)
            nc.tensor.matmul_mx(
                out=sums_y[b, lo][:],
                lhsT=v_codes[b][:].bitcast(FP8X4),
                lhsT_scale=v_scales[b][:],
                rhs=w_codes[b][:, lo * P : hi * P].bitcast(FP8X4),
                rhs_scale=w_scales[b][:, lo * P : hi * P],
                start=True,
                stop=True,
            )

        def invert(b, lo, hi):
            invs[b, lo] = place(("inv", b, lo), [P, hi - lo], F32)
            nc.vector.reciprocal(invs[b, lo][:], sums[b][:, lo:hi])

        def spread(b, lo, hi, number):
            rows_inv[b, lo] = bank_tile([P, hi - lo, P], number)
            for i in range(hi - lo):
                nc.tensor.transpose(rows_inv[b, lo][:, i, :], invs[b, lo][:, i : i + 1].to_broadcast([P, P]), ident[:])

        def take_factor(b, lo, hi, engine):
            factor = place(("factor", b, lo), [P, (hi - lo) * P], F32)
            copy_on(engine, factor[:], rows_inv[b, lo][:].rearrange("p i q -> p (i q)"))
            for j in range(lo, hi):
                factors[b, j] = (factor, lo)

        def factor_of(b, lo, hi):
            factor, first = factors[b, lo]
            return factor[:, (lo - first) * P : (hi - first) * P]

        def take_result(b, lo, hi, engine):
            results[b, lo] = place(("y", b, lo), [P, (hi - lo) * P], F32)
            copy_on(engine, results[b, lo][:], sums_y[b, lo][:])

        def divide(b, lo, hi):
            results[b, lo] = place(("y", b, lo), [P, (hi - lo) * P], F32)
            first = max(key[1] for key in sums_y if key[0] == b and key[1] <= lo)
            sums_part = sums_y[b, first][:, (lo - first) * P : (hi - first) * P]
            nc.vector.tensor_tensor(results[b, lo][:], sums_part, factor_of(b, lo, hi), ALU.mult)

        def places(b, lo, hi):
            return placed[b][:].indirect(lists["q"][:, b * COLS + lo * P // 16 : b * COLS + hi * P // 16])

        def scatter_dividing(b, lo, hi):
            nc.vector.tensor_tensor(places(b, lo, hi), results[b, lo][:], factor_of(b, lo, hi), ALU.mult)

        def scatter(b, lo, hi, engine, first=None):
            first = lo if first is None else first
            copy_on(engine, places(b, lo, hi), results[b, first][:, (lo - first) * P : (hi - first) * P])

        def store(b):
            nc.sync.dma_start(out=out[:, b * SEG : (b + 1) * SEG], in_=placed[b][:, b * SEG : (b + 1) * SEG])

        A, Z = FIRST, LAST
        nc.vector.memset(s_pool[:].bitcast(U32), 0)
        load("k", A, 0)
        nc.sync.dma_start(lists["k"][:], offs)
        load("k", A, 1)
        nc.sync.dma_start(out=s_pool[0:1, :], in_=vs[0:1, :])
        load("k", A, 2)
        load("k", A, 3)
        nc.sync.dma_start(lists["q"][:], qoffs)
        for name, b in (("q", A), ("k", Z), ("q", Z)):
            for j in range(PACK):
                load(name, b, j)
        for b in (A, Z):
            nc.sync.dma_start(out=v_pool[b][:, b * SEG : (b + 1) * SEG], in_=vT[:, b * SEG : (b + 1) * SEG])
        make_identity(nc, ident[:])
        nc.vector.memset(v_pool[Z][:, 0:SEG].bitcast(U32), 0)
        clear_result(A)
        clear_result(Z)

        gather("k", A, 0, "s")
        gather("k", A, 1, "s")
        gather_scales("v", 0, 1024)
        gather("k", A, 2, "s")
        gather("k", A, 3, "v")
        weave("k", A)
        gather("q", A, 0, "s")
        gather("q", A, 1, "s")
        quantize("k", A)
        gather("q", A, 2, "v", 0, 256)
        gather("q", A, 2, "s", 256, 512)
        gather("q", A, 3, "v", 0, 256)
        gather("q", A, 3, "s", 256, 512)
        weave("q", A, 0, 256)
        weave("q", A, 256, 512)
        quantize("q", A, 0, 256)
        quantize("q", A, 256, 512)
        turn_scales(A, "v", 4)
        turn_scales(Z, "v", 5)
        gather("k", Z, 0, "s")
        gather("k", Z, 1, "s")
        for j in range(4):
            scores(A, j)
        gather("k", Z, 2, "v")
        gather("k", Z, 3, "v")
        weave("k", Z, engine="g")
        cap(A, 0, 4)
        cap(A, 1)
        cap(A, 2)
        cap(A, 3)
        maxima(A, 0)
        gather("q", Z, 0, "s")
        maxima(A, 1)
        exps(A, 0)
        turn(A, 0, 4)
        exps(A, 1)
        turn(A, 1, 5)
        maxima(A, 2)
        maxima(A, 3)
        gather("q", Z, 1, "v")
        gather("q", Z, 2, "s")
        gather("q", Z, 3, "v", 0, 256)
        gather("q", Z, 3, "s", 256, 512)
        weave("q", Z, 0, 256)
        quantize("k", Z)
        weave("q", Z, 256, 512)
        quantize("q", Z, 0, 256)
        exps(A, 2, 2)
        turn(A, 2, 6)
        exps(A, 3)
        turn(A, 3, 7)
        gather_values(A, "s")
        gather_values(Z, "s")
        invert(A, 0, 4)
        scores(Z, 0)
        scores(Z, 1)
        weigh(A, 0, 4)
        spread(A, 0, 4, 4)
        weigh(A, 1)
        turn_values(A, 5)
        quantize("q", Z, 256, 512)
        scores(Z, 2)
        scores(Z, 3)
        weigh(A, 2)
        turn_values(Z, 6)
        weigh(A, 3)
        cap(Z, 0)
        cap(Z, 1)
        take_factor(A, 0, 4, "s")
        take_values(A, "s")
        cap(Z, 2)
        cap(Z, 3)
        maxima(Z, 0)
        quantize_weights(A, 0, 4)
        quantize_values(A)
        product(A, 0, 4, 7)
        maxima(Z, 1)
        maxima(Z, 2)
        exps(Z, 0)
        turn(Z, 0, 0)
        exps(Z, 1)
        maxima(Z, 3)
        turn(Z, 1, 1)
        exps(Z, 2)
        divide(A, 0, 2)
        invert(Z, 0, 2)
        weigh(Z, 0, 2)
        spread(Z, 0, 2, 5)
        take_values(Z, "s")
        turn(Z, 2, 2)
        exps(Z, 3)
        turn(Z, 3, 3)
        weigh(Z, 1)
        quantize_values(Z)
        divide(A, 2, 4)
        scatter(A, 0, 2, "s")
        take_factor(Z, 0, 2, "s")
        quantize_weights(Z, 0, 2)
        invert(Z, 2, 4)
        product(Z, 0, 2, 0)
        spread(Z, 2, 4, 4)
        weigh(Z, 2, 2)
        weigh(Z, 3)
        divide(Z, 0, 2)
        scatter(A, 2, 4, "s")
        store(A)
        quantize_weights(Z, 2, 4)
        product(Z, 2, 4, 1)
        scatter(Z, 0, 2, "v")
        take_factor(Z, 2, 4, "s")
        take_result(Z, 2, 4, "s")
        scatter_dividing(Z, 2, 4)
        store(Z)
